import numpy as np, ml_dtypes
CORES = [66,74,82,90,194,202,210,218]
N = 8
import mx_ref
BF = ml_dtypes.bfloat16
def gentries(a):
    return np.ascontiguousarray(a.reshape(8, 16, -1).transpose(0, 2, 1)).reshape(8, -1)
def gtable(e):
    e = np.asarray(e); return np.ascontiguousarray(e.reshape(8, -1, 16).transpose(0, 2, 1)).reshape(128, -1).astype(np.int32)
def gcols(t, e):
    v = np.concatenate([t.reshape(8, 16, -1, 4), np.zeros((8, 16, 1, 4), BF)], axis=2)
    return np.ascontiguousarray(np.stack([v[g][:, e[g]] for g in range(8)])).reshape(128, -1)
def tile(rs):
    return np.stack(rs, axis=2).reshape(128, -1).astype(BF)
def pick(q, e):
    c = np.concatenate([q[0].reshape(128, -1, 4), np.zeros((128, 1, 4), np.uint8)], axis=1); s = np.concatenate([q[1], np.ones((16, 1), np.uint8)], axis=1)
    return (np.ascontiguousarray(c[:, e].reshape(128, -1)), np.ascontiguousarray(s[:, e]))
def join(*qs):
    return (np.concatenate([q[0] for q in qs], axis=1), np.concatenate([q[1] for q in qs], axis=1))
def put(q, e, v):
    c, s = q[0].reshape(128, -1, 4).copy(), q[1].copy(); c[:, e] = v[0].reshape(128, -1, 4); s[:, e] = v[1]
    return (c.reshape(128, -1), s)
def pk(c, s):
    return (np.ascontiguousarray(c), mx_ref.live(s))
def emit(q):
    return q[0], q[1]
def packed(v, rng):
    q = [mx_ref.quantize(np.ascontiguousarray(v[r])) for r in range(N)]
    return np.stack([a for a, b in q]), np.stack([mx_ref.plane(b, rng) for a, b in q])
def values_of_codes():
    e, c = np.zeros((128, 128, 4), np.float32), np.zeros((128, 2, 4), np.uint8)
    e[np.arange(128), np.arange(128), 0] = 1
    c[:127, :, 0] = np.arange(256).reshape(2, 128).T[:127]
    return mx_ref.matmul(mx_ref.quantize(e.reshape(128, 512).astype(BF)), (c.reshape(128, 8), np.full((16, 2), 127, np.uint8))).T.reshape(-1).astype(np.float64)
CODE_VALUE, SCALE_VALUE = values_of_codes(), 2.0 ** (np.arange(256) - 127.0)
def decode(q):
    return (CODE_VALUE[q[0]].reshape(16, 8, -1, 4) * SCALE_VALUE[q[1]][:, None, :, None] + 0.0).reshape(128, -1).astype(np.float32)
def f(rng, *shape):
    return mx_ref.flush((rng.standard_normal(shape, dtype=np.float32) * np.exp2(rng.integers(-2, 3, shape[:-1] + (1,)))).astype(BF))
def wide(rng, *shape, cols=0):
    v = rng.standard_normal(shape, dtype=np.float32) * np.exp2(rng.integers(-12, 13, shape)).astype(np.float32)
    if cols: v *= np.repeat(np.exp2(rng.integers(-cols, cols + 1, shape[:-2] + (1, shape[-1] // 4))) * (rng.random(shape[:-2] + (1, shape[-1] // 4)) > 0.0625), 4, axis=-1).astype(np.float32)
    return mx_ref.flush(v.astype(BF))
C, H, R = 448, 128, 3
def follow(copies, far):
    e = np.tile(np.arange(H + C), (8, 1))
    e[:, H:] -= np.where(copies, far, 0)
    for i in range(C.bit_length()): e = np.take_along_axis(e, e, axis=1)
    return e[:, H:]
def alike(a):
    return np.stack([a] * N)
def trim(v):
    v = v.astype(np.float32)
    v[np.abs(v) < np.float32(2.0 ** -16)] = 0
    return v.astype(BF)
def weights(rng, shut=np.zeros(128, bool)):
    w = trim(f(rng, 128, 2048)).reshape(128, 4, 128, 4)
    w[shut] = 0
    w[:, :, shut] = 0
    c, p = packed(alike(w.reshape(128, 2048)), rng)
    return {"wc": c, "ws": p}
def numbers_of(rng):
    return {"x": trim(f(rng, N, 128, 4 * C)), "u": alike(np.array(f(rng, 128, 512))), "v": np.array(f(rng, N, 128, 512)), "dist": alike(gtable(rng.integers(1, H + 1, (8, C))))}
def first():
    return np.arange(128) % 16 < 8
def heads(d, s, a, b):
    x = d["x"].reshape(N, 8, 16, C, 4)
    x[:, :, :8] = (s * a).astype(np.float32).astype(BF)[:, :, None, :, None]
    u = d["u"].reshape(N, 8, 16, 8, 16, 4)
    u[:, :, :, :, 0] = 0
    for g in range(8): u[:, g, :8, g, 0] = b[g]
    return {**d, "x": x.reshape(N, 128, 4 * C), "u": u.reshape(N, 128, 512)}
def setup_inputs(rng):
    return {**numbers_of(rng), **weights(rng)}
def setup_inputs_deep(rng):
    d = numbers_of(rng)
    k = rng.permutation(8)
    far = rng.integers(1, H + 1, (8, C))
    far[k[:4]] = 1
    far[k[4:6]] = H
    s = rng.permuted(np.tile(np.arange(C) % 2 * 2.0 - 1.0, (N, 8, 1)), axis=2)
    for i in (0, 1, 2, 4, 6): s[:, k[i]] = -1
    s[:, k[1], 0] = 1
    for r in range(N): s[r, k[2], rng.permutation(C)[:3]] = 1
    s[:, k[3]] = (rng.permutation(N) % 2 * 2.0 - 1.0)[:, None]
    d["dist"] = alike(gtable(far))
    return {**heads(d, s, 1.0, [1.0] * 8), **weights(rng, first())}
def setup_inputs_near(rng):
    d = numbers_of(rng)
    s = rng.permuted(np.tile(np.arange(C) % 3 - 1.0, (N, 8, 1)), axis=2)
    k = rng.permutation(8)
    h = int(rng.integers(8))
    d = heads(d, s, np.where(k < 6, 2.0 ** -23, 2.0 ** -30)[:, None], [1.0 if k[g] < 4 else 2.0 ** -25 if k[g] < 6 else 2.0 ** -30 for g in range(8)])
    x = d["x"].reshape(N, 8, 16, C, 4)
    x[:, :, 1:8] = 0
    x[:, :, 0, :, 1:] = 0
    x[:, h, 8:] = 0
    x[:, h, 8, :, 0] = 1
    x[:, h, 9, :, 0] = -1
    u = d["u"].reshape(N, 8, 16, 8, 16, 4)
    for g in range(8):
        if k[g] < 4: u[:, h, 8:10, g, 0, 0] = 1
    shut = first()
    shut[16 * h:16 * h + 16] = True
    return {**d, "x": x.reshape(N, 128, 4 * C), "u": u.reshape(N, 128, 512), **weights(rng, shut)}
def setup_inputs_sums(rng):
    d = numbers_of(rng)
    g = 4 + 2 * int(rng.integers(2))
    blk = np.array([4, 5, 6, 7, 2 * g, 2 * g + 1, 2 * g + 2, 2 * g + 3])
    rest = rng.permutation(np.setdiff1d(np.arange(16), blk))
    x = np.zeros((N, 16, 8, C, 4), np.float32)
    w = np.zeros((128, 4, 128, 4), np.float32)
    u = d["u"].reshape(N, 128, 128, 4)
    u[:, :, ::16] = 0
    r, j = np.arange(N)[:, None], np.arange(C)
    o = np.argsort(rng.random((N, C, 8)), axis=2)
    for h in range(8):
        p, b = h // 4, h % 4
        i = np.take_along_axis(o[:, :, :4], np.argsort(rng.random((N, C, 4)), axis=2), axis=2)
        s = np.take_along_axis(o[:, :, 4:], rng.integers(0, 4, (N, C, 1)), axis=2)
        x[r, blk[i[:, :, 0]], p, j, b] = 1
        x[r, blk[i[:, :, 1]], p, j, b] = -1
        x[r, blk[s[:, :, 0]], p, j, b] = rng.choice([-1.0, 1.0], (N, C)) * 2.0 ** -26
        x[:, rest[h], 0, :, 0] = rng.integers(1, 9, (N, C)) * rng.choice([-1.0, 1.0], (N, C)) * 2.0 ** -26
        u[:, 8 * blk + p, 16 * h, b] = 1
        w[8 * blk + p, 0, 8 * rest[h], b] = 64
    c, q = packed(alike(w.reshape(128, 2048).astype(BF)), rng)
    return {**d, "x": x.reshape(N, 128, 4 * C).astype(BF), "u": u.reshape(N, 128, 512), "wc": c, "ws": q}
def setup_inputs_huge(rng):
    d = numbers_of(rng)
    s = rng.permuted(np.tile(np.arange(C) % 2 * 2.0 - 1.0, (N, 8, 1)), axis=2)
    k = rng.permutation(8)
    s[:, k[0]] = -1
    s[:, k[1]] = 1
    return {**heads(d, s, 2.0 ** 30, [2.0 ** 30] * 8), **weights(rng, first())}
def setup_inputs_spread(rng):
    d = setup_inputs(rng)
    d["x"] = trim(wide(rng, N, 128, 4 * C, cols=6))
    return d
def check_inputs(d):
    b = []
    for k in ("x", "u", "v"):
        a = np.abs(d[k].astype(np.float32))
        if not (np.isfinite(a).all() and ((a == 0) | (a >= 2.0 ** -30) & (a <= 2.0 ** 30)).all()): b.append("a value of " + k)
    for k in ("u", "wc", "dist"):
        if (d[k] != d[k][:1]).any(): b.append(k + " differs between ranks")
    s = [mx_ref.live(p) for p in d["ws"]]
    if any((p != s[0]).any() for p in s): b.append("ws differs between ranks")
    if ((d["wc"] == 127) | (d["wc"] == 255)).any(): b.append("a code of wc")
    if (d["dist"] < 1).any() or (d["dist"] > H).any(): b.append("a number of dist")
    return b
def reference(x, u, v, dist, wc, ws):
    w, qu, far = pk(wc[0], ws[0]), mx_ref.quantize(u[0]), gentries(dist[0])
    now = [x[r] for r in range(N)]
    for t in range(R):
        q = [mx_ref.quantize(now[r]) for r in range(N)]
        full = [decode(q[r]) for r in range(N)]
        roots = []
        for r in range(N):
            e = follow(mx_ref.matmul(qu, q[r])[::16] < 0, far)
            halo = full[r - 1][:, 4 * (C - H):] if r > 0 else np.zeros((128, 4 * H), np.float32)
            z = mx_ref.quantize(gcols(np.concatenate([halo, full[r]], axis=1).astype(BF), e))
            now[r] = tile([full[r][:, b::4] + mx_ref.matmul(pick(w, np.arange(128 * b, 128 * b + 128)), z) * np.float32(0.015625) for b in range(4)])
            roots.append(e - H)
    y, ol = np.zeros((N, 128, C), np.float32), np.zeros((N, 8, C), np.float32)
    oc, osc = np.zeros((N, 128, 4 * C), np.uint8), np.zeros((N, 16, C), np.uint8)
    for r in range(N):
        last = mx_ref.quantize(now[r])
        y[r] = mx_ref.matmul(mx_ref.quantize(v[r]), last)
        ol[r] = roots[r]
        oc[r], osc[r] = emit(last)
    return {"y": y, "ol": ol, "oc": oc, "osc": osc}

@@ -1,0 +1,476 @@
+from concourse.mybir import dt, AluOpType, ActivationFunctionType
+
+C, H, ROUNDS = 448, 128, 3
+LO = C - H
+MID = 192
+PAD = 8
+BIG = 1024.0
+BANK = 512
+JW = H + 520
+X4, U8, F32, BF, I32, U16 = "float8_e4m3fn_x4", "uint8", "float32", "bfloat16", "int32", "uint16"
+
+SCRATCH = {"ps": ("psum", [128, 8 * BANK], F32)}
+for _ty, _bufs in (
+        (I32, {"drep": C, "pi": 2, "pm": 2}),
+        (BF, {"xt": 4 * C, "ut": 512, "vt": 512, "em": 520, "zt": 4 * C, "tt1": 4 * C, "tt2": 4 * C, "tt3": 4 * C,
+              "fw0": 4 * (H + C), "fw1": 4 * (H + C), "fw2": 4 * (H + C)}),
+        (X4, {"qu0": 128, "qu": 128, "qv": 128, "qw": 512, "qe": 512, "qz": C, "q0": C + H, "q1": C + H, "q2": C + H, "q3": C + H}),
+        (U8, {"su0": 128, "su": 128, "sv": 128, "sw": 512, "se": 512, "sz": C, "s0": C + H, "s1": C + H, "s2": C + H, "s3": C + H}),
+        (U16, {"o1": 32, "o2": 32, "o3": 32, "f1": 32, "f2": 32, "off": 32, "lo": 32, "uo": 8}),
+        (F32, {"sg": C, "r0": 512, "ra": PAD + 512, "rb": PAD + 512, "rc": H + C, "rs": C, "vw": 3 * 512, "vs": 512,
+               "t1": 32, "m0": 32, "m1": 32, "m2": 32, "m3": 32, "pf": 2, "p4": 1, "jn": JW, "jq": C, "c16": 32, "cj0": 32,
+               "cj": 32, "kk": 256, "k0": 16, "k1": 16, "col": 8, "c1": 32, "olb": C, "yb": C})):
+    for _name, _n in _bufs.items():
+        SCRATCH[_name] = ("sbuf", [128, _n], _ty)
+
+SEMAPHORES = ["sV", "sA", "sP", "sG", "sent", "arr0", "arr1", "arr2",
+              "dD", "dXL", "dXF", "dU", "dV", "dW", "dOl", "dOut"]
+
+ALU, ACT = AluOpType, ActivationFunctionType
+
+CHUNK = {"A": (0, MID, 0, 5), "L": (LO, C, 4, 4), "B": (MID, LO, 0, 6)}
+
+ORDER = {
+    "HEAD": ("zf z0 i0 i1 i2 pm cb c28 pf i3 i4 i5 c1 k1 k0 jq em kk uo kk16 c8 cj qe1 lo cr c1w qe0 v0 kk32 qL qu ps S1 pk "
+             "qF x kk64 t1 o1 m10 m11 P kk128 z1 F0 m12 z2 m13 c3 i6 z3 sg m14 qe3 u0 qv u1 r0 u2 qe2 a0 u3 u4 a1 a2 u5 u6 "
+             "u7 F3 F1 a3 a4 c2 F2 a5 S2 W0a o2 m20 m21 m22 m23 W1a m24 rcn a6 a7 y0 b0 b1 b2 b3 y1 y2 b4 y3 y4 b5 b6 y5 "
+             "y6 y7 b7 W2a S3 W3a o3 cA"),
+    "TAIL": ("h0 h1 G1 h2 G3 G0 h3 G2 H1a H3a nA H2a h4 H0v h5 nB h6 gA3a gA0a nL gA1a gL2a gA2v gL0a gL1v zA gB1v cL gL3a "
+             "wA gB3a zL gB2a eA1a eA3a wL gB0v eA0v eA2v eL1v zB eL2a eL3v tA cB wB eL0a eB0a pA tL x eB2a pL eB1v eB3v "
+             "sA tB sL pB rA sB rL rB F0 F1 F2 F3 W0a W1a W2a W3a CA a0 a1 a2 a3 a4 a5 a6 a7 b0 b1 b2 b3 b4 b5 b6 b7"),
+    "LAST": ("h0 h1 G3 H3a h2 G0 G2 nA G1 h3 H1v H2a H0a gA3a gA1a h4 h5 nB cL gA2a gB0a h6 gA0v gB2a nL zA gL2a gL3v gL1v "
+             "wA gB1a gL0v zL gB3a wL eA1v eA0v zB eA3a eL2v eL3v eA2a eL1v eL0a cB x wB tA eB0a eB2a pA sA tL eB1v eB3v "
+             "pL sL rA rL tB pB sB rB"),
+}
+
+
+def _clash(a, b):
+    return a[0] == b[0] and a[1] < b[2] and b[1] < a[2] and (a[3] is None or b[3] is None or a[3] == b[3])
+
+
+def _emit(g, T, ops, tail):
+    queue = {"V": g.vector, "A": g.scalar, "P": g.tensor, "G": g, "S": g.sync}
+    total = {}
+    for o in ops:
+        if o["grp"]:
+            total[o["grp"]] = total.get(o["grp"], 0) + o["inc"]
+    known = {k: {} for k in queue}
+    seq = {k: 0 for k in queue}
+    reads, writes = {}, {}
+    for n, o in enumerate(ops):
+        e = o["eng"]
+        need = {}
+        hits = []
+        for a in o["R"]:
+            hits += [p for p, b in writes.get(a[0], []) if _clash(a, b)]
+            if a[0] == "ps":
+                hits += [p for p, b in reads.get(a[0], []) if p["eng"] != e and _clash(a, b)]
+        for a in o["W"]:
+            hits += [p for p, b in writes.get(a[0], []) + reads.get(a[0], []) if _clash(a, b)]
+        for p in hits:
+            if not (p["grp"] and p["grp"] == o["grp"]) and not (o["chain"] and p["eng"] == e):
+                if p["key"] not in need or need[p["key"]]["n"] < p["n"]:
+                    need[p["key"]] = p
+        o["waits"] = []
+        if e is not None:
+            for p in sorted(need.values(), key=lambda p: -p["n"]):
+                if known[e].get(p["key"], 0) < p["val"]:
+                    o["waits"].append(p)
+                    p["sig"] = True
+                    for k, v in p["after"].items():
+                        known[e][k] = max(known[e].get(k, 0), v)
+        o["n"] = n
+        if o["grp"]:
+            o["key"], o["val"] = o["grp"], 1
+        else:
+            seq[e] += 1
+            o["key"], o["val"] = e, seq[e]
+        o["after"] = dict(known[e]) if e is not None else {}
+        o["after"][o["key"]] = o["val"]
+        for a in o["R"]:
+            reads.setdefault(a[0], []).append((o, a))
+        for a in o["W"]:
+            writes.setdefault(a[0], []).append((o, a))
+    count = {k: 0 for k in queue}
+    waited = {}
+    for o in ops:
+        e = o["eng"]
+        if e is None:
+            continue
+        for p in o["waits"]:
+            name, val = (p["grp"], total[p["grp"]]) if p["grp"] else ("s" + p["eng"], p["count"])
+            queue[e].wait_ge(T.sem[name], val)
+            waited[name] = max(waited.get(name, 0), val)
+        ins = o["fn"]()
+        if o["grp"]:
+            if o["dma"]:
+                ins.then_inc(T.sem[o["grp"]], 16)
+        elif o.get("sig"):
+            count[e] += 1
+            o["count"] = count[e]
+            ins.then_inc(T.sem["s" + e], 1)
+    for name in tail:
+        if waited.get(name, 0) < total.get(name, 0):
+            g.wait_ge(T.sem[name], total[name])
+
+
+def rank_program(g, core, T, topo):
+    rank = T.rank_of(core)
+    if rank is None:
+        return
+    n_ranks = len(T.cores)
+    ops = []
+    step = [None]
+    V, A, P, S = g.vector, g.scalar, g.tensor, g.sync
+
+    def reg(xs):
+        return [(x[0], x[1], x[2], x[3] if len(x) > 3 else None) for x in xs]
+
+    def op(eng, fn, R=(), W=(), grp=None, inc=16, dma=True, chain=False):
+        ops.append({"eng": eng, "fn": fn, "R": reg(R), "W": reg(W), "grp": grp, "inc": inc, "dma": dma, "chain": chain,
+                    "step": step[0]})
+
+    def bank(k):
+        return ("ps", BANK * k, BANK * k + BANK)
+
+    def pv(k, a, b):
+        return T.ps[:, BANK * k + a:BANK * k + b]
+
+    def ts(out, in0, s1, s2, op0, op1, R, W):
+        if s2 is None:
+            op("V", lambda: V.tensor_scalar(out, in0, s1, None, op0), R, W)
+        else:
+            op("V", lambda: V.tensor_scalar(out, in0, s1, s2, op0, op1), R, W)
+
+    def tt(out, in0, in1, alu, R, W):
+        op("V", lambda: V.tensor_tensor(out, in0, in1, alu), R, W)
+
+    def cp(out, in_, R, W):
+        op("V", lambda: V.tensor_copy(out, in_), R, W)
+
+    def act(out, in_, func, R, W, scale=1.0, bias=None):
+        if bias is None:
+            op("A", lambda: A.activation(out, in_, func, scale=scale), R, W)
+        else:
+            op("A", lambda: A.activation(out, in_, func, bias=bias, scale=scale), R, W)
+
+    def fill(name, a, b, val):
+        op("V", lambda: V.memset(T[name][:, a:b], val), [], [(name, a, b)])
+
+    def iota(name, a, b, pattern, base, cm, real=True):
+        if real:
+            op("G", lambda: g.iota(T[name][:, a:b], pattern, base, cm, allow_small_or_imprecise_dtypes=True), [], [(name, a, b)])
+        else:
+            op("G", lambda: g.iota(T[name][:, a:b], pattern, base, cm), [], [(name, a, b)])
+
+    def quant(q, s, a, b, src, c0):
+        op("V", lambda: V.quantize_mx(T[q][:, a:b], T[s][:, a:b], T[src][:, c0:c0 + 4 * (b - a)]),
+           [(src, c0, c0 + 4 * (b - a))], [(q, a, b), (s, a, b)])
+
+    def mm(k, wq, ws, wa, q, s, a, b, start, stop):
+        op("P", lambda: P.matmul_mx(pv(k, 0, b - a), T[wq][:, wa:wa + 128], T[ws][:, wa:wa + 128],
+                                    T[q][:, a:b], T[s][:, a:b], start, stop),
+           [(wq, wa, wa + 128), (ws, wa, wa + 128), (q, a, b), (s, a, b)], [bank(k)], chain=not start)
+
+    def col(k):
+        return T.col[:, k:k + 1]
+
+    def creg(k):
+        return ("col", k, k + 1)
+
+    def whole(name):
+        return (name, 0, SCRATCH[name][1][1])
+
+    CB, C1, C8, C2, C3, CR, C28, C8I = 0, 1, 2, 3, 4, 5, 6, 7
+
+    def scan(out, a, b, src, lo, hi, stride):
+        op("V", lambda: V.tensor_tensor_scan(T[out][:, a:b], T.kk[:, 0:b - a], T[src][:, lo:hi:stride], 0.0, ALU.add, ALU.max),
+           [("kk", 0, b - a), (src, lo, hi)], [(out, a, b)])
+
+    def scans(base, n):
+        for k in range(n):
+            scan("vs", 64 * k, 64 * k + 64, "vw", base + k, base + 512, 8)
+
+    def phase_op(src, lo, hi, dst, base, k, offs, copy):
+        a = base + 64 * k
+        if copy:
+            cp(T[dst][:, a:a + 64], T[src][:, lo + k:hi:8], [(src, lo, hi)], [(dst, a, a + 64)])
+        else:
+            tt(T[dst][:, a:a + 64], T[dst][:, 0:a].indirect(T[offs][:, 4 * k:4 * k + 4]), T[src][:, lo + k:hi:8], ALU.max,
+               [(src, lo, hi), (dst, 0, a), (offs, 4 * k, 4 * k + 4)], [(dst, a, a + 64)])
+
+    def phase1(k):
+        phase_op("r0", 0, 512, "ra", PAD, k, "o1", k == 0)
+
+    def phase2(k):
+        phase_op("ra", PAD, PAD + 512, "rb", PAD, k, "o2", k == 0)
+
+    def follow(base, k, offs):
+        a = base + 512 + 64 * k
+        act(T.vw[:, a:a + 64], T.vw[:, base:a].indirect(T[offs][:, 4 * k:4 * k + 4]), ACT.Copy,
+            [("vw", base, a), (offs, 4 * k, 4 * k + 4)], [("vw", a, a + 64)])
+
+    def own_or(k, src, dst):
+        if k == 0:
+            ts(T.m0[:], T[src][:], float(PAD), -4 * BIG, ALU.is_lt, ALU.mult, [whole(src)], [whole("m0")])
+        elif k == 1:
+            ts(T.m1[:], T[src][:], 512.0 - PAD, None, ALU.add, None, [whole(src)], [whole("m1")])
+        elif k == 2:
+            tt(T.m2[:], T.m0[:], T.m1[:], ALU.add, [whole("m0"), whole("m1")], [whole("m2")])
+        elif k == 3:
+            tt(T.m3[:], T.m2[:], T.cj[:], ALU.max, [whole("m2"), whole("cj")], [whole("m3")])
+        else:
+            cp(T[dst][:], T.m3[:], [whole("m3")], [whole(dst)])
+
+    def send(t):
+        if rank + 1 >= n_ranks:
+            return
+        dst = T.cores[rank + 1]
+        rid, pid = topo.addr(dst, core)
+        mask = topo.mask(core, dst)
+        n_eng = len(topo.engines(core, dst))
+        q, s = "q%d" % t, "s%d" % t
+        op("G", lambda: g.remote_dma(T[q][:, C:C + H].bitcast(dt.uint8), T[q][:, LO:C].bitcast(dt.uint8),
+                                     T.sem["arr%d" % t], T.sem.sent, pid, rid, mask), [(q, LO, C)], [], "sent", n_eng, False)
+        op("G", lambda: g.remote_dma(T[s][:, C:C + H], T[s][:, LO:C],
+                                     T.sem["arr%d" % t], T.sem.sent, pid, rid, mask), [(s, LO, C)], [], "sent", n_eng, False)
+
+    def arrive(t):
+        if rank > 0:
+            n_eng = len(topo.engines(T.cores[rank - 1], core))
+            op(None, None, [], [("q%d" % t, C, C + H), ("s%d" % t, C, C + H)], "arr%d" % t, 2 * n_eng, False)
+
+    def heads(t, a, b, k):
+        mm(k, "qu", "su", 0, "q%d" % t, "s%d" % t, a, b, True, True)
+
+    def signs(a, b, k):
+        act(T.sg[:, a:b], pv(k, 0, b - a), ACT.Sign, [bank(k)], [("sg", a, b)])
+
+    def first(a, b):
+        op("V", lambda: V.tensor_tensor_scan(T.r0[:, a:b], T.jq[:, a:b], T.sg[:, a:b], -2.0, ALU.max, ALU.min),
+           [("jq", a, b), ("sg", a, b)], [("r0", a, b)])
+
+    def sums(t, ch):
+        a, b, k0, kp = CHUNK[ch]
+        for k in range(4):
+            mm(k0 + k, "qe", "se", 128 * k, "q%d" % t, "s%d" % t, a, b, True, False)
+
+    def scaled(out, k, n, W, eng):
+        if eng == "v":
+            ts(out, pv(k, 0, n), 1.0 / 64, None, ALU.mult, None, [bank(k)], W)
+        else:
+            act(out, pv(k, 0, n), ACT.Copy, [bank(k)], W, scale=1.0 / 64)
+
+    def unpack(t, k, far):
+        if not far:
+            mm(k, "qe", "se", 128 * k, "q%d" % t, "s%d" % t, 0, C, True, True)
+        elif rank > 0:
+            mm(4 + k, "qe", "se", 128 * k, "q%d" % t, "s%d" % t, C, C + H, True, True)
+
+    def window(t, k, far, eng):
+        fw, w = "fw%d" % t, (H + C) * k
+        if not far:
+            scaled(T[fw][:, w + H:w + H + C], k, C, [(fw, w + H, w + H + C)], eng)
+        elif rank > 0:
+            scaled(T[fw][:, w:w + H], 4 + k, H, [(fw, w, w + H)], eng)
+
+    def lists(ch):
+        a, b, k0, kp = CHUNK[ch]
+        scan("rs", a, b, "rc", H + a, H + b, 1)
+        ts(T.off[:, a // 16:b // 16], T.rs[:, a + 15:b:16], col(CR), BIG, ALU.subtract, ALU.mult,
+           [("rs", a, b), creg(CR)], [("off", a // 16, b // 16)])
+
+    def gather(t, ch, k, eng):
+        a, b, k0, kp = CHUNK[ch]
+        fw = "fw%d" % t
+        w = (H + C) * k
+        R = [(fw, w, w + H + b), ("off", a // 16, b // 16)]
+        W = [("zt", 4 * a, 4 * b, k)]
+        src = T[fw][:, w:w + H + b].indirect(T.off[:, a // 16:b // 16])
+        if eng == "v":
+            cp(T.zt[:, 4 * a + k:4 * b:4], src, R, W)
+        else:
+            act(T.zt[:, 4 * a + k:4 * b:4], src, ACT.Copy, R, W)
+
+    def layer(ch):
+        a, b, k0, kp = CHUNK[ch]
+        for k in range(4):
+            mm(k0 + k, "qw", "sw", 128 * k, "qz", "sz", a, b, False, True)
+
+    def state(t, ch, k, eng):
+        a, b, k0, kp = CHUNK[ch]
+        tn = "tt%d" % (t + 1)
+        scaled(T[tn][:, 4 * a + k:4 * b:4], k0 + k, b - a, [(tn, 4 * a, 4 * b, k)], eng)
+
+    def zero_halo():
+        if rank == 0:
+            for t in range(ROUNDS):
+                for k in range(4):
+                    fill("fw%d" % t, (H + C) * k, (H + C) * k + H, 0.0)
+
+    def own_slots():
+        act(col(C8I), T.pf[:, 0:1], ACT.Copy, [("pf", 0, 1)], [creg(C8I)], 8.0)
+        act(T.cj[:], T.cj0[:], ACT.Identity, [whole("cj0"), creg(C8I)], [whole("cj")], 1.0, col(C8I))
+
+    for t in range(ROUNDS):
+        arrive(t)
+    for i in range(16):
+        eng, q = ("S", S) if i % 2 == 0 else ("A", A)
+        op(eng, lambda i=i, q=q: q.dma_start(T.drep[i::16, :], T.dist[:]), [], [("drep", 0, C)], "dD")
+    op("S", lambda: S.dma_start(T.xt[:, 4 * LO:4 * C], T.x[:, 4 * LO:4 * C]), [], [("xt", 4 * LO, 4 * C)], "dXL")
+    op("A", lambda: A.dma_start(T.ut[:], T.u[:]), [], [("ut", 0, 512)], "dU")
+    op("S", lambda: S.dma_start(T.xt[:, 0:4 * LO], T.x[:, 0:4 * LO]), [], [("xt", 0, 4 * LO)], "dXF")
+    op("S", lambda: S.dma_start(T.qw[:].bitcast(dt.uint8), T.wc[:]), [], [("qw", 0, 512)], "dW")
+    op("S", lambda: S.dma_start(T.sw[:], T.ws[:]), [], [("sw", 0, 512)], "dW")
+    op("S", lambda: S.dma_start(T.vt[:], T.v[:]), [], [("vt", 0, 512)], "dV")
+
+    i_col, ireg = T.pf[:, 0:1], ("pf", 0, 1)
+    head = {
+        "i0": lambda: iota("pi", 0, 1, [[0, 1]], 0, 1, False),
+        "i1": lambda: iota("pi", 1, 2, [[0, 1]], 0, 2, False),
+        "i2": lambda: iota("jn", H - 8, JW, [[1, JW - H + 8]], -8, 0),
+        "i3": lambda: iota("p4", 0, 1, [[0, 1]], 3, 4),
+        "i4": lambda: iota("c16", 0, 32, [[0, 8], [16, 4]], 0, 0),
+        "i5": lambda: iota("cj0", 0, 32, [[1, 8], [128, 4]], 0, 0),
+        "i6": lambda: iota("jn", 0, H - 8, [[1, H - 8]], -H, 0),
+        "z0": lambda: fill("vw", C, 512, float(H)),
+        "z1": lambda: fill("r0", C, 512, -1.0),
+        "z2": lambda: fill("ra", 0, PAD, -2 * BIG),
+        "z3": lambda: fill("rb", 0, PAD, -2 * BIG),
+        "zf": zero_halo,
+        "pm": lambda: ts(T.pm[:], T.pi[:], 15, None, ALU.bitwise_and, None, [whole("pi")], [whole("pm")]),
+        "c28": lambda: ts(col(C28), T.pm[:, 0:1], 28.0, None, ALU.mult, None, [("pm", 0, 1)], [creg(C28)]),
+        "pf": lambda: cp(T.pf[:], T.pm[:], [whole("pm")], [whole("pf")]),
+        "cb": lambda: ts(col(CB), T.pm[:, 0:1], 15.0, BIG, ALU.is_lt, ALU.mult, [("pm", 0, 1)], [creg(CB)]),
+        "c1": lambda: ts(col(C1), i_col, -511.0 / 64, col(CB), ALU.mult, ALU.add, [ireg, creg(CB)], [creg(C1)]),
+        "k0": lambda: ts(T.k0[:], T.jn[:, H:H + 16], i_col, -2 * BIG, ALU.is_equal, ALU.mult, [("jn", H, H + 16), ireg], [whole("k0")]),
+        "k1": lambda: ts(T.k1[:], T.jn[:, H - 1:H + 15], i_col, BIG, ALU.is_equal, ALU.mult, [("jn", H - 1, H + 15), ireg], [whole("k1")]),
+        "lo": lambda: ts(T.lo[:, 0:28], T.jn[:, H:H + 28], col(C28), None, ALU.add, None, [("jn", H, H + 28), creg(C28)], [("lo", 0, 28)]),
+        "kk": lambda: tt(T.kk[:, 0:16], T.k0[:], T.k1[:], ALU.add, [whole("k0"), whole("k1")], [("kk", 0, 16)]),
+        "uo": lambda: cp(T.uo[:], T.jn[:, H:H + 128:16], [("jn", H, H + 128)], [whole("uo")]),
+        "em": lambda: ts(T.em[:], T.jn[:, H:H + 520], T.p4[:], 64.0, ALU.is_equal, ALU.mult, [("jn", H, JW), whole("p4")], [whole("em")]),
+        "c1w": lambda: ts(T.c1[:], T.c16[:], -511.0 / 64, col(C1), ALU.mult, ALU.add, [whole("c16"), creg(C1)], [whole("c1")]),
+        "cj": own_slots,
+        "c8": lambda: act(col(C8), col(CB), ACT.Identity, [creg(CB)], [creg(C8)], 8.0, 8.0),
+        "c3": lambda: act(col(C3), col(CB), ACT.Identity, [creg(CB)], [creg(C3)], 1.0, float(H)),
+        "cr": lambda: act(col(CR), col(CB), ACT.Identity, [creg(CB)], [creg(CR)], 1.0, -0.625),
+        "c2": lambda: act(col(C2), T.pf[:, 1:2], ACT.Identity, [("pf", 1, 2), creg(C8)], [creg(C2)], -255.5, col(C8)),
+        "jq": lambda: act(T.jq[:], T.jn[:, H:H + C], ACT.Identity, [("jn", H, H + C)], [whole("jq")], 1.0 / BIG, -0.5),
+        "rcn": lambda: act(T.rc[:, 0:H], T.jn[:, 0:H], ACT.Identity, [("jn", 0, H)], [("rc", 0, H)], 1.0 / BIG, -0.5),
+        "v0": lambda: tt(T.vw[:, 0:C], T.drep[:].indirect(T.lo[:, 0:28]), T.jn[:, H:H + C], ALU.subtract,
+                         [whole("drep"), ("lo", 0, 28), ("jn", H, H + C)], [("vw", 0, C)]),
+        "qL": lambda: quant("q0", "s0", LO, C, "xt", 4 * LO),
+        "qF": lambda: quant("q0", "s0", 0, LO, "xt", 0),
+        "qu": lambda: quant("qu0", "su0", 0, 128, "ut", 0),
+        "qv": lambda: quant("qv", "sv", 0, 128, "vt", 0),
+        "x": lambda: send(0),
+        "S1": lambda: scans(0, 8),
+        "S2": lambda: scans(512, 8),
+        "S3": lambda: scans(1024, 7),
+        "t1": lambda: tt(T.t1[:], T.vs[:, 15:512:16], T.c1[:], ALU.subtract, [whole("vs"), whole("c1")], [whole("t1")]),
+        "pk": lambda: cp(T.qu[:].bitcast(dt.uint32), T.qu0[:].bitcast(dt.uint32).indirect(T.uo[:]), [whole("qu0"), whole("uo")], [whole("qu")]),
+        "ps": lambda: op("A", lambda: A.activation(T.su[:], T.su0[:].indirect(T.uo[:]), ACT.Copy), [whole("su0"), whole("uo")], [whole("su")]),
+        "o1": lambda: ts(T.o1[:], T.t1[:], -64.0, float(PAD), ALU.mult, ALU.add, [whole("t1")], [whole("o1")]),
+        "o2": lambda: ts(T.o2[:], T.vs[:, 15:512:16], -8.0, col(C2), ALU.mult, ALU.add, [whole("vs"), creg(C2)], [whole("o2")]),
+        "o3": lambda: ts(T.o3[:, 0:28], T.vs[:, 15:C:16], -1.0, col(C3), ALU.mult, ALU.add, [whole("vs"), creg(C3)], [("o3", 0, 28)]),
+        "P": lambda: heads(0, 0, C, 4),
+        "sg": lambda: signs(0, C, 4),
+        "r0": lambda: first(0, C),
+        "cA": lambda: sums(0, "A"),
+    }
+    for w in (16, 32, 64, 128):
+        head["kk%d" % w] = lambda w=w: act(T.kk[:, w:2 * w], T.kk[:, 0:w], ACT.Copy, [("kk", 0, w)], [("kk", w, 2 * w)])
+    for k in range(8):
+        head["u%d" % k] = lambda k=k: follow(0, k, "f1")
+        head["y%d" % k] = lambda k=k: follow(512, k, "f2")
+        head["a%d" % k] = lambda k=k: phase1(k)
+        head["b%d" % k] = lambda k=k: phase2(k)
+    for k in range(5):
+        head["m1%d" % k] = lambda k=k: own_or(k, "o1", "f1")
+        head["m2%d" % k] = lambda k=k: own_or(k, "o2", "f2")
+    for k in range(4):
+        head["qe%d" % k] = lambda k=k: quant("qe", "se", 128 * k, 128 * k + 128, "em", 3 - k)
+        head["F%d" % k] = lambda k=k: unpack(0, k, False)
+        for eng in "av":
+            head["W%d%s" % (k, eng)] = lambda k=k, eng=eng: window(0, k, False, eng)
+    for w in ORDER["HEAD"].split():
+        step[0] = ("HEAD", w)
+        head[w]()
+
+    for t in range(ROUNDS):
+        last = t == ROUNDS - 1
+        part = "LAST" if last else "TAIL"
+        final = [w[1] for w in ORDER[part].split() if w[0] == "t"][-1]
+        qn, sn, tn = "q%d" % (t + 1), "s%d" % (t + 1), "tt%d" % (t + 1)
+        for w in ORDER[part].split():
+            step[0] = (part if t != 1 else None, w)
+            kind = w[0]
+            if kind == "x":
+                if not last:
+                    send(t + 1)
+                else:
+                    act(T.olb[:], T.rc[:, H:H + C], ACT.Identity, [("rc", H, H + C)], [whole("olb")], BIG, 512.0)
+                    op("G", lambda: g.dma_start(T.ol[:], T.olb[0::16, :]), [whole("olb")], [], "dOl")
+                continue
+            if kind in "FGWHabh":
+                k = int(w[1])
+                if kind == "F":
+                    unpack(t + 1, k, False)
+                elif kind == "W":
+                    window(t + 1, k, False, w[2])
+                elif kind == "G":
+                    unpack(t, k, True)
+                elif kind == "H":
+                    window(t, k, True, w[2])
+                elif kind == "a":
+                    phase1(k)
+                elif kind == "b":
+                    phase2(k)
+                else:
+                    phase_op("rb", PAD, PAD + 512, "rc", H, k, "o3", False)
+                continue
+            ch = w[1]
+            a, b, k0, kp = CHUNK[ch]
+            if kind == "n":
+                lists(ch)
+            elif kind == "g":
+                gather(t, ch, int(w[2]), w[3])
+            elif kind == "z":
+                quant("qz", "sz", a, b, "zt", 4 * a)
+            elif kind == "w":
+                layer(ch)
+            elif kind == "c":
+                sums(t, ch)
+            elif kind == "C":
+                sums(t + 1, ch)
+            elif kind == "e":
+                state(t, ch, int(w[2]), w[3])
+            elif kind == "t":
+                quant(qn, sn, a, b, tn, 4 * a)
+                if last:
+                    op("S", lambda a=a, b=b, qn=qn: S.dma_start(T.oc[:, 4 * a:4 * b], T[qn][:, a:b].bitcast(dt.uint8)), [(qn, a, b)], [], "dOut")
+                if last and ch == final:
+                    for k in range(4):
+                        eng, q = [("S", S), ("A", A)][k % 2]
+                        op(eng, lambda k=k, q=q, sn=sn: q.dma_start(T.osc[4 * k:4 * k + 4, :], T[sn][32 * k:32 * k + 4, 0:C]),
+                           [(sn, 0, C)], [], "dOut")
+            elif kind == "p":
+                if not last:
+                    heads(t + 1, a, b, kp)
+                else:
+                    mm(kp, "qv", "sv", 0, qn, sn, a, b, True, True)
+            elif kind == "s":
+                if not last:
+                    signs(a, b, kp)
+                elif ch == final:
+                    cp(T.yb[:, a:b], pv(kp, 0, b - a), [bank(kp)], [("yb", a, b)])
+                else:
+                    act(T.yb[:, a:b], pv(kp, 0, b - a), ACT.Copy, [bank(kp)], [("yb", a, b)])
+            elif kind == "r":
+                if not last:
+                    first(a, b)
+                else:
+                    eng, q = ("A", A) if ch == final else ("S", S)
+                    op(eng, lambda a=a, b=b, q=q: q.dma_start(T.y[:, a:b], T.yb[:, a:b]), [("yb", a, b)], [], "dOut")
+
+    _emit(g, T, ops, ["sent", "dOl", "dOut"])

@@ -12,14 +12,14 @@ X4, U8, F32, BF, I32, U16 = "float8_e4m3fn_x4", "uint8", "float32", "bfloat16", 
 SCRATCH = {"ps": ("psum", [128, 8 * BANK], F32)}
 for _ty, _bufs in (
         (I32, {"drep": C, "pi": 2, "pm": 2}),
-        (BF, {"xt": 4 * C, "ut": 512, "vt": 512, "em": 520, "zt": 4 * C, "tt1": 4 * C, "tt2": 4 * C, "tt3": 4 * C,
-              "fw0": 4 * (H + C), "fw1": 4 * (H + C), "fw2": 4 * (H + C)}),
+        (BF, {"xt": 4 * C, "ut": 512, "vt": 512, "em": 520, "zt": 4 * C, "tt1": 4 * C,
+              "tt2": 4 * C, "tt3": 4 * C, "fw0": 4 * (H + C), "fw1": 4 * (H + C), "fw2": 4 * (H + C)}),
         (X4, {"qu0": 128, "qu": 128, "qv": 128, "qw": 512, "qe": 512, "qz": C, "q0": C + H, "q1": C + H, "q2": C + H, "q3": C + H}),
         (U8, {"su0": 128, "su": 128, "sv": 128, "sw": 512, "se": 512, "sz": C, "s0": C + H, "s1": C + H, "s2": C + H, "s3": C + H}),
-        (U16, {"o1": 32, "o2": 32, "o3": 32, "f1": 32, "f2": 32, "off": 32, "lo": 32, "uo": 8}),
-        (F32, {"sg": C, "r0": 512, "ra": PAD + 512, "rb": PAD + 512, "rc": H + C, "rs": C, "vw": 3 * 512, "vs": 512,
-               "t1": 32, "m0": 32, "m1": 32, "m2": 32, "m3": 32, "pf": 2, "p4": 1, "jn": JW, "jq": C, "c16": 32, "cj0": 32,
-               "cj": 32, "kk": 256, "k0": 16, "k1": 16, "col": 8, "c1": 32, "olb": C, "yb": C})):
+        (U16, {"o1": 32, "o2": 32, "o3": 32, "off": 32, "lo": 32, "uo": 8}),
+        (F32, {"sg": C, "r0": 512, "ra": PAD + 512, "rb": PAD + 512, "rc": H + C, "rs": C, "v0": 512, "va": PAD + 512,
+               "vb": PAD + 512, "vs": 512, "t1": 32, "pf": 2, "p4": 1, "jn": JW, "jq": C, "c16": 32,
+               "kk": 256, "k0": 16, "k1": 16, "col": 8, "c1": 32, "olb": C, "yb": C})):
     for _name, _n in _bufs.items():
         SCRATCH[_name] = ("sbuf", [128, _n], _ty)
 
@@ -31,16 +31,15 @@ ALU, ACT = AluOpType, ActivationFunctionType
 CHUNK = {"A": (0, MID, 0, 5), "L": (LO, C, 4, 4), "B": (MID, LO, 0, 6)}
 
 ORDER = {
-    "HEAD": ("zf z0 i0 i1 i2 pm cb c28 pf i3 i4 i5 c1 k1 k0 jq em kk uo kk16 c8 cj qe1 lo cr c1w qe0 v0 kk32 qL qu ps S1 pk "
-             "qF x kk64 t1 o1 m10 m11 P kk128 z1 F0 m12 z2 m13 c3 i6 z3 sg m14 qe3 u0 qv u1 r0 u2 qe2 a0 u3 u4 a1 a2 u5 u6 "
-             "u7 F3 F1 a3 a4 c2 F2 a5 S2 W0a o2 m20 m21 m22 m23 W1a m24 rcn a6 a7 y0 b0 b1 b2 b3 y1 y2 b4 y3 y4 b5 b6 y5 "
-             "y6 y7 b7 W2a S3 W3a o3 cA"),
-    "TAIL": ("h0 h1 G1 h2 G3 G0 h3 G2 H1a H3a nA H2a h4 H0v h5 nB h6 gA3a gA0a nL gA1a gL2a gA2v gL0a gL1v zA gB1v cL gL3a "
-             "wA gB3a zL gB2a eA1a eA3a wL gB0v eA0v eA2v eL1v zB eL2a eL3v tA cB wB eL0a eB0a pA tL x eB2a pL eB1v eB3v "
-             "sA tB sL pB rA sB rL rB F0 F1 F2 F3 W0a W1a W2a W3a CA a0 a1 a2 a3 a4 a5 a6 a7 b0 b1 b2 b3 b4 b5 b6 b7"),
-    "LAST": ("h0 h1 G3 H3a h2 G0 G2 nA G1 h3 H1v H2a H0a gA3a gA1a h4 h5 nB cL gA2a gB0a h6 gA0v gB2a nL zA gL2a gL3v gL1v "
-             "wA gB1a gL0v zL gB3a wL eA1v eA0v zB eA3a eL2v eL3v eA2a eL1v eL0a cB x wB tA eB0a eB2a pA sA tL eB1v eB3v "
-             "pL sL rA rL tB pB sB rB"),
+    "HEAD": ("zf z3 i0 i1 i2 pm z2 pf cb c28 z0 i3 c1 c8 k1 k0 i4 lo cr i6 em uo kk c1w v0 c3 rcn kk16 kk32 qu qL x S1 pk qF "
+             "t1 qe2 u0 ps o1 jq qe1 u1 z1 u2 P sg qe0 u3 r0 u4 a0 c2 qe3 a1 u5 F3 a2 F1 F2 u6 a3 W2a u7 F0 a4 W1a S2 kk64 "
+             "a5 y0 o2 a6 qv a7 y1 b0 y2 b1 y3 b2 y4 kk128 b3 y5 b4 y6 b5 y7 b6 W0a S3 b7 W3a o3 cA"),
+    "TAIL": ("h0 G0 h1 G2 h2 h3 H2a nA h4 H0v G1 H1v G3 gA0a h5 gA1a gA2a H3v h6 nB gA3a nL gB3v gL3v gL0a cL gL2a gB1a gB0a "
+             "zA gL1v gB2v zL wA eA0v eA1a eA2v eA3a wL eL1a zB eL0v cB wB eL2v eL3v tL pL eB0a tA pA eB1a x eB3a sL eB2v "
+             "tB pB sA rA rL sB rB F0 F1 F2 F3 W0a W1a W2a W3a CA a0 a1 a2 a3 a4 a5 a6 a7 b0 b1 b2 b3 b4 b5 b6 b7"),
+    "LAST": ("G3 H3a G2 h0 H2a G0 G1 h1 h2 h3 nA h4 h5 H0v H1v h6 gA3a gA1a gA2v gA0a nL nB zA gL1v wA gL0a gL2v cL gB1v gL3a "
+             "x zL gB2a wL eA1v eA0v eA2v gB3a eL1v eA3a tA gB0a zB cB pA eL0v eL3a eL2v sA wB tL pL eB1a eB3a eB0v eB2v "
+             "sL tB rA pB sB rB rL"),
 }
 
 
@@ -120,15 +119,13 @@ def rank_program(g, core, T, topo):
         return
     n_ranks = len(T.cores)
     ops = []
-    step = [None]
     V, A, P, S = g.vector, g.scalar, g.tensor, g.sync
 
     def reg(xs):
         return [(x[0], x[1], x[2], x[3] if len(x) > 3 else None) for x in xs]
 
     def op(eng, fn, R=(), W=(), grp=None, inc=16, dma=True, chain=False):
-        ops.append({"eng": eng, "fn": fn, "R": reg(R), "W": reg(W), "grp": grp, "inc": inc, "dma": dma, "chain": chain,
-                    "step": step[0]})
+        ops.append({"eng": eng, "fn": fn, "R": reg(R), "W": reg(W), "grp": grp, "inc": inc, "dma": dma, "chain": chain})
 
     def bank(k):
         return ("ps", BANK * k, BANK * k + BANK)
@@ -181,15 +178,15 @@ def rank_program(g, core, T, topo):
     def whole(name):
         return (name, 0, SCRATCH[name][1][1])
 
-    CB, C1, C8, C2, C3, CR, C28, C8I = 0, 1, 2, 3, 4, 5, 6, 7
+    CB, C1, C8, C2, C3, CR, C28 = 0, 1, 2, 3, 4, 5, 6
 
     def scan(out, a, b, src, lo, hi, stride):
         op("V", lambda: V.tensor_tensor_scan(T[out][:, a:b], T.kk[:, 0:b - a], T[src][:, lo:hi:stride], 0.0, ALU.add, ALU.max),
            [("kk", 0, b - a), (src, lo, hi)], [(out, a, b)])
 
-    def scans(base, n):
+    def scans(src, base, n):
         for k in range(n):
-            scan("vs", 64 * k, 64 * k + 64, "vw", base + k, base + 512, 8)
+            scan("vs", 64 * k, 64 * k + 64, src, base + k, base + 512, 8)
 
     def phase_op(src, lo, hi, dst, base, k, offs, copy):
         a = base + 64 * k
@@ -199,28 +196,11 @@ def rank_program(g, core, T, topo):
             tt(T[dst][:, a:a + 64], T[dst][:, 0:a].indirect(T[offs][:, 4 * k:4 * k + 4]), T[src][:, lo + k:hi:8], ALU.max,
                [(src, lo, hi), (dst, 0, a), (offs, 4 * k, 4 * k + 4)], [(dst, a, a + 64)])
 
-    def phase1(k):
-        phase_op("r0", 0, 512, "ra", PAD, k, "o1", k == 0)
+    def phase1(k, src="r0", dst="ra"):
+        phase_op(src, 0, 512, dst, PAD, k, "o1", k == 0)
 
-    def phase2(k):
-        phase_op("ra", PAD, PAD + 512, "rb", PAD, k, "o2", k == 0)
-
-    def follow(base, k, offs):
-        a = base + 512 + 64 * k
-        act(T.vw[:, a:a + 64], T.vw[:, base:a].indirect(T[offs][:, 4 * k:4 * k + 4]), ACT.Copy,
-            [("vw", base, a), (offs, 4 * k, 4 * k + 4)], [("vw", a, a + 64)])
-
-    def own_or(k, src, dst):
-        if k == 0:
-            ts(T.m0[:], T[src][:], float(PAD), -4 * BIG, ALU.is_lt, ALU.mult, [whole(src)], [whole("m0")])
-        elif k == 1:
-            ts(T.m1[:], T[src][:], 512.0 - PAD, None, ALU.add, None, [whole(src)], [whole("m1")])
-        elif k == 2:
-            tt(T.m2[:], T.m0[:], T.m1[:], ALU.add, [whole("m0"), whole("m1")], [whole("m2")])
-        elif k == 3:
-            tt(T.m3[:], T.m2[:], T.cj[:], ALU.max, [whole("m2"), whole("cj")], [whole("m3")])
-        else:
-            cp(T[dst][:], T.m3[:], [whole("m3")], [whole(dst)])
+    def phase2(k, src="ra", dst="rb"):
+        phase_op(src, PAD, PAD + 512, dst, PAD, k, "o2", k == 0)
 
     def send(t):
         if rank + 1 >= n_ranks:
@@ -308,16 +288,12 @@ def rank_program(g, core, T, topo):
                 for k in range(4):
                     fill("fw%d" % t, (H + C) * k, (H + C) * k + H, 0.0)
 
-    def own_slots():
-        act(col(C8I), T.pf[:, 0:1], ACT.Copy, [("pf", 0, 1)], [creg(C8I)], 8.0)
-        act(T.cj[:], T.cj0[:], ACT.Identity, [whole("cj0"), creg(C8I)], [whole("cj")], 1.0, col(C8I))
-
     for t in range(ROUNDS):
         arrive(t)
     for i in range(16):
         eng, q = ("S", S) if i % 2 == 0 else ("A", A)
         op(eng, lambda i=i, q=q: q.dma_start(T.drep[i::16, :], T.dist[:]), [], [("drep", 0, C)], "dD")
-    op("S", lambda: S.dma_start(T.xt[:, 4 * LO:4 * C], T.x[:, 4 * LO:4 * C]), [], [("xt", 4 * LO, 4 * C)], "dXL")
+    op("A", lambda: A.dma_start(T.xt[:, 4 * LO:4 * C], T.x[:, 4 * LO:4 * C]), [], [("xt", 4 * LO, 4 * C)], "dXL")
     op("A", lambda: A.dma_start(T.ut[:], T.u[:]), [], [("ut", 0, 512)], "dU")
     op("S", lambda: S.dma_start(T.xt[:, 0:4 * LO], T.x[:, 0:4 * LO]), [], [("xt", 0, 4 * LO)], "dXF")
     op("S", lambda: S.dma_start(T.qw[:].bitcast(dt.uint8), T.wc[:]), [], [("qw", 0, 512)], "dW")
@@ -331,12 +307,11 @@ def rank_program(g, core, T, topo):
         "i2": lambda: iota("jn", H - 8, JW, [[1, JW - H + 8]], -8, 0),
         "i3": lambda: iota("p4", 0, 1, [[0, 1]], 3, 4),
         "i4": lambda: iota("c16", 0, 32, [[0, 8], [16, 4]], 0, 0),
-        "i5": lambda: iota("cj0", 0, 32, [[1, 8], [128, 4]], 0, 0),
         "i6": lambda: iota("jn", 0, H - 8, [[1, H - 8]], -H, 0),
-        "z0": lambda: fill("vw", C, 512, float(H)),
+        "z0": lambda: fill("v0", C, 512, float(H)),
         "z1": lambda: fill("r0", C, 512, -1.0),
-        "z2": lambda: fill("ra", 0, PAD, -2 * BIG),
-        "z3": lambda: fill("rb", 0, PAD, -2 * BIG),
+        "z2": lambda: [fill(n, 0, PAD, -2 * BIG) for n in ("ra", "va")],
+        "z3": lambda: [fill(n, 0, PAD, -2 * BIG) for n in ("rb", "vb")],
         "zf": zero_halo,
         "pm": lambda: ts(T.pm[:], T.pi[:], 15, None, ALU.bitwise_and, None, [whole("pi")], [whole("pm")]),
         "c28": lambda: ts(col(C28), T.pm[:, 0:1], 28.0, None, ALU.mult, None, [("pm", 0, 1)], [creg(C28)]),
@@ -350,23 +325,22 @@ def rank_program(g, core, T, topo):
         "uo": lambda: cp(T.uo[:], T.jn[:, H:H + 128:16], [("jn", H, H + 128)], [whole("uo")]),
         "em": lambda: ts(T.em[:], T.jn[:, H:H + 520], T.p4[:], 64.0, ALU.is_equal, ALU.mult, [("jn", H, JW), whole("p4")], [whole("em")]),
         "c1w": lambda: ts(T.c1[:], T.c16[:], -511.0 / 64, col(C1), ALU.mult, ALU.add, [whole("c16"), creg(C1)], [whole("c1")]),
-        "cj": own_slots,
         "c8": lambda: act(col(C8), col(CB), ACT.Identity, [creg(CB)], [creg(C8)], 8.0, 8.0),
         "c3": lambda: act(col(C3), col(CB), ACT.Identity, [creg(CB)], [creg(C3)], 1.0, float(H)),
         "cr": lambda: act(col(CR), col(CB), ACT.Identity, [creg(CB)], [creg(CR)], 1.0, -0.625),
         "c2": lambda: act(col(C2), T.pf[:, 1:2], ACT.Identity, [("pf", 1, 2), creg(C8)], [creg(C2)], -255.5, col(C8)),
         "jq": lambda: act(T.jq[:], T.jn[:, H:H + C], ACT.Identity, [("jn", H, H + C)], [whole("jq")], 1.0 / BIG, -0.5),
         "rcn": lambda: act(T.rc[:, 0:H], T.jn[:, 0:H], ACT.Identity, [("jn", 0, H)], [("rc", 0, H)], 1.0 / BIG, -0.5),
-        "v0": lambda: tt(T.vw[:, 0:C], T.drep[:].indirect(T.lo[:, 0:28]), T.jn[:, H:H + C], ALU.subtract,
-                         [whole("drep"), ("lo", 0, 28), ("jn", H, H + C)], [("vw", 0, C)]),
+        "v0": lambda: tt(T.v0[:, 0:C], T.drep[:].indirect(T.lo[:, 0:28]), T.jn[:, H:H + C], ALU.subtract,
+                         [whole("drep"), ("lo", 0, 28), ("jn", H, H + C)], [("v0", 0, C)]),
         "qL": lambda: quant("q0", "s0", LO, C, "xt", 4 * LO),
         "qF": lambda: quant("q0", "s0", 0, LO, "xt", 0),
         "qu": lambda: quant("qu0", "su0", 0, 128, "ut", 0),
         "qv": lambda: quant("qv", "sv", 0, 128, "vt", 0),
         "x": lambda: send(0),
-        "S1": lambda: scans(0, 8),
-        "S2": lambda: scans(512, 8),
-        "S3": lambda: scans(1024, 7),
+        "S1": lambda: scans("v0", 0, 8),
+        "S2": lambda: scans("va", PAD, 8),
+        "S3": lambda: scans("vb", PAD, 7),
         "t1": lambda: tt(T.t1[:], T.vs[:, 15:512:16], T.c1[:], ALU.subtract, [whole("vs"), whole("c1")], [whole("t1")]),
         "pk": lambda: cp(T.qu[:].bitcast(dt.uint32), T.qu0[:].bitcast(dt.uint32).indirect(T.uo[:]), [whole("qu0"), whole("uo")], [whole("qu")]),
         "ps": lambda: op("A", lambda: A.activation(T.su[:], T.su0[:].indirect(T.uo[:]), ACT.Copy), [whole("su0"), whole("uo")], [whole("su")]),
@@ -381,20 +355,15 @@ def rank_program(g, core, T, topo):
     for w in (16, 32, 64, 128):
         head["kk%d" % w] = lambda w=w: act(T.kk[:, w:2 * w], T.kk[:, 0:w], ACT.Copy, [("kk", 0, w)], [("kk", w, 2 * w)])
     for k in range(8):
-        head["u%d" % k] = lambda k=k: follow(0, k, "f1")
-        head["y%d" % k] = lambda k=k: follow(512, k, "f2")
+        head["u%d" % k] = lambda k=k: phase1(k, "v0", "va")
+        head["y%d" % k] = lambda k=k: phase2(k, "va", "vb")
         head["a%d" % k] = lambda k=k: phase1(k)
         head["b%d" % k] = lambda k=k: phase2(k)
-    for k in range(5):
-        head["m1%d" % k] = lambda k=k: own_or(k, "o1", "f1")
-        head["m2%d" % k] = lambda k=k: own_or(k, "o2", "f2")
     for k in range(4):
         head["qe%d" % k] = lambda k=k: quant("qe", "se", 128 * k, 128 * k + 128, "em", 3 - k)
         head["F%d" % k] = lambda k=k: unpack(0, k, False)
-        for eng in "av":
-            head["W%d%s" % (k, eng)] = lambda k=k, eng=eng: window(0, k, False, eng)
+        head["W%da" % k] = lambda k=k: window(0, k, False, "a")
     for w in ORDER["HEAD"].split():
-        step[0] = ("HEAD", w)
         head[w]()
 
     for t in range(ROUNDS):
@@ -403,7 +372,6 @@ def rank_program(g, core, T, topo):
         final = [w[1] for w in ORDER[part].split() if w[0] == "t"][-1]
         qn, sn, tn = "q%d" % (t + 1), "s%d" % (t + 1), "tt%d" % (t + 1)
         for w in ORDER[part].split():
-            step[0] = (part if t != 1 else None, w)
             kind = w[0]
             if kind == "x":
                 if not last:
@@ -470,7 +438,7 @@ def rank_program(g, core, T, topo):
                 if not last:
                     first(a, b)
                 else:
-                    eng, q = ("A", A) if ch == final else ("S", S)
-                    op(eng, lambda a=a, b=b, q=q: q.dma_start(T.y[:, a:b], T.yb[:, a:b]), [("yb", a, b)], [], "dOut")
+                    eng, q, grp = ("A", A, "dOut") if ch == final else ("G", g, "dOl") if ch == "A" else ("S", S, "dOut")
+                    op(eng, lambda a=a, b=b, q=q: q.dma_start(T.y[:, a:b], T.yb[:, a:b]), [("yb", a, b)], [], grp)
 
     _emit(g, T, ops, ["sent", "dOl", "dOut"])

@@ -1,10 +1,10 @@
 from concourse.mybir import dt, AluOpType, ActivationFunctionType
 
 C, H, ROUNDS = 448, 128, 3
-LO = C - H
-MID = 192
+MID = 256
 PAD = 8
 BIG = 1024.0
+TINY = 2.0 ** -99
 BANK = 512
 JW = H + 520
 X4, U8, F32, BF, I32, U16 = "float8_e4m3fn_x4", "uint8", "float32", "bfloat16", "int32", "uint16"
@@ -17,9 +17,10 @@ for _ty, _bufs in (
         (X4, {"qu0": 128, "qu": 128, "qv": 128, "qw": 512, "qe": 512, "qz": C, "q0": C + H, "q1": C + H, "q2": C + H, "q3": C + H}),
         (U8, {"su0": 128, "su": 128, "sv": 128, "sw": 512, "se": 512, "sz": C, "s0": C + H, "s1": C + H, "s2": C + H, "s3": C + H}),
         (U16, {"o1": 32, "o2": 32, "o3": 32, "off": 32, "lo": 32, "uo": 8}),
-        (F32, {"sg": C, "r0": 512, "ra": PAD + 512, "rb": PAD + 512, "rc": H + C, "rs": C, "v0": 512, "va": PAD + 512,
-               "vb": PAD + 512, "vs": 512, "t1": 32, "pf": 2, "p4": 1, "jn": JW, "jq": C, "c16": 32,
-               "kk": 256, "k0": 16, "k1": 16, "col": 8, "c1": 32, "olb": C, "yb": C})):
+        (F32, {"r0": 512, "raX": PAD + MID, "raY": PAD + MID, "rbX": PAD + MID, "rbY": PAD + MID, "rc": H + C, "rs": C,
+               "v0": 512, "vaX": PAD + MID, "vaY": PAD + MID, "vbX": PAD + MID, "vbY": PAD + MID,
+               "vs1": 512, "vs2": 512, "vs3": 512, "t1": 32, "pf": 2, "p4": 1, "jn": JW, "jq": C, "c16": 32,
+               "kk": 64, "km": 256, "k2": 16, "k0": 16, "k1": 16, "col": 16, "c1": 32, "olb": C, "ea": 520, "yb": C})):
     for _name, _n in _bufs.items():
         SCRATCH[_name] = ("sbuf", [128, _n], _ty)
 
@@ -28,19 +29,9 @@ SEMAPHORES = ["sV", "sA", "sP", "sG", "sent", "arr0", "arr1", "arr2",
 
 ALU, ACT = AluOpType, ActivationFunctionType
 
-CHUNK = {"A": (0, MID, 0, 5), "L": (LO, C, 4, 4), "B": (MID, LO, 0, 6)}
+HALF = {"X": (0, MID, 0), "Y": (MID, C, 4)}
 
-ORDER = {
-    "HEAD": ("zf z3 i0 i1 i2 pm z2 pf cb c28 z0 i3 c1 c8 k1 k0 i4 lo cr i6 em uo kk c1w v0 c3 rcn kk16 kk32 qu qL x S1 pk qF "
-             "t1 qe2 u0 ps o1 jq qe1 u1 z1 u2 P sg qe0 u3 r0 u4 a0 c2 qe3 a1 u5 F3 a2 F1 F2 u6 a3 W2a u7 F0 a4 W1a S2 kk64 "
-             "a5 y0 o2 a6 qv a7 y1 b0 y2 b1 y3 b2 y4 kk128 b3 y5 b4 y6 b5 y7 b6 W0a S3 b7 W3a o3 cA"),
-    "TAIL": ("h0 G0 h1 G2 h2 h3 H2a nA h4 H0v G1 H1v G3 gA0a h5 gA1a gA2a H3v h6 nB gA3a nL gB3v gL3v gL0a cL gL2a gB1a gB0a "
-             "zA gL1v gB2v zL wA eA0v eA1a eA2v eA3a wL eL1a zB eL0v cB wB eL2v eL3v tL pL eB0a tA pA eB1a x eB3a sL eB2v "
-             "tB pB sA rA rL sB rB F0 F1 F2 F3 W0a W1a W2a W3a CA a0 a1 a2 a3 a4 a5 a6 a7 b0 b1 b2 b3 b4 b5 b6 b7"),
-    "LAST": ("G3 H3a G2 h0 H2a G0 G1 h1 h2 h3 nA h4 h5 H0v H1v h6 gA3a gA1a gA2v gA0a nL nB zA gL1v wA gL0a gL2v cL gB1v gL3a "
-             "x zL gB2a wL eA1v eA0v eA2v gB3a eL1v eA3a tA gB0a zB cB pA eL0v eL3a eL2v sA wB tL pL eB1a eB3a eB0v eB2v "
-             "sL tB rA pB sB rB rL"),
-}
+ORDER = "zf z3 z2 i0 i3 i1 z1 pm cb pf i2 c28 c1 k1 k0 z0 lo i4 uo kk kk16 c1w v0 qu kk32 S16 S11 S10 S13 S15 ea S14 S17 S12 uX0.a ps qX t1 qY o1 em pk p0Y uX1 cs c8 uY0.a uY1 qe3 c2 uX2 uY2 uX3 p0X c3 uY3 qe2 uX4 uY4 qe1 uX5 uY5 jq r0X a0X0.a uX6 uY6 qe0 uX7 r0Y k2 S2X1 a0Y0.a S2X6 S2X4 S2X7 uY7 S2X0 S2X3 ci S2X5 a0X1 S2X2 S2Y3 F0Y2 F0X3 F0X0 F0Y3 S2Y0 o2X S2Y2 S2Y4 yX0.a yX1 a0X2 S2Y6 yX2 a0X3 S2Y7 yX3 i6 S2Y1 rcn S2Y5 yX4 F0X2 km km16 W0X0.a c2y a0X4 yY0.a o2Y yX5 a0X5 F0Y0 yY1 yX6 a0X6 x0 yY2 a0X7 b0X0.a yX7 a0Y1 yY3 S33 b0X1 S32 W0Y2.a a0Y2 b0X2 F0Y1 S30 b0X3 S31 b0X4 o3X a0Y3 F0X1 W0X1.a b0X5 a0Y4 b0X6 yY4 W0X2.a G0X2 W0X3.a a0Y5 b0X7 c0Y2 G0X0 G0X1 km32 yY5 h0X0 km64 km128 H0X2.a W0Y1.a W0Y3.a a0Y6 h0X1 c0Y3 a0Y7 h0X2 yY6 h0X3 b0Y0.a b0Y1 n0X b0Y2 cr m0X H0X0.a G0X3 b0Y3 W0Y0.a g0X0.v yY7 b0Y4 H0X3.a c0X0 S36 b0Y5 H0X1.a c0X1 S34 S35 g0X1.a c0X2 g0X3.a b0Y6 o3Y b0Y7 g0X2.a z0X c0X3 c0Y1 w0X0 e0X0.a w0X2 w0X1 e0X1.a h0Y4 h0Y5 h0Y6 n0Y w0X3 e0X3.a e0X2.v c0Y0 m0Y g0Y0.a t0X g0Y2.a p1X g0Y3.v r1X g0Y1.a F1X0 qv a1X0.a z0Y w0Y3 a1X1 e0Y3.a a1X2 a1X3 w0Y0 e0Y0.v w0Y2 a1X4 e0Y2.a a1X5 w0Y1 e0Y1.a t0Y x1 F1X1 F1X2 W1X2.a F1X3 p1Y a1X6 a1X7 b1X0.a F1Y0 r1Y a1Y0.v W1Y0.a b1X1 a1Y1 b1X2 F1Y2 F1Y1 W1Y2.a a1Y2 b1X3 a1Y3 b1X4 a1Y4 W1X3.a F1Y3 W1Y3.a W1Y1.a c1Y2 b1X5 G1X2 a1Y5 b1X6 a1Y6 a1Y7 W1X1.a G1X1 b1X7 W1X0.a b1Y0.v h1X0 c1Y3 b1Y1 b1Y2 h1X1 b1Y3 b1Y4 h1X2 b1Y5 h1X3 b1Y6 b1Y7 n1X G1X3 G1X0 H1X1.a c1X1 h1Y4 H1X3.a c1X3 m1X h1Y5 H1X2.a h1Y6 g1X3.a H1X0.v c1Y1 g1X2.a n1Y m1Y g1X0.v c1X0 c1X2 g1Y2.v g1X1.a z1X g1Y3.v w1X0 g1Y0.a g1Y1.a e1X0.a w1X1 w1X2 e1X2.a z1Y w1X3 w1Y2 e1Y2.a w1Y3 e1Y3.a e1X1.v c1Y0 w1Y0 e1Y0.a e1X3.v t1X w1Y1 e1Y1.v t1Y x2 p2X F2X2 W2X2.a F2X1 r2X a2X0.a p2Y r2Y a2X1 a2X2 a2Y0.a a2Y1 a2X3 a2Y2 a2X4 a2Y3 a2X5 F2Y1 a2Y4 a2X6 a2Y5 F2Y3 a2X7 a2Y6 F2X3 b2X0.v F2X0 W2X0.a F2Y2 a2Y7 W2X1.a b2X1 F2Y0 G2X0 b2X2 b2Y0.a b2Y1 b2X3 b2Y2 W2Y1.a b2X4 b2Y3 b2X5 W2X3.a W2Y3.a c2Y3 b2Y4 b2X6 b2Y5 b2X7 G2X2 h2X0 G2X1 b2Y6 h2X1 b2Y7 W2Y2.a G2X3 c2Y1 W2Y0.a H2X3.a h2X2 h2X3 h2Y4 n2X c2X3 h2Y5 H2X1.a H2X2.a m2X h2Y6 c2Y2 g2X2.a H2X0.v g2X0.a c2Y0 c2X1 g2X3.a n2Y c2X0 m2Y g2Y2.a g2X1.v g2Y3.v z2X c2X2 w2X2 g2Y1.a w2X0 w2X1 e2X2.a g2Y0.v z2Y e2X0.v w2X3 e2X3.a w2Y1 e2X1.v w2Y2 e2Y2.a e2Y1.v w2Y3 e2Y3.v w2Y0 e2Y0.a ol.a t2X OX p3X t2Y od s3X.v p3Y s3Y.a YX OY os YY"
 
 
 def _clash(a, b):
@@ -151,6 +142,12 @@ def rank_program(g, core, T, topo):
         else:
             op("A", lambda: A.activation(out, in_, func, bias=bias, scale=scale), R, W)
 
+    def move(out, in_, R, W, eng):
+        if eng == "v":
+            cp(out, in_, R, W)
+        else:
+            act(out, in_, ACT.Copy, R, W)
+
     def fill(name, a, b, val):
         op("V", lambda: V.memset(T[name][:, a:b], val), [], [(name, a, b)])
 
@@ -178,29 +175,28 @@ def rank_program(g, core, T, topo):
     def whole(name):
         return (name, 0, SCRATCH[name][1][1])
 
-    CB, C1, C8, C2, C3, CR, C28 = 0, 1, 2, 3, 4, 5, 6
+    CB, C1, C8, C2, C3, CR, C28, C2Y, CS, CI = range(10)
 
     def scan(out, a, b, src, lo, hi, stride):
         op("V", lambda: V.tensor_tensor_scan(T[out][:, a:b], T.kk[:, 0:b - a], T[src][:, lo:hi:stride], 0.0, ALU.add, ALU.max),
            [("kk", 0, b - a), (src, lo, hi)], [(out, a, b)])
 
-    def scans(src, base, n):
-        for k in range(n):
-            scan("vs", 64 * k, 64 * k + 64, src, base + k, base + 512, 8)
-
-    def phase_op(src, lo, hi, dst, base, k, offs, copy):
-        a = base + 64 * k
-        if copy:
-            cp(T[dst][:, a:a + 64], T[src][:, lo + k:hi:8], [(src, lo, hi)], [(dst, a, a + 64)])
+    def phase_op(src, lo, hi, step, dst, a, n, offs, oc, eng):
+        if eng:
+            move(T[dst][:, a:a + n], T[src][:, lo:hi:step], [(src, lo, hi)], [(dst, a, a + n)], eng)
         else:
-            tt(T[dst][:, a:a + 64], T[dst][:, 0:a].indirect(T[offs][:, 4 * k:4 * k + 4]), T[src][:, lo + k:hi:8], ALU.max,
-               [(src, lo, hi), (dst, 0, a), (offs, 4 * k, 4 * k + 4)], [(dst, a, a + 64)])
+            tt(T[dst][:, a:a + n], T[dst][:, 0:a].indirect(T[offs][:, oc:oc + n // 16]), T[src][:, lo:hi:step], ALU.max,
+               [(src, lo, hi), (dst, 0, a), (offs, oc, oc + n // 16)], [(dst, a, a + n)])
 
-    def phase1(k, src="r0", dst="ra"):
-        phase_op(src, 0, 512, dst, PAD, k, "o1", k == 0)
+    def phase1(h, k, eng, src, dst):
+        a = HALF[h][0]
+        phase_op(src, a + k, a + MID, 8, dst + h, PAD + 32 * k, 32, "o1", 4 * k + a // 128, eng)
 
-    def phase2(k, src="ra", dst="rb"):
-        phase_op(src, PAD, PAD + 512, dst, PAD, k, "o2", k == 0)
+    def phase2(h, k, eng, src, dst):
+        phase_op(src + h, PAD + k, PAD + MID, 8, dst + h, PAD + 32 * k, 32, "o2", 2 * k + HALF[h][0] // 16, eng)
+
+    def phase3(h, k):
+        phase_op("rb" + h, PAD + k % 4, PAD + MID, 4, "rc", H + 64 * k, 64, "o3", 4 * k, None)
 
     def send(t):
         if rank + 1 >= n_ranks:
@@ -210,30 +206,15 @@ def rank_program(g, core, T, topo):
         mask = topo.mask(core, dst)
         n_eng = len(topo.engines(core, dst))
         q, s = "q%d" % t, "s%d" % t
-        op("G", lambda: g.remote_dma(T[q][:, C:C + H].bitcast(dt.uint8), T[q][:, LO:C].bitcast(dt.uint8),
-                                     T.sem["arr%d" % t], T.sem.sent, pid, rid, mask), [(q, LO, C)], [], "sent", n_eng, False)
-        op("G", lambda: g.remote_dma(T[s][:, C:C + H], T[s][:, LO:C],
-                                     T.sem["arr%d" % t], T.sem.sent, pid, rid, mask), [(s, LO, C)], [], "sent", n_eng, False)
+        op("G", lambda: g.remote_dma(T[q][:, 0:H].bitcast(dt.uint8), T[q][:, C:C + H].bitcast(dt.uint8),
+                                     T.sem["arr%d" % t], T.sem.sent, pid, rid, mask), [(q, C, C + H)], [], "sent", n_eng, False)
+        op("G", lambda: g.remote_dma(T[s][:, 0:H], T[s][:, C:C + H],
+                                     T.sem["arr%d" % t], T.sem.sent, pid, rid, mask), [(s, C, C + H)], [], "sent", n_eng, False)
 
     def arrive(t):
         if rank > 0:
             n_eng = len(topo.engines(T.cores[rank - 1], core))
-            op(None, None, [], [("q%d" % t, C, C + H), ("s%d" % t, C, C + H)], "arr%d" % t, 2 * n_eng, False)
-
-    def heads(t, a, b, k):
-        mm(k, "qu", "su", 0, "q%d" % t, "s%d" % t, a, b, True, True)
-
-    def signs(a, b, k):
-        act(T.sg[:, a:b], pv(k, 0, b - a), ACT.Sign, [bank(k)], [("sg", a, b)])
-
-    def first(a, b):
-        op("V", lambda: V.tensor_tensor_scan(T.r0[:, a:b], T.jq[:, a:b], T.sg[:, a:b], -2.0, ALU.max, ALU.min),
-           [("jq", a, b), ("sg", a, b)], [("r0", a, b)])
-
-    def sums(t, ch):
-        a, b, k0, kp = CHUNK[ch]
-        for k in range(4):
-            mm(k0 + k, "qe", "se", 128 * k, "q%d" % t, "s%d" % t, a, b, True, False)
+            op(None, None, [], [("q%d" % t, 0, H), ("s%d" % t, 0, H)], "arr%d" % t, 2 * n_eng, False)
 
     def scaled(out, k, n, W, eng):
         if eng == "v":
@@ -241,204 +222,159 @@ def rank_program(g, core, T, topo):
         else:
             act(out, pv(k, 0, n), ACT.Copy, [bank(k)], W, scale=1.0 / 64)
 
-    def unpack(t, k, far):
-        if not far:
-            mm(k, "qe", "se", 128 * k, "q%d" % t, "s%d" % t, 0, C, True, True)
-        elif rank > 0:
-            mm(4 + k, "qe", "se", 128 * k, "q%d" % t, "s%d" % t, C, C + H, True, True)
-
-    def window(t, k, far, eng):
-        fw, w = "fw%d" % t, (H + C) * k
-        if not far:
-            scaled(T[fw][:, w + H:w + H + C], k, C, [(fw, w + H, w + H + C)], eng)
-        elif rank > 0:
-            scaled(T[fw][:, w:w + H], 4 + k, H, [(fw, w, w + H)], eng)
-
-    def lists(ch):
-        a, b, k0, kp = CHUNK[ch]
-        scan("rs", a, b, "rc", H + a, H + b, 1)
-        ts(T.off[:, a // 16:b // 16], T.rs[:, a + 15:b:16], col(CR), BIG, ALU.subtract, ALU.mult,
-           [("rs", a, b), creg(CR)], [("off", a // 16, b // 16)])
-
-    def gather(t, ch, k, eng):
-        a, b, k0, kp = CHUNK[ch]
-        fw = "fw%d" % t
-        w = (H + C) * k
-        R = [(fw, w, w + H + b), ("off", a // 16, b // 16)]
-        W = [("zt", 4 * a, 4 * b, k)]
-        src = T[fw][:, w:w + H + b].indirect(T.off[:, a // 16:b // 16])
-        if eng == "v":
-            cp(T.zt[:, 4 * a + k:4 * b:4], src, R, W)
-        else:
-            act(T.zt[:, 4 * a + k:4 * b:4], src, ACT.Copy, R, W)
-
-    def layer(ch):
-        a, b, k0, kp = CHUNK[ch]
-        for k in range(4):
-            mm(k0 + k, "qw", "sw", 128 * k, "qz", "sz", a, b, False, True)
-
-    def state(t, ch, k, eng):
-        a, b, k0, kp = CHUNK[ch]
-        tn = "tt%d" % (t + 1)
-        scaled(T[tn][:, 4 * a + k:4 * b:4], k0 + k, b - a, [(tn, 4 * a, 4 * b, k)], eng)
-
     def zero_halo():
         if rank == 0:
             for t in range(ROUNDS):
                 for k in range(4):
                     fill("fw%d" % t, (H + C) * k, (H + C) * k + H, 0.0)
 
+    def round_step(kind, t, h, k, eng):
+        a, b, k0 = HALF[h]
+        q, s, fw, tn = "q%d" % t, "s%d" % t, "fw%d" % t, "tt%d" % (t + 1)
+        w = (H + C) * k
+        if kind == "p":
+            wq, ws = ("qu", "su") if t < ROUNDS else ("qv", "sv")
+            mm(k0 + 3, wq, ws, 0, q, s, H + a, H + b, True, True)
+        elif kind == "r":
+            tt(T.r0[:, a:b], pv(k0 + 3, 0, b - a), T.jq[:, a:b], ALU.min, [bank(k0 + 3), ("jq", a, b)], [("r0", a, b)])
+        elif kind == "s":
+            move(T.yb[:, a:b], pv(k0 + 3, 0, b - a), [bank(k0 + 3)], [("yb", a, b)], eng)
+        elif kind == "a":
+            phase1(h, k, eng, "r0", "ra")
+        elif kind == "b":
+            phase2(h, k, eng, "ra", "rb")
+        elif kind == "h":
+            phase3(h, k)
+        elif kind == "n":
+            op("V", lambda: V.tensor_tensor_scan(T.rs[:, a:b], T.km[:, 0:b - a], T.rc[:, H + a:H + b], col(CI), ALU.mult, ALU.max),
+               [("km", 0, b - a), ("rc", H + a, H + b), creg(CI)], [("rs", a, b)])
+        elif kind == "m":
+            ts(T.off[:, a // 16:b // 16], T.rs[:, a + 15:b:16], col(CR), BIG + H, ALU.mult, ALU.add,
+               [("rs", a, b), creg(CR)], [("off", a // 16, b // 16)])
+        elif kind == "F":
+            mm(k0 + k, "qe", "se", 128 * k, q, s, H + a, H + b, True, True)
+        elif kind == "W":
+            scaled(T[fw][:, w + H + a:w + H + b], k0 + k, b - a, [(fw, w + H + a, w + H + b)], eng)
+        elif kind == "G":
+            if rank > 0:
+                mm(k0 + k, "qe", "se", 128 * k, q, s, 0, H, True, True)
+        elif kind == "H":
+            if rank > 0:
+                scaled(T[fw][:, w:w + H], k0 + k, H, [(fw, w, w + H)], eng)
+        elif kind == "c":
+            mm(k0 + k, "qe", "se", 128 * k, q, s, H + a, H + b, True, False)
+        elif kind == "g":
+            move(T.zt[:, 4 * a + k:4 * b:4], T[fw][:, w:w + H + b].indirect(T.off[:, a // 16:b // 16]),
+                 [(fw, w, w + H + b), ("off", a // 16, b // 16)], [("zt", 4 * a, 4 * b, k)], eng)
+        elif kind == "z":
+            quant("qz", "sz", a, b, "zt", 4 * a)
+        elif kind == "w":
+            mm(k0 + k, "qw", "sw", 128 * k, "qz", "sz", a, b, False, True)
+        elif kind == "e":
+            scaled(T[tn][:, 4 * a + k:4 * b:4], k0 + k, b - a, [(tn, 4 * a, 4 * b, k)], eng)
+        elif kind == "t":
+            quant("q%d" % (t + 1), "s%d" % (t + 1), H + a, H + b, tn, 4 * a)
+
+    def store(eng, out, in_, R):
+        q = {"S": S, "A": A, "G": g}[eng]
+        op(eng, lambda: q.dma_start(out, in_), R, [], "dOl" if eng == "G" else "dOut")
+
     for t in range(ROUNDS):
         arrive(t)
     for i in range(16):
         eng, q = ("S", S) if i % 2 == 0 else ("A", A)
         op(eng, lambda i=i, q=q: q.dma_start(T.drep[i::16, :], T.dist[:]), [], [("drep", 0, C)], "dD")
-    op("A", lambda: A.dma_start(T.xt[:, 4 * LO:4 * C], T.x[:, 4 * LO:4 * C]), [], [("xt", 4 * LO, 4 * C)], "dXL")
+    op("A", lambda: A.dma_start(T.xt[:, 4 * MID:4 * C], T.x[:, 4 * MID:4 * C]), [], [("xt", 4 * MID, 4 * C)], "dXL")
     op("A", lambda: A.dma_start(T.ut[:], T.u[:]), [], [("ut", 0, 512)], "dU")
-    op("S", lambda: S.dma_start(T.xt[:, 0:4 * LO], T.x[:, 0:4 * LO]), [], [("xt", 0, 4 * LO)], "dXF")
+    op("S", lambda: S.dma_start(T.xt[:, 0:4 * MID], T.x[:, 0:4 * MID]), [], [("xt", 0, 4 * MID)], "dXF")
     op("S", lambda: S.dma_start(T.qw[:].bitcast(dt.uint8), T.wc[:]), [], [("qw", 0, 512)], "dW")
     op("S", lambda: S.dma_start(T.sw[:], T.ws[:]), [], [("sw", 0, 512)], "dW")
     op("S", lambda: S.dma_start(T.vt[:], T.v[:]), [], [("vt", 0, 512)], "dV")
 
     i_col, ireg = T.pf[:, 0:1], ("pf", 0, 1)
-    head = {
+    qn, sn = "q%d" % ROUNDS, "s%d" % ROUNDS
+    once = {
         "i0": lambda: iota("pi", 0, 1, [[0, 1]], 0, 1, False),
-        "i1": lambda: iota("pi", 1, 2, [[0, 1]], 0, 2, False),
+        "i1": lambda: iota("pi", 1, 2, [[0, 1]], 0, 4, False),
         "i2": lambda: iota("jn", H - 8, JW, [[1, JW - H + 8]], -8, 0),
-        "i3": lambda: iota("p4", 0, 1, [[0, 1]], 3, 4),
-        "i4": lambda: iota("c16", 0, 32, [[0, 8], [16, 4]], 0, 0),
+        "i3": lambda: iota("p4", 0, 1, [[0, 1]], -3, -4),
+        "i4": lambda: iota("c16", 0, 32, [[0, 8], [32 * MID, 2], [255 * 16, 2]], 0, 0),
         "i6": lambda: iota("jn", 0, H - 8, [[1, H - 8]], -H, 0),
         "z0": lambda: fill("v0", C, 512, float(H)),
         "z1": lambda: fill("r0", C, 512, -1.0),
-        "z2": lambda: [fill(n, 0, PAD, -2 * BIG) for n in ("ra", "va")],
-        "z3": lambda: [fill(n, 0, PAD, -2 * BIG) for n in ("rb", "vb")],
+        "z2": lambda: [fill(n, 0, PAD, -2 * BIG) for n in ("vaX", "vaY", "raX", "raY")],
+        "z3": lambda: [fill(n, 0, PAD, -2 * BIG) for n in ("vbX", "vbY", "rbX", "rbY")],
         "zf": zero_halo,
         "pm": lambda: ts(T.pm[:], T.pi[:], 15, None, ALU.bitwise_and, None, [whole("pi")], [whole("pm")]),
         "c28": lambda: ts(col(C28), T.pm[:, 0:1], 28.0, None, ALU.mult, None, [("pm", 0, 1)], [creg(C28)]),
         "pf": lambda: cp(T.pf[:], T.pm[:], [whole("pm")], [whole("pf")]),
         "cb": lambda: ts(col(CB), T.pm[:, 0:1], 15.0, BIG, ALU.is_lt, ALU.mult, [("pm", 0, 1)], [creg(CB)]),
-        "c1": lambda: ts(col(C1), i_col, -511.0 / 64, col(CB), ALU.mult, ALU.add, [ireg, creg(CB)], [creg(C1)]),
+        "c1": lambda: ts(col(C1), i_col, -255.0 / 32, col(CB), ALU.mult, ALU.add, [ireg, creg(CB)], [creg(C1)]),
         "k0": lambda: ts(T.k0[:], T.jn[:, H:H + 16], i_col, -2 * BIG, ALU.is_equal, ALU.mult, [("jn", H, H + 16), ireg], [whole("k0")]),
         "k1": lambda: ts(T.k1[:], T.jn[:, H - 1:H + 15], i_col, BIG, ALU.is_equal, ALU.mult, [("jn", H - 1, H + 15), ireg], [whole("k1")]),
         "lo": lambda: ts(T.lo[:, 0:28], T.jn[:, H:H + 28], col(C28), None, ALU.add, None, [("jn", H, H + 28), creg(C28)], [("lo", 0, 28)]),
         "kk": lambda: tt(T.kk[:, 0:16], T.k0[:], T.k1[:], ALU.add, [whole("k0"), whole("k1")], [("kk", 0, 16)]),
         "uo": lambda: cp(T.uo[:], T.jn[:, H:H + 128:16], [("jn", H, H + 128)], [whole("uo")]),
-        "em": lambda: ts(T.em[:], T.jn[:, H:H + 520], T.p4[:], 64.0, ALU.is_equal, ALU.mult, [("jn", H, JW), whole("p4")], [whole("em")]),
-        "c1w": lambda: ts(T.c1[:], T.c16[:], -511.0 / 64, col(C1), ALU.mult, ALU.add, [whole("c16"), creg(C1)], [whole("c1")]),
-        "c8": lambda: act(col(C8), col(CB), ACT.Identity, [creg(CB)], [creg(C8)], 8.0, 8.0),
+        "ea": lambda: act(T.ea[:], T.jn[:, H:JW], ACT.Abs, [("jn", H, JW), whole("p4")], [whole("ea")], 1.0, T.p4[:]),
+        "em": lambda: act(T.em[:], T.ea[:], ACT.Relu, [whole("ea")], [whole("em")], -64.0, 64.0),
+        "c1w": lambda: ts(T.c1[:], T.c16[:], -1.0 / 32, col(C1), ALU.mult, ALU.add, [whole("c16"), creg(C1)], [whole("c1")]),
+        "c8": lambda: act(col(C8), col(CB), ACT.Identity, [creg(CB)], [creg(C8)], 4.0, float(PAD)),
         "c3": lambda: act(col(C3), col(CB), ACT.Identity, [creg(CB)], [creg(C3)], 1.0, float(H)),
-        "cr": lambda: act(col(CR), col(CB), ACT.Identity, [creg(CB)], [creg(CR)], 1.0, -0.625),
-        "c2": lambda: act(col(C2), T.pf[:, 1:2], ACT.Identity, [("pf", 1, 2), creg(C8)], [creg(C2)], -255.5, col(C8)),
-        "jq": lambda: act(T.jq[:], T.jn[:, H:H + C], ACT.Identity, [("jn", H, H + C)], [whole("jq")], 1.0 / BIG, -0.5),
-        "rcn": lambda: act(T.rc[:, 0:H], T.jn[:, 0:H], ACT.Identity, [("jn", 0, H)], [("rc", 0, H)], 1.0 / BIG, -0.5),
+        "cr": lambda: act(col(CR), col(CB), ACT.Identity, [creg(CB)], [creg(CR)], -2.0 / BIG / TINY, 1.0 / TINY),
+        "cs": lambda: act(col(CS), col(CB), ACT.Identity, [creg(CB)], [creg(CS)], -4.0 / BIG ** 3, 2.0 / BIG ** 2),
+        "ci": lambda: act(col(CI), col(CB), ACT.Identity, [creg(CB)], [creg(CI)], 2.0 / BIG, -1.0),
+        "c2": lambda: act(col(C2), T.pf[:, 1:2], ACT.Identity, [("pf", 1, 2), creg(C8)], [creg(C2)], -255.0 / 4, col(C8)),
+        "c2y": lambda: act(col(C2Y), col(C2), ACT.Identity, [creg(C2)], [creg(C2Y)], 1.0, -4.0 * MID),
+        "k2": lambda: act(T.k2[:], T.kk[:, 0:16], ACT.Square, [("kk", 0, 16)], [whole("k2")]),
+        "km": lambda: act(T.km[:, 0:16], T.k2[:], ACT.Identity, [whole("k2"), creg(CS)], [("km", 0, 16)], col(CS), 1.0),
+        "jq": lambda: act(T.jq[:], T.jn[:, H:H + C], ACT.Identity, [("jn", H, H + C)], [whole("jq")], TINY, -BIG * TINY),
+        "rcn": lambda: act(T.rc[:, 0:H], T.jn[:, 0:H], ACT.Identity, [("jn", 0, H)], [("rc", 0, H)], TINY, -BIG * TINY),
         "v0": lambda: tt(T.v0[:, 0:C], T.drep[:].indirect(T.lo[:, 0:28]), T.jn[:, H:H + C], ALU.subtract,
                          [whole("drep"), ("lo", 0, 28), ("jn", H, H + C)], [("v0", 0, C)]),
-        "qL": lambda: quant("q0", "s0", LO, C, "xt", 4 * LO),
-        "qF": lambda: quant("q0", "s0", 0, LO, "xt", 0),
+        "qY": lambda: quant("q0", "s0", H + MID, H + C, "xt", 4 * MID),
+        "qX": lambda: quant("q0", "s0", H, H + MID, "xt", 0),
         "qu": lambda: quant("qu0", "su0", 0, 128, "ut", 0),
         "qv": lambda: quant("qv", "sv", 0, 128, "vt", 0),
-        "x": lambda: send(0),
-        "S1": lambda: scans("v0", 0, 8),
-        "S2": lambda: scans("va", PAD, 8),
-        "S3": lambda: scans("vb", PAD, 7),
-        "t1": lambda: tt(T.t1[:], T.vs[:, 15:512:16], T.c1[:], ALU.subtract, [whole("vs"), whole("c1")], [whole("t1")]),
+        "t1": lambda: tt(T.t1[:], T.vs1[:, 15:512:16], T.c1[:], ALU.subtract, [whole("vs1"), whole("c1")], [whole("t1")]),
         "pk": lambda: cp(T.qu[:].bitcast(dt.uint32), T.qu0[:].bitcast(dt.uint32).indirect(T.uo[:]), [whole("qu0"), whole("uo")], [whole("qu")]),
         "ps": lambda: op("A", lambda: A.activation(T.su[:], T.su0[:].indirect(T.uo[:]), ACT.Copy), [whole("su0"), whole("uo")], [whole("su")]),
-        "o1": lambda: ts(T.o1[:], T.t1[:], -64.0, float(PAD), ALU.mult, ALU.add, [whole("t1")], [whole("o1")]),
-        "o2": lambda: ts(T.o2[:], T.vs[:, 15:512:16], -8.0, col(C2), ALU.mult, ALU.add, [whole("vs"), creg(C2)], [whole("o2")]),
-        "o3": lambda: ts(T.o3[:, 0:28], T.vs[:, 15:C:16], -1.0, col(C3), ALU.mult, ALU.add, [whole("vs"), creg(C3)], [("o3", 0, 28)]),
-        "P": lambda: heads(0, 0, C, 4),
-        "sg": lambda: signs(0, C, 4),
-        "r0": lambda: first(0, C),
-        "cA": lambda: sums(0, "A"),
+        "o1": lambda: ts(T.o1[:], T.t1[:], -32.0, float(PAD), ALU.mult, ALU.add, [whole("t1")], [whole("o1")]),
+        "ol": lambda: act(T.olb[:], T.rc[:, H:H + C], ACT.Identity, [("rc", H, H + C)], [whole("olb")], 1.0 / TINY, BIG),
+        "od": lambda: store("G", T.ol[:], T.olb[0::16, :], [whole("olb")]),
+        "os": lambda: [store("SA"[k % 2], T.osc[4 * k:4 * k + 4, :], T[sn][32 * k:32 * k + 4, H:H + C], [(sn, H, H + C)]) for k in range(4)],
     }
-    for w in (16, 32, 64, 128):
-        head["kk%d" % w] = lambda w=w: act(T.kk[:, w:2 * w], T.kk[:, 0:w], ACT.Copy, [("kk", 0, w)], [("kk", w, 2 * w)])
+    for name, top in (("kk", 64), ("km", 256)):
+        for w in (16, 32, 64, 128):
+            if w < top:
+                once["%s%d" % (name, w)] = lambda w=w, name=name: act(T[name][:, w:2 * w], T[name][:, 0:w], ACT.Copy, [(name, 0, w)], [(name, w, 2 * w)])
     for k in range(8):
-        head["u%d" % k] = lambda k=k: phase1(k, "v0", "va")
-        head["y%d" % k] = lambda k=k: phase2(k, "va", "vb")
-        head["a%d" % k] = lambda k=k: phase1(k)
-        head["b%d" % k] = lambda k=k: phase2(k)
+        once["S1%d" % k] = lambda k=k: scan("vs1", 64 * k, 64 * k + 64, "v0", k, 512, 8)
+    for k in range(7):
+        once["S3%d" % k] = lambda k=k: scan("vs3", 64 * k, 64 * k + 64, "vb" + "XY"[k // 4], PAD + k % 4, PAD + MID, 4)
     for k in range(4):
-        head["qe%d" % k] = lambda k=k: quant("qe", "se", 128 * k, 128 * k + 128, "em", 3 - k)
-        head["F%d" % k] = lambda k=k: unpack(0, k, False)
-        head["W%da" % k] = lambda k=k: window(0, k, False, "a")
-    for w in ORDER["HEAD"].split():
-        head[w]()
-
+        once["qe%d" % k] = lambda k=k: quant("qe", "se", 128 * k, 128 * k + 128, "em", 3 - k)
     for t in range(ROUNDS):
-        last = t == ROUNDS - 1
-        part = "LAST" if last else "TAIL"
-        final = [w[1] for w in ORDER[part].split() if w[0] == "t"][-1]
-        qn, sn, tn = "q%d" % (t + 1), "s%d" % (t + 1), "tt%d" % (t + 1)
-        for w in ORDER[part].split():
-            kind = w[0]
-            if kind == "x":
-                if not last:
-                    send(t + 1)
-                else:
-                    act(T.olb[:], T.rc[:, H:H + C], ACT.Identity, [("rc", H, H + C)], [whole("olb")], BIG, 512.0)
-                    op("G", lambda: g.dma_start(T.ol[:], T.olb[0::16, :]), [whole("olb")], [], "dOl")
-                continue
-            if kind in "FGWHabh":
-                k = int(w[1])
-                if kind == "F":
-                    unpack(t + 1, k, False)
-                elif kind == "W":
-                    window(t + 1, k, False, w[2])
-                elif kind == "G":
-                    unpack(t, k, True)
-                elif kind == "H":
-                    window(t, k, True, w[2])
-                elif kind == "a":
-                    phase1(k)
-                elif kind == "b":
-                    phase2(k)
-                else:
-                    phase_op("rb", PAD, PAD + 512, "rc", H, k, "o3", False)
-                continue
-            ch = w[1]
-            a, b, k0, kp = CHUNK[ch]
-            if kind == "n":
-                lists(ch)
-            elif kind == "g":
-                gather(t, ch, int(w[2]), w[3])
-            elif kind == "z":
-                quant("qz", "sz", a, b, "zt", 4 * a)
-            elif kind == "w":
-                layer(ch)
-            elif kind == "c":
-                sums(t, ch)
-            elif kind == "C":
-                sums(t + 1, ch)
-            elif kind == "e":
-                state(t, ch, int(w[2]), w[3])
-            elif kind == "t":
-                quant(qn, sn, a, b, tn, 4 * a)
-                if last:
-                    op("S", lambda a=a, b=b, qn=qn: S.dma_start(T.oc[:, 4 * a:4 * b], T[qn][:, a:b].bitcast(dt.uint8)), [(qn, a, b)], [], "dOut")
-                if last and ch == final:
-                    for k in range(4):
-                        eng, q = [("S", S), ("A", A)][k % 2]
-                        op(eng, lambda k=k, q=q, sn=sn: q.dma_start(T.osc[4 * k:4 * k + 4, :], T[sn][32 * k:32 * k + 4, 0:C]),
-                           [(sn, 0, C)], [], "dOut")
-            elif kind == "p":
-                if not last:
-                    heads(t + 1, a, b, kp)
-                else:
-                    mm(kp, "qv", "sv", 0, qn, sn, a, b, True, True)
-            elif kind == "s":
-                if not last:
-                    signs(a, b, kp)
-                elif ch == final:
-                    cp(T.yb[:, a:b], pv(kp, 0, b - a), [bank(kp)], [("yb", a, b)])
-                else:
-                    act(T.yb[:, a:b], pv(kp, 0, b - a), ACT.Copy, [bank(kp)], [("yb", a, b)])
-            elif kind == "r":
-                if not last:
-                    first(a, b)
-                else:
-                    eng, q, grp = ("A", A, "dOut") if ch == final else ("G", g, "dOl") if ch == "A" else ("S", S, "dOut")
-                    op(eng, lambda a=a, b=b, q=q: q.dma_start(T.y[:, a:b], T.yb[:, a:b]), [("yb", a, b)], [], grp)
+        once["x%d" % t] = lambda t=t: send(t)
+    for h, (a, b, k0) in HALF.items():
+        c2 = C2Y if a else C2
+        for k in range(8):
+            once["S2%s%d" % (h, k)] = lambda h=h, k=k, a=a: scan("vs2", a + 32 * k, a + 32 * k + 32, "va" + h, PAD + k, PAD + MID, 8)
+        once["o2" + h] = lambda a=a, c2=c2: ts(T.o2[:, a // 16:a // 16 + 16], T.vs2[:, a + 15:a + MID:16], -4.0, col(c2), ALU.mult, ALU.add,
+                                               [("vs2", a, a + MID), creg(c2)], [("o2", a // 16, a // 16 + 16)])
+        once["o3" + h] = lambda a=a, b=b: ts(T.o3[:, a // 16:b // 16], T.vs3[:, a + 15:b:16], -1.0, col(C3), ALU.mult, ALU.add,
+                                             [("vs3", a, b), creg(C3)], [("o3", a // 16, b // 16)])
+        once["O" + h] = lambda a=a, b=b: store("S", T.oc[:, 4 * a:4 * b], T[qn][:, H + a:H + b].bitcast(dt.uint8), [(qn, H + a, H + b)])
+        once["Y" + h] = lambda a=a, b=b: store("A" if a else "S", T.y[:, a:b], T.yb[:, a:b], [("yb", a, b)])
+
+    for word in ORDER.split():
+        name, eng = word.split(".") if "." in word else (word, None)
+        if name in once:
+            once[name]()
+        elif name[0] == "u":
+            phase1(name[1], int(name[2]), eng, "v0", "va")
+        elif name[0] == "y":
+            phase2(name[1], int(name[2]), eng, "va", "vb")
+        else:
+            round_step(name[0], int(name[1]), name[2], int(name[3:] or 0), eng)
 
     _emit(g, T, ops, ["sent", "dOl", "dOut"])

@@ -1,26 +1,24 @@
 from concourse.mybir import dt, AluOpType, ActivationFunctionType
 
 C, H, ROUNDS = 448, 128, 3
-MID = 256
-PAD = 8
+Q = 64
+SEG = 264
 BIG = 1024.0
-TINY = 2.0 ** -99
+TINY = 2.0 ** -98
 BANK = 512
-JW = H + 520
 X4, U8, F32, BF, I32, U16 = "float8_e4m3fn_x4", "uint8", "float32", "bfloat16", "int32", "uint16"
 
 SCRATCH = {"ps": ("psum", [128, 8 * BANK], F32)}
 for _ty, _bufs in (
-        (I32, {"drep": C, "pi": 2, "pm": 2}),
-        (BF, {"xt": 4 * C, "ut": 512, "vt": 512, "em": 520, "zt": 4 * C, "tt1": 4 * C,
+        (I32, {"drep": C + 8, "pi": 1, "pm": 2, "it": 64, "jm": 64}),
+        (BF, {"xt": 4 * C, "ut": 512, "vt": 512, "e64": 520, "em": 520, "zt": 4 * C, "tt1": 4 * C,
               "tt2": 4 * C, "tt3": 4 * C, "fw0": 4 * (H + C), "fw1": 4 * (H + C), "fw2": 4 * (H + C)}),
         (X4, {"qu0": 128, "qu": 128, "qv": 128, "qw": 512, "qe": 512, "qz": C, "q0": C + H, "q1": C + H, "q2": C + H, "q3": C + H}),
         (U8, {"su0": 128, "su": 128, "sv": 128, "sw": 512, "se": 512, "sz": C, "s0": C + H, "s1": C + H, "s2": C + H, "s3": C + H}),
-        (U16, {"o1": 32, "o2": 32, "o3": 32, "off": 32, "lo": 32, "uo": 8}),
-        (F32, {"r0": 512, "raX": PAD + MID, "raY": PAD + MID, "rbX": PAD + MID, "rbY": PAD + MID, "rc": H + C, "rs": C,
-               "v0": 512, "vaX": PAD + MID, "vaY": PAD + MID, "vbX": PAD + MID, "vbY": PAD + MID,
-               "vs1": 512, "vs2": 512, "vs3": 512, "t1": 32, "pf": 2, "p4": 1, "jn": JW, "jq": C, "c16": 32,
-               "kk": 64, "km": 256, "k2": 16, "k0": 16, "k1": 16, "col": 16, "c1": 32, "olb": C, "ea": 520, "yb": C})):
+        (U16, {"o1": 24, "o2": 24, "o3": 24, "o4": 28, "off": 28, "lo": 32, "uo": 8}),
+        (F32, {"lv": 12 * SEG, "rc": H + C, "rs": C, "vs1": 384, "vs2": 384, "vs3": 384, "vs4": C,
+               "jv": 256, "jq": 512, "lt": 32, "cc": 64, "sel": 64, "pre": 64, "ka": 64,
+               "k1": 64, "km": 64, "hn": H, "col": 16, "olb": C, "yb": C})):
     for _name, _n in _bufs.items():
         SCRATCH[_name] = ("sbuf", [128, _n], _ty)
 
@@ -29,9 +27,12 @@ SEMAPHORES = ["sV", "sA", "sP", "sG", "sent", "arr0", "arr1", "arr2",
 
 ALU, ACT = AluOpType, ActivationFunctionType
 
-HALF = {"X": (0, MID, 0), "Y": (MID, C, 4)}
+HALF = {"X": (0, 4, 0, 7), "Y": (256, 3, 1, 3)}
+PIECE = {"P": (0, 128, (4, 5, 6, 7), (0, 1, 2, 3)), "Q": (128, 256, (4, 5, 6, 7), (4, 5, 6, 7)), "R": (256, C, (0, 1, 2, 3), (0, 1, 2, 3))}
+HALO_BANKS = (4, 5, 6, 7)
+MID = 256
 
-ORDER = "zf z3 z2 i0 i3 i1 z1 pm cb pf i2 c28 c1 k1 k0 z0 lo i4 uo kk kk16 c1w v0 qu kk32 S16 S11 S10 S13 S15 ea S14 S17 S12 uX0.a ps qX t1 qY o1 em pk p0Y uX1 cs c8 uY0.a uY1 qe3 c2 uX2 uY2 uX3 p0X c3 uY3 qe2 uX4 uY4 qe1 uX5 uY5 jq r0X a0X0.a uX6 uY6 qe0 uX7 r0Y k2 S2X1 a0Y0.a S2X6 S2X4 S2X7 uY7 S2X0 S2X3 ci S2X5 a0X1 S2X2 S2Y3 F0Y2 F0X3 F0X0 F0Y3 S2Y0 o2X S2Y2 S2Y4 yX0.a yX1 a0X2 S2Y6 yX2 a0X3 S2Y7 yX3 i6 S2Y1 rcn S2Y5 yX4 F0X2 km km16 W0X0.a c2y a0X4 yY0.a o2Y yX5 a0X5 F0Y0 yY1 yX6 a0X6 x0 yY2 a0X7 b0X0.a yX7 a0Y1 yY3 S33 b0X1 S32 W0Y2.a a0Y2 b0X2 F0Y1 S30 b0X3 S31 b0X4 o3X a0Y3 F0X1 W0X1.a b0X5 a0Y4 b0X6 yY4 W0X2.a G0X2 W0X3.a a0Y5 b0X7 c0Y2 G0X0 G0X1 km32 yY5 h0X0 km64 km128 H0X2.a W0Y1.a W0Y3.a a0Y6 h0X1 c0Y3 a0Y7 h0X2 yY6 h0X3 b0Y0.a b0Y1 n0X b0Y2 cr m0X H0X0.a G0X3 b0Y3 W0Y0.a g0X0.v yY7 b0Y4 H0X3.a c0X0 S36 b0Y5 H0X1.a c0X1 S34 S35 g0X1.a c0X2 g0X3.a b0Y6 o3Y b0Y7 g0X2.a z0X c0X3 c0Y1 w0X0 e0X0.a w0X2 w0X1 e0X1.a h0Y4 h0Y5 h0Y6 n0Y w0X3 e0X3.a e0X2.v c0Y0 m0Y g0Y0.a t0X g0Y2.a p1X g0Y3.v r1X g0Y1.a F1X0 qv a1X0.a z0Y w0Y3 a1X1 e0Y3.a a1X2 a1X3 w0Y0 e0Y0.v w0Y2 a1X4 e0Y2.a a1X5 w0Y1 e0Y1.a t0Y x1 F1X1 F1X2 W1X2.a F1X3 p1Y a1X6 a1X7 b1X0.a F1Y0 r1Y a1Y0.v W1Y0.a b1X1 a1Y1 b1X2 F1Y2 F1Y1 W1Y2.a a1Y2 b1X3 a1Y3 b1X4 a1Y4 W1X3.a F1Y3 W1Y3.a W1Y1.a c1Y2 b1X5 G1X2 a1Y5 b1X6 a1Y6 a1Y7 W1X1.a G1X1 b1X7 W1X0.a b1Y0.v h1X0 c1Y3 b1Y1 b1Y2 h1X1 b1Y3 b1Y4 h1X2 b1Y5 h1X3 b1Y6 b1Y7 n1X G1X3 G1X0 H1X1.a c1X1 h1Y4 H1X3.a c1X3 m1X h1Y5 H1X2.a h1Y6 g1X3.a H1X0.v c1Y1 g1X2.a n1Y m1Y g1X0.v c1X0 c1X2 g1Y2.v g1X1.a z1X g1Y3.v w1X0 g1Y0.a g1Y1.a e1X0.a w1X1 w1X2 e1X2.a z1Y w1X3 w1Y2 e1Y2.a w1Y3 e1Y3.a e1X1.v c1Y0 w1Y0 e1Y0.a e1X3.v t1X w1Y1 e1Y1.v t1Y x2 p2X F2X2 W2X2.a F2X1 r2X a2X0.a p2Y r2Y a2X1 a2X2 a2Y0.a a2Y1 a2X3 a2Y2 a2X4 a2Y3 a2X5 F2Y1 a2Y4 a2X6 a2Y5 F2Y3 a2X7 a2Y6 F2X3 b2X0.v F2X0 W2X0.a F2Y2 a2Y7 W2X1.a b2X1 F2Y0 G2X0 b2X2 b2Y0.a b2Y1 b2X3 b2Y2 W2Y1.a b2X4 b2Y3 b2X5 W2X3.a W2Y3.a c2Y3 b2Y4 b2X6 b2Y5 b2X7 G2X2 h2X0 G2X1 b2Y6 h2X1 b2Y7 W2Y2.a G2X3 c2Y1 W2Y0.a H2X3.a h2X2 h2X3 h2Y4 n2X c2X3 h2Y5 H2X1.a H2X2.a m2X h2Y6 c2Y2 g2X2.a H2X0.v g2X0.a c2Y0 c2X1 g2X3.a n2Y c2X0 m2Y g2Y2.a g2X1.v g2Y3.v z2X c2X2 w2X2 g2Y1.a w2X0 w2X1 e2X2.a g2Y0.v z2Y e2X0.v w2X3 e2X3.a w2Y1 e2X1.v w2Y2 e2Y2.a e2Y1.v w2Y3 e2Y3.v w2Y0 e2Y0.a ol.a t2X OX p3X t2Y od s3X.v p3Y s3Y.a YX OY os YY"
+ORDER = "fe ipi fpad iit pmi fd icc c2 jm km pmr ijv la sel ks pre ka ilt ci c1 lb fray lo k1 iem uo c3 v0X v0Y S1X2 S1X3 jqX.a S1X1 qe1 qY o1X2 qe0 S1Y1 qu u1X1 S1Y3 S1Y2 qe2 cr.a u1X2 pk m1.a cb.a u1X3 qX o1Y2 F0R0 ps.a S2X1 p0Y p0X F0P1 qe3 jqY.a S2X2 S2X3 u1Y1 m4.a r0Y3 W0R0.a r0X1 r0X0 r0Y1 m16.a r0X3 F0R2 F0P2 r0X2 o2X2 c0P0 a0X1 u1Y2 F0R1 u2X0.a u2X1 a0X2 u1Y3 xq0 r0Y0 a0X3 u2X2 S2Y3 xs0 a0Y1 F0P0 S2Y2 F0P3 W0P0.a W0P2.a S2Y1 u2X3 F0Q0 b0X0.a r0Y2 W0R2.a b0X1 u2Y0.a ihn W0P1.a W0P3.a o2Y2 S3X2 S3X3 S3X1 b0X2 F0Q2 u2Y1 u3X0.a F0R3 rcn.a o3X2 b0X3 d0X0.a W0Q0.a F0Q3 F0Q1 u2Y2 u3X1 a0Y2 u2Y3 u3X2 d0X1 W0Q2.a W0Q1.a a0Y3 u3X3 b0Y0.a d0X2 S3Y1 S4X1 S4X3 S4X2 S4X0 b0Y1 d0X3 o4X0 G0P0 S3Y2 G0P2 W0R3.a u3Y0.a c0P2 S3Y3 b0Y2 h0X0 o3Y2 b0Y3 W0Q3.a H0P0.a c0Q0 H0P2.a c0Q2 h0X1 G0P3 n0X0 u3Y1 n0X1 h0X2 u3Y2 W0R1.a m0P d0Y0.a h0X3 n0X2 u3Y3 n0X3 d0Y1 G0P1 S4Y2 H0P3.a H0P1.a g0P2.a c0P3 c0Q1 S4Y1 m0Q S4Y0 d0Y2 g0P0.v g0P1.a d0Y3 g0P3.a c0P1 o4Y0 g0Q0.a c0Q3 z0P w0P3 w0P1 g0Q1.v g0Q3.a h0Y0 g0Q2.a z0Q e0P3.a w0P2 h0Y1 e0P2.v w0P0 n0Y0 w0Q2 e0P1.a e0P0.a w0Q3 h0Y2 n0Y1 w0Q0 e0Q2.a e0Q3.v n0Y2 w0Q1 e0Q1.v e0Q0.a m0R g0R1.a t0P g0R3.a c0R2 t0Q g0R2.v F1P1 p1X g0R0.v r1X0 r1X2 r1X1 z0R a1X1 c0R1 F1P0 r1X3 c0R0 a1X2 a1X3 c0R3 w0R2 w0R3 e0R3.v w0R0 w0R1 W1P1.a b1X0.v W1P0.a e0R2.a e0R1.v F1Q0 e0R0.a F1P2 b1X1 t0R b1X2 p1Y xq1 b1X3 F1R0 r1Y1 r1Y0 W1P2.a W1Q0.a xs1 r1Y3 W1R0.a F1R1 W1R1.a d1X0.v r1Y2 F1P3 a1Y1 F1R2 F1Q1 W1P3.a d1X1 W1Q1.a a1Y2 d1X2 a1Y3 b1Y0.v W1R2.a d1X3 F1R3 W1R3.a b1Y1 F1Q3 h1X0 b1Y2 W1Q3.a h1X1 b1Y3 h1X2 F1Q2 G1P1 G1P3 n1X1 W1Q2.a G1P2 c1P0 G1P0 d1Y0.a n1X0 c1P3 h1X3 H1P3.a c1P2 H1P2.a m1P d1Y1 n1X2 g1P3.a H1P1.v n1X3 d1Y2 g1P2.a c1Q1 H1P0.v c1Q0 g1P1.a m1Q g1Q0.a c1Q2 d1Y3 g1Q2.a g1P0.v h1Y0 z1P c1Q3 h1Y1 c1P1 g1Q1.v w1P0 h1Y2 w1P2 g1Q3.a e1P0.a z1Q n1Y2 w1P1 w1P3 w1Q2 n1Y0 n1Y1 e1P2.v w1Q1 w1Q3 m1R e1Q1.v e1Q3.v e1P1.a w1Q0 e1Q0.v e1P3.a c1R1 t1P e1Q2.a t1Q c1R3 c1R0 g1R0.v c1R2 qv g1R1.a p2X r2X1 F2P2 F2P1 g1R3.a g1R2.a r2X0 W2P1.a z1R W2P2.a F2P0 r2X2 w1R2 a2X1 w1R1 r2X3 w1R0 e1R1.a a2X2 e1R2.v w1R3 a2X3 F2P3 e1R3.v b2X0.v e1R0.a F2Q1 t1R W2P0.a p2Y b2X1 W2P3.a F2Q2 F2Q3 b2X2 F2R2 r2Y0 r2Y1 r2Y2 b2X3 F2R1 a2Y1 d2X0.v r2Y3 F2Q0 a2Y2 xq2 W2Q2.a W2Q1.a d2X1 a2Y3 xs2 d2X2 F2R0 b2Y0.v d2X3 F2R3 b2Y1 W2Q3.a W2R2.a h2X0 W2R1.a W2R3.a W2R0.a G2P1 W2Q0.a G2P2 H2P1.a b2Y2 G2P0 h2X1 c2P2 G2P3 b2Y3 h2X2 c2P1 c2P0 d2Y0.v n2X1 H2P2.a n2X0 n2X2 d2Y1 c2Q2 H2P0.a m2P h2X3 d2Y2 H2P3.v g2P2.a n2X3 g2P1.a c2Q0 d2Y3 m2Q g2P0.v c2P3 g2P3.a g2Q2.a h2Y0 c2Q1 z2P h2Y1 w2P0 w2P2 g2Q3.a g2Q1.a g2Q0.a n2Y0 w2P1 h2Y2 w2P3 n2Y1 e2P0.v n2Y2 c2Q3 e2P2.v m2R c2R0 z2Q w2Q1 w2Q2 g2R2.v e2P1.a w2Q0 w2Q3 g2R0.v e2P3.a c2R1 e2Q2.v g2R1.a c2R3 e2Q3.v c2R2 g2R3.a z2R t2P e2Q0.a w2R3 e2Q1.a w2R0 w2R2 t2Q y3Q e2R3.v s3Q.v w2R1 y3P OP.s e2R1.v OQ.s ol.a e2R0.a od.g YQ.s s3P.v YP.s e2R2.a t2R os0.s os3.a os1.a y3R os2.s OR.s s3R.v YR.s"
 
 
 def _clash(a, b):
@@ -110,19 +111,20 @@ def rank_program(g, core, T, topo):
         return
     n_ranks = len(T.cores)
     ops = []
+    now = [None]
     V, A, P, S = g.vector, g.scalar, g.tensor, g.sync
 
     def reg(xs):
         return [(x[0], x[1], x[2], x[3] if len(x) > 3 else None) for x in xs]
 
     def op(eng, fn, R=(), W=(), grp=None, inc=16, dma=True, chain=False):
-        ops.append({"eng": eng, "fn": fn, "R": reg(R), "W": reg(W), "grp": grp, "inc": inc, "dma": dma, "chain": chain})
+        ops.append({"eng": eng, "fn": fn, "R": reg(R), "W": reg(W), "grp": grp, "inc": inc, "dma": dma, "chain": chain, "word": now[0]})
 
     def bank(k):
         return ("ps", BANK * k, BANK * k + BANK)
 
-    def pv(k, a, b):
-        return T.ps[:, BANK * k + a:BANK * k + b]
+    def pv(k, a, b, step=1):
+        return T.ps[:, BANK * k + a:BANK * k + b:step]
 
     def ts(out, in0, s1, s2, op0, op1, R, W):
         if s2 is None:
@@ -133,83 +135,115 @@ def rank_program(g, core, T, topo):
     def tt(out, in0, in1, alu, R, W):
         op("V", lambda: V.tensor_tensor(out, in0, in1, alu), R, W)
 
-    def cp(out, in_, R, W):
-        op("V", lambda: V.tensor_copy(out, in_), R, W)
-
-    def act(out, in_, func, R, W, scale=1.0, bias=None):
-        if bias is None:
-            op("A", lambda: A.activation(out, in_, func, scale=scale), R, W)
-        else:
-            op("A", lambda: A.activation(out, in_, func, bias=bias, scale=scale), R, W)
-
     def move(out, in_, R, W, eng):
         if eng == "v":
-            cp(out, in_, R, W)
+            op("V", lambda: V.tensor_copy(out, in_), R, W)
         else:
-            act(out, in_, ACT.Copy, R, W)
+            op("A", lambda: A.activation(out, in_, ACT.Copy), R, W)
 
-    def fill(name, a, b, val):
-        op("V", lambda: V.memset(T[name][:, a:b], val), [], [(name, a, b)])
+    def affine(out, in_, mul, add, R, W, eng):
+        if eng == "v":
+            ts(out, in_, mul, add, ALU.mult, ALU.add, R, W)
+        else:
+            op("A", lambda: A.activation(out, in_, ACT.Identity, bias=add, scale=mul), R, W)
 
-    def iota(name, a, b, pattern, base, cm, real=True):
+    def fill(name, a, b, val, step=1):
+        op("V", lambda: V.memset(T[name][:, a:b:step], val), [], [(name, a, b)])
+
+    def iota(name, pattern, base, cm, real=True):
         if real:
-            op("G", lambda: g.iota(T[name][:, a:b], pattern, base, cm, allow_small_or_imprecise_dtypes=True), [], [(name, a, b)])
+            op("G", lambda: g.iota(T[name][:], pattern, base, cm, allow_small_or_imprecise_dtypes=True), [], [whole(name)])
         else:
-            op("G", lambda: g.iota(T[name][:, a:b], pattern, base, cm), [], [(name, a, b)])
+            op("G", lambda: g.iota(T[name][:], pattern, base, cm), [], [whole(name)])
 
     def quant(q, s, a, b, src, c0):
         op("V", lambda: V.quantize_mx(T[q][:, a:b], T[s][:, a:b], T[src][:, c0:c0 + 4 * (b - a)]),
            [(src, c0, c0 + 4 * (b - a))], [(q, a, b), (s, a, b)])
 
     def mm(k, wq, ws, wa, q, s, a, b, start, stop):
-        op("P", lambda: P.matmul_mx(pv(k, 0, b - a), T[wq][:, wa:wa + 128], T[ws][:, wa:wa + 128],
+        op("P", lambda: P.matmul_mx(T.ps[:, BANK * k:BANK * k + b - a], T[wq][:, wa:wa + 128], T[ws][:, wa:wa + 128],
                                     T[q][:, a:b], T[s][:, a:b], start, stop),
            [(wq, wa, wa + 128), (ws, wa, wa + 128), (q, a, b), (s, a, b)], [bank(k)], chain=not start)
 
-    def col(k):
-        return T.col[:, k:k + 1]
+    def col(k, n=1):
+        return T.col[:, k:k + n]
 
-    def creg(k):
-        return ("col", k, k + 1)
+    def creg(k, n=1):
+        return ("col", k, k + n)
 
     def whole(name):
         return (name, 0, SCRATCH[name][1][1])
 
-    CB, C1, C8, C2, C3, CR, C28, C2Y, CS, CI = range(10)
+    C1, C2, C3, LA, LB, KS, CI, CR, M1, M4, M16, CB = range(12)
 
-    def scan(out, a, b, src, lo, hi, stride):
-        op("V", lambda: V.tensor_tensor_scan(T[out][:, a:b], T.kk[:, 0:b - a], T[src][:, lo:hi:stride], 0.0, ALU.add, ALU.max),
-           [("kk", 0, b - a), (src, lo, hi)], [(out, a, b)])
+    def seg(side, level, h):
+        return SEG * (6 * side + 2 * (level - 1) + HALF[h][2])
 
-    def phase_op(src, lo, hi, step, dst, a, n, offs, oc, eng):
-        if eng:
-            move(T[dst][:, a:a + n], T[src][:, lo:hi:step], [(src, lo, hi)], [(dst, a, a + n)], eng)
+    def gather_max(out, win, offs, in1, R, W):
+        tt(out, win.indirect(offs), in1, ALU.max, R, W)
+
+    def level_step(side, level, h, k, eng):
+        _, nb, num, _ = HALF[h]
+        d = seg(side, level, h)
+        lo = d + 1 + Q * k
+        name, oc = "o%d" % level, 12 * num + 4 * (k - 1)
+        if level == 1:
+            n = 16 * nb if side == 0 else Q
+            gather_max(T.lv[:, lo:lo + n], T.lv[:, d:lo], T[name][:, oc:oc + n // 16], T.lv[:, lo:lo + n],
+                       [("lv", d, lo + n), (name, oc, oc + 4)], [("lv", lo, lo + n)])
+            return
+        s = seg(side, level - 1, h)
+        own, src = T.lv[:, s + 1 + k:s + 257:4], ("lv", s, s + 257)
+        if k == 0:
+            move(T.lv[:, lo:lo + Q], own, [src], [("lv", lo, lo + Q)], eng)
         else:
-            tt(T[dst][:, a:a + n], T[dst][:, 0:a].indirect(T[offs][:, oc:oc + n // 16]), T[src][:, lo:hi:step], ALU.max,
-               [(src, lo, hi), (dst, 0, a), (offs, oc, oc + n // 16)], [(dst, a, a + n)])
+            gather_max(T.lv[:, lo:lo + Q], T.lv[:, d:lo], T[name][:, oc:oc + 4], own,
+                       [src, ("lv", d, lo), (name, oc, oc + 4)], [("lv", lo, lo + Q)])
 
-    def phase1(h, k, eng, src, dst):
-        a = HALF[h][0]
-        phase_op(src, a + k, a + MID, 8, dst + h, PAD + 32 * k, 32, "o1", 4 * k + a // 128, eng)
+    def last_level(h, k):
+        a = HALF[h][0] + Q * k
+        s = seg(0, 3, h)
+        gather_max(T.rc[:, H + a:H + a + Q], T.rc[:, 0:H + a], T.o4[:, a // 16:a // 16 + 4], T.lv[:, s + 1 + k:s + 257:4],
+                   [("lv", s, s + 257), ("rc", 0, H + a), ("o4", a // 16, a // 16 + 4)], [("rc", H + a, H + a + Q)])
 
-    def phase2(h, k, eng, src, dst):
-        phase_op(src + h, PAD + k, PAD + MID, 8, dst + h, PAD + 32 * k, 32, "o2", 2 * k + HALF[h][0] // 16, eng)
+    def pick(level, h, k):
+        a, _, num, _ = HALF[h]
+        out = "vs%d" % level
+        o = a + Q * k if level == 4 else 192 * num + Q * (k - 1)
+        s = seg(1, max(level - 1, 1), h)
+        if level == 1:
+            src, R = T.lv[:, s + 1 + Q * k:s + 1 + Q * k + Q], ("lv", s + 1 + Q * k, s + 1 + Q * k + Q)
+            op("V", lambda: V.tensor_tensor_scan(T[out][:, o:o + Q], src, T.k1[:], -4 * BIG, ALU.max, ALU.add),
+               [R, whole("k1")], [(out, o, o + Q)])
+        else:
+            src, R = T.lv[:, s + 1 + k:s + 257:4], ("lv", s, s + 257)
+            op("V", lambda: V.tensor_tensor_scan(T[out][:, o:o + Q], T.km[:], src, col(CB), ALU.mult, ALU.max),
+               [R, whole("km"), creg(CB)], [(out, o, o + Q)])
 
-    def phase3(h, k):
-        phase_op("rb" + h, PAD + k % 4, PAD + MID, 4, "rc", H + 64 * k, 64, "o3", 4 * k, None)
+    def offsets(level, h, part):
+        a, nb, num, _ = HALF[h]
+        src, out = "vs%d" % level, "o%d" % level
+        if level == 4:
+            ts(T.o4[:, a // 16:a // 16 + 4 * nb], T.vs4[:, a + 15:a + Q * nb:16], col(M1), H + a - BIG, ALU.mult, ALU.add,
+               [(src, a, a + Q * nb), creg(M1)], [(out, a // 16, a // 16 + 4 * nb)])
+            return
+        lo, hi = ((0, 1), (1, 3), (0, 3))[part]
+        mul, c = ((C1, C1), (M16, C2), (M4, C3))[level - 1]
+        ts(T[out][:, 12 * num + 4 * lo:12 * num + 4 * hi], T[src][:, 192 * num + Q * lo + 15:192 * num + Q * hi:16],
+           -64.0 if level == 1 else col(mul), col(c), ALU.mult, ALU.add,
+           [(src, 192 * num + Q * lo, 192 * num + Q * hi), creg(c), creg(mul)], [(out, 12 * num + 4 * lo, 12 * num + 4 * hi)])
 
-    def send(t):
+    def send(name, wide):
         if rank + 1 >= n_ranks:
             return
         dst = T.cores[rank + 1]
         rid, pid = topo.addr(dst, core)
         mask = topo.mask(core, dst)
-        n_eng = len(topo.engines(core, dst))
-        q, s = "q%d" % t, "s%d" % t
-        op("G", lambda: g.remote_dma(T[q][:, 0:H].bitcast(dt.uint8), T[q][:, C:C + H].bitcast(dt.uint8),
-                                     T.sem["arr%d" % t], T.sem.sent, pid, rid, mask), [(q, C, C + H)], [], "sent", n_eng, False)
-        op("G", lambda: g.remote_dma(T[s][:, 0:H], T[s][:, C:C + H],
-                                     T.sem["arr%d" % t], T.sem.sent, pid, rid, mask), [(s, C, C + H)], [], "sent", n_eng, False)
+        out, in_ = T[name][:, 0:H], T[name][:, C:C + H]
+        if wide:
+            out, in_ = out.bitcast(dt.uint8), in_.bitcast(dt.uint8)
+        op("G", lambda: g.remote_dma(out, in_, T.sem["arr" + name[1]], T.sem.sent, pid, rid, mask),
+           [(name, C, C + H)], [], "sent", len(topo.engines(core, dst)), False)
 
     def arrive(t):
         if rank > 0:
@@ -220,161 +254,163 @@ def rank_program(g, core, T, topo):
         if eng == "v":
             ts(out, pv(k, 0, n), 1.0 / 64, None, ALU.mult, None, [bank(k)], W)
         else:
-            act(out, pv(k, 0, n), ACT.Copy, [bank(k)], W, scale=1.0 / 64)
+            op("A", lambda: A.activation(out, pv(k, 0, n), ACT.Copy, scale=1.0 / 64), [bank(k)], W)
 
-    def zero_halo():
-        if rank == 0:
-            for t in range(ROUNDS):
-                for k in range(4):
-                    fill("fw%d" % t, (H + C) * k, (H + C) * k + H, 0.0)
+    def root_step(kind, t, h, k, eng):
+        a, nb, num, pb = HALF[h]
+        q, s = "q%d" % t, "s%d" % t
+        if kind == "p":
+            mm(pb, "qu", "su", 0, q, s, H + a, H + a + Q * nb, True, True)
+        elif kind == "r":
+            lo, n, j = seg(0, 1, h) + 1 + Q * k, 16 * nb, 256 * num + Q * k
+            tt(T.lv[:, lo:lo + n], pv(pb, k, Q * nb, 4), T.jq[:, j:j + n], ALU.min, [bank(pb), ("jq", j, j + n)], [("lv", lo, lo + n)])
+        elif kind in "abd":
+            level_step(0, 1 + "abd".index(kind), h, k, eng)
+        elif kind == "h":
+            last_level(h, k)
+        elif kind == "n":
+            a += Q * k
+            op("V", lambda: V.tensor_tensor_scan(T.rs[:, a:a + Q], T.km[:], T.rc[:, H + a:H + a + Q], col(CI), ALU.mult, ALU.max),
+               [whole("km"), ("rc", H + a, H + a + Q), creg(CI)], [("rs", a, a + Q)])
 
-    def round_step(kind, t, h, k, eng):
-        a, b, k0 = HALF[h]
+    def layer_step(kind, t, h, k, eng):
+        a, b, fb, sb = PIECE[h]
         q, s, fw, tn = "q%d" % t, "s%d" % t, "fw%d" % t, "tt%d" % (t + 1)
         w = (H + C) * k
-        if kind == "p":
-            wq, ws = ("qu", "su") if t < ROUNDS else ("qv", "sv")
-            mm(k0 + 3, wq, ws, 0, q, s, H + a, H + b, True, True)
-        elif kind == "r":
-            tt(T.r0[:, a:b], pv(k0 + 3, 0, b - a), T.jq[:, a:b], ALU.min, [bank(k0 + 3), ("jq", a, b)], [("r0", a, b)])
+        if kind == "y":
+            mm(sb[3], "qv", "sv", 0, q, s, H + a, H + b, True, True)
         elif kind == "s":
-            move(T.yb[:, a:b], pv(k0 + 3, 0, b - a), [bank(k0 + 3)], [("yb", a, b)], eng)
-        elif kind == "a":
-            phase1(h, k, eng, "r0", "ra")
-        elif kind == "b":
-            phase2(h, k, eng, "ra", "rb")
-        elif kind == "h":
-            phase3(h, k)
-        elif kind == "n":
-            op("V", lambda: V.tensor_tensor_scan(T.rs[:, a:b], T.km[:, 0:b - a], T.rc[:, H + a:H + b], col(CI), ALU.mult, ALU.max),
-               [("km", 0, b - a), ("rc", H + a, H + b), creg(CI)], [("rs", a, b)])
+            move(T.yb[:, a:b], pv(sb[3], 0, b - a), [bank(sb[3])], [("yb", a, b)], eng)
         elif kind == "m":
             ts(T.off[:, a // 16:b // 16], T.rs[:, a + 15:b:16], col(CR), BIG + H, ALU.mult, ALU.add,
                [("rs", a, b), creg(CR)], [("off", a // 16, b // 16)])
         elif kind == "F":
-            mm(k0 + k, "qe", "se", 128 * k, q, s, H + a, H + b, True, True)
+            mm(fb[k], "qe", "se", 128 * k, q, s, H + a, H + b, True, True)
         elif kind == "W":
-            scaled(T[fw][:, w + H + a:w + H + b], k0 + k, b - a, [(fw, w + H + a, w + H + b)], eng)
+            scaled(T[fw][:, w + H + a:w + H + b], fb[k], b - a, [(fw, w + H + a, w + H + b)], eng)
         elif kind == "G":
             if rank > 0:
-                mm(k0 + k, "qe", "se", 128 * k, q, s, 0, H, True, True)
+                mm(HALO_BANKS[k], "qe", "se", 128 * k, q, s, 0, H, True, True)
         elif kind == "H":
             if rank > 0:
-                scaled(T[fw][:, w:w + H], k0 + k, H, [(fw, w, w + H)], eng)
+                scaled(T[fw][:, w:w + H], HALO_BANKS[k], H, [(fw, w, w + H)], eng)
+            else:
+                affine(T[fw][:, w:w + H], T.e64[:, 0:H], 0.0, 0.0, [("e64", 0, H)], [(fw, w, w + H)], eng)
         elif kind == "c":
-            mm(k0 + k, "qe", "se", 128 * k, q, s, H + a, H + b, True, False)
+            mm(sb[k], "qe", "se", 128 * k, q, s, H + a, H + b, True, False)
         elif kind == "g":
             move(T.zt[:, 4 * a + k:4 * b:4], T[fw][:, w:w + H + b].indirect(T.off[:, a // 16:b // 16]),
                  [(fw, w, w + H + b), ("off", a // 16, b // 16)], [("zt", 4 * a, 4 * b, k)], eng)
         elif kind == "z":
             quant("qz", "sz", a, b, "zt", 4 * a)
         elif kind == "w":
-            mm(k0 + k, "qw", "sw", 128 * k, "qz", "sz", a, b, False, True)
+            mm(sb[k], "qw", "sw", 128 * k, "qz", "sz", a, b, False, True)
         elif kind == "e":
-            scaled(T[tn][:, 4 * a + k:4 * b:4], k0 + k, b - a, [(tn, 4 * a, 4 * b, k)], eng)
+            scaled(T[tn][:, 4 * a + k:4 * b:4], sb[k], b - a, [(tn, 4 * a, 4 * b, k)], eng)
         elif kind == "t":
             quant("q%d" % (t + 1), "s%d" % (t + 1), H + a, H + b, tn, 4 * a)
 
+    def dma(eng, out, in_, R, W, grp):
+        q = {"s": S, "a": A, "g": g}[eng]
+        op(eng.upper(), lambda: q.dma_start(out, in_), R, W, grp)
+
     def store(eng, out, in_, R):
-        q = {"S": S, "A": A, "G": g}[eng]
-        op(eng, lambda: q.dma_start(out, in_), R, [], "dOl" if eng == "G" else "dOut")
+        dma(eng, out, in_, R, [], "dOl" if eng == "g" else "dOut")
 
     for t in range(ROUNDS):
+        now[0] = "arr%d" % t
         arrive(t)
+    now[0] = "load"
     for i in range(16):
-        eng, q = ("S", S) if i % 2 == 0 else ("A", A)
-        op(eng, lambda i=i, q=q: q.dma_start(T.drep[i::16, :], T.dist[:]), [], [("drep", 0, C)], "dD")
-    op("A", lambda: A.dma_start(T.xt[:, 4 * MID:4 * C], T.x[:, 4 * MID:4 * C]), [], [("xt", 4 * MID, 4 * C)], "dXL")
-    op("A", lambda: A.dma_start(T.ut[:], T.u[:]), [], [("ut", 0, 512)], "dU")
-    op("S", lambda: S.dma_start(T.xt[:, 0:4 * MID], T.x[:, 0:4 * MID]), [], [("xt", 0, 4 * MID)], "dXF")
-    op("S", lambda: S.dma_start(T.qw[:].bitcast(dt.uint8), T.wc[:]), [], [("qw", 0, 512)], "dW")
-    op("S", lambda: S.dma_start(T.sw[:], T.ws[:]), [], [("sw", 0, 512)], "dW")
-    op("S", lambda: S.dma_start(T.vt[:], T.v[:]), [], [("vt", 0, 512)], "dV")
+        dma("sa"[i % 2], T.drep[i::16, 0:C], T.dist[:], [], [("drep", 0, C)], "dD")
+    dma("a", T.xt[:, 4 * MID:4 * C], T.x[:, 4 * MID:4 * C], [], [("xt", 4 * MID, 4 * C)], "dXL")
+    dma("a", T.ut[:], T.u[:], [], [("ut", 0, 512)], "dU")
+    dma("s", T.xt[:, 0:4 * MID], T.x[:, 0:4 * MID], [], [("xt", 0, 4 * MID)], "dXF")
+    dma("s", T.qw[:].bitcast(dt.uint8), T.wc[:], [], [("qw", 0, 512)], "dW")
+    dma("s", T.sw[:], T.ws[:], [], [("sw", 0, 512)], "dW")
+    dma("s", T.vt[:], T.v[:], [], [("vt", 0, 512)], "dV")
 
-    i_col, ireg = T.pf[:, 0:1], ("pf", 0, 1)
     qn, sn = "q%d" % ROUNDS, "s%d" % ROUNDS
+    pi_, pr_ = T.pm[:, 0:1], T.pm[:, 1:2]
+    ireg, rreg = ("pm", 0, 1), ("pm", 1, 2)
+    ray = seg(0, 1, "Y") + 1
     once = {
-        "i0": lambda: iota("pi", 0, 1, [[0, 1]], 0, 1, False),
-        "i1": lambda: iota("pi", 1, 2, [[0, 1]], 0, 4, False),
-        "i2": lambda: iota("jn", H - 8, JW, [[1, JW - H + 8]], -8, 0),
-        "i3": lambda: iota("p4", 0, 1, [[0, 1]], -3, -4),
-        "i4": lambda: iota("c16", 0, 32, [[0, 8], [32 * MID, 2], [255 * 16, 2]], 0, 0),
-        "i6": lambda: iota("jn", 0, H - 8, [[1, H - 8]], -H, 0),
-        "z0": lambda: fill("v0", C, 512, float(H)),
-        "z1": lambda: fill("r0", C, 512, -1.0),
-        "z2": lambda: [fill(n, 0, PAD, -2 * BIG) for n in ("vaX", "vaY", "raX", "raY")],
-        "z3": lambda: [fill(n, 0, PAD, -2 * BIG) for n in ("vbX", "vbY", "rbX", "rbY")],
-        "zf": zero_halo,
-        "pm": lambda: ts(T.pm[:], T.pi[:], 15, None, ALU.bitwise_and, None, [whole("pi")], [whole("pm")]),
-        "c28": lambda: ts(col(C28), T.pm[:, 0:1], 28.0, None, ALU.mult, None, [("pm", 0, 1)], [creg(C28)]),
-        "pf": lambda: cp(T.pf[:], T.pm[:], [whole("pm")], [whole("pf")]),
-        "cb": lambda: ts(col(CB), T.pm[:, 0:1], 15.0, BIG, ALU.is_lt, ALU.mult, [("pm", 0, 1)], [creg(CB)]),
-        "c1": lambda: ts(col(C1), i_col, -255.0 / 32, col(CB), ALU.mult, ALU.add, [ireg, creg(CB)], [creg(C1)]),
-        "k0": lambda: ts(T.k0[:], T.jn[:, H:H + 16], i_col, -2 * BIG, ALU.is_equal, ALU.mult, [("jn", H, H + 16), ireg], [whole("k0")]),
-        "k1": lambda: ts(T.k1[:], T.jn[:, H - 1:H + 15], i_col, BIG, ALU.is_equal, ALU.mult, [("jn", H - 1, H + 15), ireg], [whole("k1")]),
-        "lo": lambda: ts(T.lo[:, 0:28], T.jn[:, H:H + 28], col(C28), None, ALU.add, None, [("jn", H, H + 28), creg(C28)], [("lo", 0, 28)]),
-        "kk": lambda: tt(T.kk[:, 0:16], T.k0[:], T.k1[:], ALU.add, [whole("k0"), whole("k1")], [("kk", 0, 16)]),
-        "uo": lambda: cp(T.uo[:], T.jn[:, H:H + 128:16], [("jn", H, H + 128)], [whole("uo")]),
-        "ea": lambda: act(T.ea[:], T.jn[:, H:JW], ACT.Abs, [("jn", H, JW), whole("p4")], [whole("ea")], 1.0, T.p4[:]),
-        "em": lambda: act(T.em[:], T.ea[:], ACT.Relu, [whole("ea")], [whole("em")], -64.0, 64.0),
-        "c1w": lambda: ts(T.c1[:], T.c16[:], -1.0 / 32, col(C1), ALU.mult, ALU.add, [whole("c16"), creg(C1)], [whole("c1")]),
-        "c8": lambda: act(col(C8), col(CB), ACT.Identity, [creg(CB)], [creg(C8)], 4.0, float(PAD)),
-        "c3": lambda: act(col(C3), col(CB), ACT.Identity, [creg(CB)], [creg(C3)], 1.0, float(H)),
-        "cr": lambda: act(col(CR), col(CB), ACT.Identity, [creg(CB)], [creg(CR)], -2.0 / BIG / TINY, 1.0 / TINY),
-        "cs": lambda: act(col(CS), col(CB), ACT.Identity, [creg(CB)], [creg(CS)], -4.0 / BIG ** 3, 2.0 / BIG ** 2),
-        "ci": lambda: act(col(CI), col(CB), ACT.Identity, [creg(CB)], [creg(CI)], 2.0 / BIG, -1.0),
-        "c2": lambda: act(col(C2), T.pf[:, 1:2], ACT.Identity, [("pf", 1, 2), creg(C8)], [creg(C2)], -255.0 / 4, col(C8)),
-        "c2y": lambda: act(col(C2Y), col(C2), ACT.Identity, [creg(C2)], [creg(C2Y)], 1.0, -4.0 * MID),
-        "k2": lambda: act(T.k2[:], T.kk[:, 0:16], ACT.Square, [("kk", 0, 16)], [whole("k2")]),
-        "km": lambda: act(T.km[:, 0:16], T.k2[:], ACT.Identity, [whole("k2"), creg(CS)], [("km", 0, 16)], col(CS), 1.0),
-        "jq": lambda: act(T.jq[:], T.jn[:, H:H + C], ACT.Identity, [("jn", H, H + C)], [whole("jq")], TINY, -BIG * TINY),
-        "rcn": lambda: act(T.rc[:, 0:H], T.jn[:, 0:H], ACT.Identity, [("jn", 0, H)], [("rc", 0, H)], TINY, -BIG * TINY),
-        "v0": lambda: tt(T.v0[:, 0:C], T.drep[:].indirect(T.lo[:, 0:28]), T.jn[:, H:H + C], ALU.subtract,
-                         [whole("drep"), ("lo", 0, 28), ("jn", H, H + C)], [("v0", 0, C)]),
-        "qY": lambda: quant("q0", "s0", H + MID, H + C, "xt", 4 * MID),
-        "qX": lambda: quant("q0", "s0", H, H + MID, "xt", 0),
-        "qu": lambda: quant("qu0", "su0", 0, 128, "ut", 0),
-        "qv": lambda: quant("qv", "sv", 0, 128, "vt", 0),
-        "t1": lambda: tt(T.t1[:], T.vs1[:, 15:512:16], T.c1[:], ALU.subtract, [whole("vs1"), whole("c1")], [whole("t1")]),
-        "pk": lambda: cp(T.qu[:].bitcast(dt.uint32), T.qu0[:].bitcast(dt.uint32).indirect(T.uo[:]), [whole("qu0"), whole("uo")], [whole("qu")]),
-        "ps": lambda: op("A", lambda: A.activation(T.su[:], T.su0[:].indirect(T.uo[:]), ACT.Copy), [whole("su0"), whole("uo")], [whole("su")]),
-        "o1": lambda: ts(T.o1[:], T.t1[:], -32.0, float(PAD), ALU.mult, ALU.add, [whole("t1")], [whole("o1")]),
-        "ol": lambda: act(T.olb[:], T.rc[:, H:H + C], ACT.Identity, [("rc", H, H + C)], [whole("olb")], 1.0 / TINY, BIG),
-        "od": lambda: store("G", T.ol[:], T.olb[0::16, :], [whole("olb")]),
-        "os": lambda: [store("SA"[k % 2], T.osc[4 * k:4 * k + 4, :], T[sn][32 * k:32 * k + 4, H:H + C], [(sn, H, H + C)]) for k in range(4)],
+        "ipi": lambda e: iota("pi", [[0, 1]], 0, 1, False),
+        "ilt": lambda e: iota("lt", [[16, 2], [28, 4], [4, 4]], 0, 0),
+        "ijv": lambda e: iota("jv", [[1, 4], [4, Q]], int(BIG), 0),
+        "iit": lambda e: iota("it", [[2, 64]], 256, -2, False),
+        "icc": lambda e: iota("cc", [[255, 4], [0, 16]], int(4 * BIG), 0),
+        "ihn": lambda e: iota("hn", [[1, H]], -H - int(BIG), 0),
+        "fpad": lambda e: fill("lv", 0, 12 * SEG, -2 * BIG, SEG),
+        "fray": lambda e: fill("lv", ray, ray + 256, -1.0),
+        "fd": lambda e: fill("drep", C, C + 8, 1),
+        "fe": lambda e: fill("e64", 0, 520, 64.0),
+        "iem": lambda e: op("G", lambda: g.affine_select(T.em[:], T.e64[:], [[1, 520]], ALU.is_equal, 0.0, -3, -4), [whole("e64")], [whole("em")]),
+        "pmi": lambda e: ts(pi_, T.pi[:], 15, None, ALU.bitwise_and, None, [whole("pi")], [ireg]),
+        "pmr": lambda e: ts(pr_, T.pi[:], 3, None, ALU.bitwise_and, None, [whole("pi")], [rreg]),
+        "la": lambda e: ts(col(LA), pi_, 0.25, None, ALU.mult, None, [ireg], [creg(LA)]),
+        "lb": lambda e: ts(col(LB), pr_, 111.75, None, ALU.mult, None, [rreg], [creg(LB)]),
+        "lo": lambda e: ts(T.lo[:], T.lt[:], col(LA), col(LB), ALU.add, ALU.add, [whole("lt"), creg(LA, 2)], [whole("lo")]),
+        "c2": lambda e: ts(col(C2), pi_, -255.0, 1 - 16 * BIG, ALU.mult, ALU.add, [ireg], [creg(C2)]),
+        "c3": lambda e: ts(col(C3), pr_, -255.0, 1 - 4 * BIG, ALU.mult, ALU.add, [rreg], [creg(C3)]),
+        "ks": lambda e: ts(col(KS), pi_, 0.0, -128 * BIG, ALU.is_equal, ALU.mult, [ireg], [creg(KS)]),
+        "c1": lambda e: ts(col(C1), col(C2), 16 * BIG, col(KS), ALU.add, ALU.add, [creg(C2), creg(KS)], [creg(C1)]),
+        "ci": lambda e: ts(col(CI), pi_, 15.0, 0.5, ALU.is_lt, ALU.subtract, [ireg], [creg(CI)]),
+        "cr": lambda e: affine(col(CR), col(CI), -2.0 / TINY, 0.0, [creg(CI)], [creg(CR)], e),
+        "m1": lambda e: affine(col(M1), col(CI), 2.0, 0.0, [creg(CI)], [creg(M1)], e),
+        "m4": lambda e: affine(col(M4), col(CI), 8.0, 0.0, [creg(CI)], [creg(M4)], e),
+        "m16": lambda e: affine(col(M16), col(CI), 32.0, 0.0, [creg(CI)], [creg(M16)], e),
+        "cb": lambda e: affine(col(CB), col(CI), 4 * BIG, 0.0, [creg(CI)], [creg(CB)], e),
+        "jm": lambda e: ts(T.jm[:], T.it[:], 31, None, ALU.bitwise_and, None, [whole("it")], [whole("jm")]),
+        "km": lambda e: ts(T.km[:], T.jm[:], -3.0, 1.0, ALU.add, ALU.min, [whole("jm")], [whole("km")]),
+        "sel": lambda e: ts(T.sel[:], T.jm[:], 0.0, 0.25, ALU.is_equal, ALU.mult, [whole("jm")], [whole("sel")]),
+        "pre": lambda e: ts(T.pre[:], T.jm[:], 30.0, -2 * BIG, ALU.is_equal, ALU.mult, [whole("jm")], [whole("pre")]),
+        "ka": lambda e: tt(T.ka[:], T.sel[:], T.cc[:], ALU.mult, [whole("sel"), whole("cc")], [whole("ka")]),
+        "k1": lambda e: tt(T.k1[:], T.ka[:], T.pre[:], ALU.add, [whole("ka"), whole("pre")], [whole("k1")]),
+        "rcn": lambda e: affine(T.rc[:, 0:H], T.hn[:], TINY, 0.0, [whole("hn")], [("rc", 0, H)], e),
+        "uo": lambda e: ts(T.uo[:], T.jv[:, 0:32:4], BIG, None, ALU.subtract, None, [("jv", 0, 32)], [whole("uo")]),
+        "qu": lambda e: quant("qu0", "su0", 0, 128, "ut", 0),
+        "pk": lambda e: op("V", lambda: V.tensor_copy(T.qu[:].bitcast(dt.uint32), T.qu0[:].bitcast(dt.uint32).indirect(T.uo[:])),
+                           [whole("qu0"), whole("uo")], [whole("qu")]),
+        "ps": lambda e: move(T.su[:], T.su0[:].indirect(T.uo[:]), [whole("su0"), whole("uo")], [whole("su")], e),
+        "qY": lambda e: quant("q0", "s0", H + MID, H + C, "xt", 4 * MID),
+        "qX": lambda e: quant("q0", "s0", H, H + MID, "xt", 0),
+        "qv": lambda e: quant("qv", "sv", 0, 128, "vt", 0),
+        "ol": lambda e: affine(T.olb[:], T.rc[:, H:H + C], 1.0 / TINY, BIG, [("rc", H, H + C)], [whole("olb")], e),
+        "od": lambda e: store(e, T.ol[:], T.olb[0::16, :], [whole("olb")]),
     }
-    for name, top in (("kk", 64), ("km", 256)):
-        for w in (16, 32, 64, 128):
-            if w < top:
-                once["%s%d" % (name, w)] = lambda w=w, name=name: act(T[name][:, w:2 * w], T[name][:, 0:w], ACT.Copy, [(name, 0, w)], [(name, w, 2 * w)])
-    for k in range(8):
-        once["S1%d" % k] = lambda k=k: scan("vs1", 64 * k, 64 * k + 64, "v0", k, 512, 8)
-    for k in range(7):
-        once["S3%d" % k] = lambda k=k: scan("vs3", 64 * k, 64 * k + 64, "vb" + "XY"[k // 4], PAD + k % 4, PAD + MID, 4)
     for k in range(4):
-        once["qe%d" % k] = lambda k=k: quant("qe", "se", 128 * k, 128 * k + 128, "em", 3 - k)
+        once["qe%d" % k] = lambda e, k=k: quant("qe", "se", 128 * k, 128 * k + 128, "em", 3 - k)
+        once["os%d" % k] = lambda e, k=k: store(e, T.osc[4 * k:4 * k + 4, :], T[sn][32 * k:32 * k + 4, H:H + C], [(sn, H, H + C)])
+    for h, (a, nb, num, _) in HALF.items():
+        va = seg(1, 1, h) + 1
+        once["jq" + h] = lambda e, a=a, num=num: affine(T.jq[:, 256 * num:256 * num + 256], T.jv[:], TINY, (a - 2 * BIG) * TINY,
+                                                        [whole("jv")], [("jq", 256 * num, 256 * num + 256)], e)
+        once["v0" + h] = lambda e, va=va, num=num: tt(T.lv[:, va:va + 256], T.drep[:].indirect(T.lo[:, 16 * num:16 * num + 16]), T.jv[:], ALU.subtract,
+                                                      [whole("drep"), ("lo", 16 * num, 16 * num + 16), whole("jv")], [("lv", va, va + 256)])
+        for level in (1, 2, 3, 4):
+            for k in (range(nb) if level == 4 else range(1, 4)):
+                once["S%d%s%d" % (level, h, k)] = lambda e, level=level, h=h, k=k: pick(level, h, k)
+            for part in range(1 if level == 4 else 3):
+                once["o%d%s%d" % (level, h, part)] = lambda e, level=level, h=h, part=part: offsets(level, h, part)
+            if level < 4:
+                for k in range(4):
+                    once["u%d%s%d" % (level, h, k)] = lambda e, level=level, h=h, k=k: level_step(1, level, h, k, e)
     for t in range(ROUNDS):
-        once["x%d" % t] = lambda t=t: send(t)
-    for h, (a, b, k0) in HALF.items():
-        c2 = C2Y if a else C2
-        for k in range(8):
-            once["S2%s%d" % (h, k)] = lambda h=h, k=k, a=a: scan("vs2", a + 32 * k, a + 32 * k + 32, "va" + h, PAD + k, PAD + MID, 8)
-        once["o2" + h] = lambda a=a, c2=c2: ts(T.o2[:, a // 16:a // 16 + 16], T.vs2[:, a + 15:a + MID:16], -4.0, col(c2), ALU.mult, ALU.add,
-                                               [("vs2", a, a + MID), creg(c2)], [("o2", a // 16, a // 16 + 16)])
-        once["o3" + h] = lambda a=a, b=b: ts(T.o3[:, a // 16:b // 16], T.vs3[:, a + 15:b:16], -1.0, col(C3), ALU.mult, ALU.add,
-                                             [("vs3", a, b), creg(C3)], [("o3", a // 16, b // 16)])
-        once["O" + h] = lambda a=a, b=b: store("S", T.oc[:, 4 * a:4 * b], T[qn][:, H + a:H + b].bitcast(dt.uint8), [(qn, H + a, H + b)])
-        once["Y" + h] = lambda a=a, b=b: store("A" if a else "S", T.y[:, a:b], T.yb[:, a:b], [("yb", a, b)])
+        once["xq%d" % t] = lambda e, t=t: send("q%d" % t, True)
+        once["xs%d" % t] = lambda e, t=t: send("s%d" % t, False)
+    for h, (a, b, _, _) in PIECE.items():
+        once["O" + h] = lambda e, a=a, b=b: store(e, T.oc[:, 4 * a:4 * b], T[qn][:, H + a:H + b].bitcast(dt.uint8), [(qn, H + a, H + b)])
+        once["Y" + h] = lambda e, a=a, b=b: store(e, T.y[:, a:b], T.yb[:, a:b], [("yb", a, b)])
 
     for word in ORDER.split():
         name, eng = word.split(".") if "." in word else (word, None)
+        now[0] = word
         if name in once:
-            once[name]()
-        elif name[0] == "u":
-            phase1(name[1], int(name[2]), eng, "v0", "va")
-        elif name[0] == "y":
-            phase2(name[1], int(name[2]), eng, "va", "vb")
+            once[name](eng)
+        elif name[0] in "prabdhn":
+            root_step(name[0], int(name[1]), name[2], int(name[3:] or 0), eng)
         else:
-            round_step(name[0], int(name[1]), name[2], int(name[3:] or 0), eng)
+            layer_step(name[0], int(name[1]), name[2], int(name[3:] or 0), eng)
 
     _emit(g, T, ops, ["sent", "dOl", "dOut"])

@@ -10,29 +10,31 @@ X4, U8, F32, BF, I32, U16 = "float8_e4m3fn_x4", "uint8", "float32", "bfloat16", 
 
 SCRATCH = {"ps": ("psum", [128, 8 * BANK], F32)}
 for _ty, _bufs in (
-        (I32, {"drep": C + 8, "pi": 1, "pm": 2, "it": 64, "jm": 64}),
-        (BF, {"xt": 4 * C, "ut": 512, "vt": 512, "e64": 520, "em": 520, "zt": 4 * C, "tt1": 4 * C,
+        (I32, {"drep": C, "ty": 12, "tb": 12, "pi": 1, "pm": 2, "it": 64, "jm": 64}),
+        (BF, {"xt": 4 * C, "ut": 512, "vt": 512, "e64": 128, "em": 520, "zt": 4 * C, "tt1": 4 * C,
               "tt2": 4 * C, "tt3": 4 * C, "fw0": 4 * (H + C), "fw1": 4 * (H + C), "fw2": 4 * (H + C)}),
         (X4, {"qu0": 128, "qu": 128, "qv": 128, "qw": 512, "qe": 512, "qz": C, "q0": C + H, "q1": C + H, "q2": C + H, "q3": C + H}),
         (U8, {"su0": 128, "su": 128, "sv": 128, "sw": 512, "se": 512, "sz": C, "s0": C + H, "s1": C + H, "s2": C + H, "s3": C + H}),
-        (U16, {"o1": 24, "o2": 24, "o3": 24, "o4": 28, "off": 28, "lo": 32, "uo": 8}),
-        (F32, {"lv": 12 * SEG, "rc": H + C, "rs": C, "vs1": 384, "vs2": 384, "vs3": 384, "vs4": C,
-               "jv": 256, "jq": 512, "lt": 32, "cc": 64, "sel": 64, "pre": 64, "ka": 64,
-               "k1": 64, "km": 64, "hn": H, "col": 16, "olb": C, "yb": C})):
+        (U16, {"o1": 24, "o2": 24, "o3": 24, "o4": 32, "off": 28, "lo": 32, "uo": 8}),
+        (F32, {"lv": 12 * SEG, "rc": H + C, "rs": C, "vs": 1664, "w28": 12, "wb": 12, "wc2": 12,
+               "jvX": 256, "jvY": 192, "jq": 512, "lt": 16, "ly": 12, "pf": 2, "ct": 12, "bt": 24, "t1": 24,
+               "km": 64, "hn": H, "col": 24, "olb": C, "yb": C})):
     for _name, _n in _bufs.items():
         SCRATCH[_name] = ("sbuf", [128, _n], _ty)
 
 SEMAPHORES = ["sV", "sA", "sP", "sG", "sent", "arr0", "arr1", "arr2",
-              "dD", "dXL", "dXF", "dU", "dV", "dW", "dOl", "dOut"]
+              "dD", "dXL", "dXF", "dU", "dV", "dW", "dOut"]
 
 ALU, ACT = AluOpType, ActivationFunctionType
 
 HALF = {"X": (0, 4, 0, 7), "Y": (256, 3, 1, 3)}
-PIECE = {"P": (0, 128, (4, 5, 6, 7), (0, 1, 2, 3)), "Q": (128, 256, (4, 5, 6, 7), (4, 5, 6, 7)), "R": (256, C, (0, 1, 2, 3), (0, 1, 2, 3))}
+PIECE = {"P": (0, 128, (0, 1, 2, 3)), "Q": (128, 256, (4, 5, 6, 7)), "R": (256, C, (0, 1, 2, 3))}
+UNPACK = {"P": (0, 128, (4, 5, 6, 4)), "Q": (128, 256, (5, 6, 4, 5)), "R": (256, C, (0, 1, 2, 0))}
 HALO_BANKS = (4, 5, 6, 7)
+LAST = "PQR"
 MID = 256
 
-ORDER = "fe ipi fpad iit pmi fd icc c2 jm km pmr ijv la sel ks pre ka ilt ci c1 lb fray lo k1 iem uo c3 v0X v0Y S1X2 S1X3 jqX.a S1X1 qe1 qY o1X2 qe0 S1Y1 qu u1X1 S1Y3 S1Y2 qe2 cr.a u1X2 pk m1.a cb.a u1X3 qX o1Y2 F0R0 ps.a S2X1 p0Y p0X F0P1 qe3 jqY.a S2X2 S2X3 u1Y1 m4.a r0Y3 W0R0.a r0X1 r0X0 r0Y1 m16.a r0X3 F0R2 F0P2 r0X2 o2X2 c0P0 a0X1 u1Y2 F0R1 u2X0.a u2X1 a0X2 u1Y3 xq0 r0Y0 a0X3 u2X2 S2Y3 xs0 a0Y1 F0P0 S2Y2 F0P3 W0P0.a W0P2.a S2Y1 u2X3 F0Q0 b0X0.a r0Y2 W0R2.a b0X1 u2Y0.a ihn W0P1.a W0P3.a o2Y2 S3X2 S3X3 S3X1 b0X2 F0Q2 u2Y1 u3X0.a F0R3 rcn.a o3X2 b0X3 d0X0.a W0Q0.a F0Q3 F0Q1 u2Y2 u3X1 a0Y2 u2Y3 u3X2 d0X1 W0Q2.a W0Q1.a a0Y3 u3X3 b0Y0.a d0X2 S3Y1 S4X1 S4X3 S4X2 S4X0 b0Y1 d0X3 o4X0 G0P0 S3Y2 G0P2 W0R3.a u3Y0.a c0P2 S3Y3 b0Y2 h0X0 o3Y2 b0Y3 W0Q3.a H0P0.a c0Q0 H0P2.a c0Q2 h0X1 G0P3 n0X0 u3Y1 n0X1 h0X2 u3Y2 W0R1.a m0P d0Y0.a h0X3 n0X2 u3Y3 n0X3 d0Y1 G0P1 S4Y2 H0P3.a H0P1.a g0P2.a c0P3 c0Q1 S4Y1 m0Q S4Y0 d0Y2 g0P0.v g0P1.a d0Y3 g0P3.a c0P1 o4Y0 g0Q0.a c0Q3 z0P w0P3 w0P1 g0Q1.v g0Q3.a h0Y0 g0Q2.a z0Q e0P3.a w0P2 h0Y1 e0P2.v w0P0 n0Y0 w0Q2 e0P1.a e0P0.a w0Q3 h0Y2 n0Y1 w0Q0 e0Q2.a e0Q3.v n0Y2 w0Q1 e0Q1.v e0Q0.a m0R g0R1.a t0P g0R3.a c0R2 t0Q g0R2.v F1P1 p1X g0R0.v r1X0 r1X2 r1X1 z0R a1X1 c0R1 F1P0 r1X3 c0R0 a1X2 a1X3 c0R3 w0R2 w0R3 e0R3.v w0R0 w0R1 W1P1.a b1X0.v W1P0.a e0R2.a e0R1.v F1Q0 e0R0.a F1P2 b1X1 t0R b1X2 p1Y xq1 b1X3 F1R0 r1Y1 r1Y0 W1P2.a W1Q0.a xs1 r1Y3 W1R0.a F1R1 W1R1.a d1X0.v r1Y2 F1P3 a1Y1 F1R2 F1Q1 W1P3.a d1X1 W1Q1.a a1Y2 d1X2 a1Y3 b1Y0.v W1R2.a d1X3 F1R3 W1R3.a b1Y1 F1Q3 h1X0 b1Y2 W1Q3.a h1X1 b1Y3 h1X2 F1Q2 G1P1 G1P3 n1X1 W1Q2.a G1P2 c1P0 G1P0 d1Y0.a n1X0 c1P3 h1X3 H1P3.a c1P2 H1P2.a m1P d1Y1 n1X2 g1P3.a H1P1.v n1X3 d1Y2 g1P2.a c1Q1 H1P0.v c1Q0 g1P1.a m1Q g1Q0.a c1Q2 d1Y3 g1Q2.a g1P0.v h1Y0 z1P c1Q3 h1Y1 c1P1 g1Q1.v w1P0 h1Y2 w1P2 g1Q3.a e1P0.a z1Q n1Y2 w1P1 w1P3 w1Q2 n1Y0 n1Y1 e1P2.v w1Q1 w1Q3 m1R e1Q1.v e1Q3.v e1P1.a w1Q0 e1Q0.v e1P3.a c1R1 t1P e1Q2.a t1Q c1R3 c1R0 g1R0.v c1R2 qv g1R1.a p2X r2X1 F2P2 F2P1 g1R3.a g1R2.a r2X0 W2P1.a z1R W2P2.a F2P0 r2X2 w1R2 a2X1 w1R1 r2X3 w1R0 e1R1.a a2X2 e1R2.v w1R3 a2X3 F2P3 e1R3.v b2X0.v e1R0.a F2Q1 t1R W2P0.a p2Y b2X1 W2P3.a F2Q2 F2Q3 b2X2 F2R2 r2Y0 r2Y1 r2Y2 b2X3 F2R1 a2Y1 d2X0.v r2Y3 F2Q0 a2Y2 xq2 W2Q2.a W2Q1.a d2X1 a2Y3 xs2 d2X2 F2R0 b2Y0.v d2X3 F2R3 b2Y1 W2Q3.a W2R2.a h2X0 W2R1.a W2R3.a W2R0.a G2P1 W2Q0.a G2P2 H2P1.a b2Y2 G2P0 h2X1 c2P2 G2P3 b2Y3 h2X2 c2P1 c2P0 d2Y0.v n2X1 H2P2.a n2X0 n2X2 d2Y1 c2Q2 H2P0.a m2P h2X3 d2Y2 H2P3.v g2P2.a n2X3 g2P1.a c2Q0 d2Y3 m2Q g2P0.v c2P3 g2P3.a g2Q2.a h2Y0 c2Q1 z2P h2Y1 w2P0 w2P2 g2Q3.a g2Q1.a g2Q0.a n2Y0 w2P1 h2Y2 w2P3 n2Y1 e2P0.v n2Y2 c2Q3 e2P2.v m2R c2R0 z2Q w2Q1 w2Q2 g2R2.v e2P1.a w2Q0 w2Q3 g2R0.v e2P3.a c2R1 e2Q2.v g2R1.a c2R3 e2Q3.v c2R2 g2R3.a z2R t2P e2Q0.a w2R3 e2Q1.a w2R0 w2R2 t2Q y3Q e2R3.v s3Q.v w2R1 y3P OP.s e2R1.v OQ.s ol.a e2R0.a od.g YQ.s s3P.v YP.s e2R2.a t2R os0.s os3.a os1.a y3R os2.s OR.s s3R.v YR.s"
+ORDER = "fe fz ipi pmi iit pmr fpad fvs jm l3 ci m4.a ily lb pf la l84.a km cr.a m16.v cb.a MGX.v iem ty qe3 qe2 ilt tb w28.a lo qe0 qe1 ijvX wb v0X wc uo ict m64.a qu S1X3 jqX.a MGY.v S1X1 S1X2 BTX.a C2Y.a ijvY pk ly C1X.a o1X0 C3X.a qX F0P0 C2X.a ihn o1X2 ps.a p0X v0Y u1X1 F0P1 BTY.a rcn.a qY F0R0 p0Y u1X2 C1Y.a r0X1 F0P2 F0R2 S1Y2 r0X0 xq0 xs0 W0P0.a S1Y1 u1X3 r0X3 jqY.a a0X1 o1Y0 u2X0.a S2X1 S2X3 S2X2 F0P3 r0X2 o1Y2 F0R1 r0Y0 W0R0.a r0Y1 o2X2 W0P3.a F0R3 a0X2 u1Y1 u2X1 a0X3 u1Y2 u2X2 a0Y1 S2Y1 W0R2.a W0P1.a F0Q0 u2X3 b0X0.a S2Y2 b0X1 F0Q2 S2Y3 u2Y0.a W0R3.a S3X1 S3X3 S3X2 b0X2 r0Y2 o3X2 W0R1.a o2Y2 b0X3 u3X0.a u3X1 u2Y1 W0P2.a a0Y2 C3Y.a F0Q1 d0X0.a W0Q1.a u3X2 u2Y2 d0X1 u3X3 u2Y3 d0X2 b0Y0.a m1.a G0P3 G0P2 S4X0 H0P2.a c0Q2 W0Q2.a G0P0 W0Q0.a S4X3 u3Y0.a H0P3.a F0Q3 S4X1 c0P2 S4X2 b0Y1 d0X3 o4X0 H0P0.a S3Y3 b0Y2 S3Y1 S3Y2 h0X0 W0Q3.a G0P1 b0Y3 c0P3 o3Y2 h0X1 n0X0 u3Y1 n0X1 h0X2 c0P1 u3Y2 d0Y0.a d0Y1 H0P1.a m0P g0P0.a h0X3 u3Y3 d0Y2 n0X2 c0Q0 n0X3 S4Y2 g0P1.a S4Y3 S4Y1 g0P2.a S4Y0 m0Q g0Q1.a c0Q3 c0Q1 c0P0 g0P3.v d0Y3 o4Y0 g0Q2.a g0Q0.a z0P w0P0 h0Y0 e0P0.a w0P1 e0P1.a g0Q3.v w0P3 h0Y1 z0Q e0P3.a h0Y2 w0P2 e0P2.v n0Y0 h0Y3 w0Q2 w0Q3 w0Q0 e0Q2.a n0Y1 e0Q3.v w0Q1 n0Y2 e0Q1.v e0Q0.a c0R2 m0R g0R2.a t0P F1P1 t0Q g0R1.a p1X g0R0.v g0R3.v c0R1 r1X0 F1P2 W1P2.a r1X1 c0R3 r1X2 c0R0 F1P0 z0R w0R0 a1X1 w0R2 r1X3 W1P0.v a1X2 w0R3 e0R0.a e0R3.a qv a1X3 w0R1 e0R1.v F1P3 b1X0.v b1X1 e0R2.a t0R p1Y b1X2 b1X3 F1R0 W1P1.a F1Q1 r1Y1 xq1 xs1 W1P3.a r1Y0 W1Q1.a d1X0.v r1Y2 a1Y1 F1Q2 d1X1 a1Y2 d1X2 F1Q0 W1Q2.a b1Y0.v d1X3 b1Y1 h1X0 c1P3 b1Y2 F1R2 W1R0.a h1X1 b1Y3 F1R1 F1R3 W1Q0.a n1X0 W1R2.a n1X1 F1Q3 W1R1.a W1Q3.a c1P1 d1Y0.v h1X2 m1P W1R3.a G1P3 H1P3.a G1P1 H1P1.a c1P0 G1P2 d1Y1 G1P0 h1X3 n1X2 d1Y2 n1X3 H1P2.v d1Y3 H1P0.a g1P3.a m1Q g1P1.a c1Q3 g1P0.a g1P2.v h1Y0 z1P w1P3 g1Q1.a g1Q3.a w1P0 c1P2 h1Y1 w1P2 g1Q2.v c1Q2 c1Q1 c1Q0 h1Y2 n1Y0 w1P1 g1Q0.a z1Q w1Q3 w1Q2 e1P3.a h1Y3 w1Q0 w1Q1 e1P0.v c1R0 e1P2.a n1Y1 n1Y2 e1Q3.v e1P1.a m1R e1Q0.v e1Q2.a t1P e1Q1.a F2P1 g1R0.v t1Q g1R2.a g1R1.a F2P2 g1R3.v W2P1.a W2P2.v z1R c1R3 p2X r2X0 r2X1 c1R2 F2Q0 F2Q1 c1R1 w1R3 a2X1 r2X3 r2X2 w1R1 e1R1.v w1R0 w1R2 W2Q1.a a2X2 e1R2.v a2X3 e1R3.a e1R0.a t1R xq2 F2P0 b2X0.v p2Y W2P0.a b2X1 F2P3 F2R2 F2R0 W2Q0.a r2Y0 W2R2.a W2R0.a F2R3 xs2 r2Y1 W2P3.a F2R1 F2Q2 W2Q2.a b2X2 r2Y2 a2Y1 b2X3 a2Y2 d2X0.v W2R1.a b2Y0.v d2X1 b2Y1 d2X2 F2Q3 c2P3 W2Q3.a W2R3.a b2Y2 G2P0 d2X3 b2Y3 d2Y0.a H2P0.a h2X0 G2P3 h2X1 G2P1 H2P1.a G2P2 H2P2.a n2X0 H2P3.a d2Y1 n2X1 c2P0 h2X2 d2Y2 m2P h2X3 d2Y3 n2X3 c2Q1 c2P1 n2X2 g2P1.a h2Y0 c2Q2 c2Q0 g2P0.a g2P2.v g2P3.a m2Q g2Q0.a h2Y1 g2Q1.a z2P g2Q2.a h2Y2 g2Q3.v h2Y3 c2P2 n2Y0 w2P1 w2P3 e2P3.a n2Y1 w2P2 e2P1.a w2P0 n2Y2 z2Q w2Q1 c2R1 e2P2.a m2R g2R0.a w2Q0 g2R2.a c2Q3 w2Q2 e2P0.v c2R2 c2R0 g2R1.v g2R3.v t2P z2R e2Q0.a w2Q3 e2Q2.v oy.v e2Q1.a e2Q3.a y3P s3P.v c2R3 w2R1 t2Q OP.s w2R3 e2R3.v w2R2 e2R1.a w2R0 e2R0.v YP.s OQ.s y3Q s3Q.v YQ.s e2R2.a t2R ol.a y3R os3.a OR.s os1.a os2.s s3R.v od.s os0.s YR.s"
 
 
 def _clash(a, b):
@@ -174,7 +176,7 @@ def rank_program(g, core, T, topo):
     def whole(name):
         return (name, 0, SCRATCH[name][1][1])
 
-    C1, C2, C3, LA, LB, KS, CI, CR, M1, M4, M16, CB = range(12)
+    C1, LA, LB, CI, CR, M1, M4, M16, CB, M64, L3, L84, MG = [0] + list(range(6, 18))
 
     def seg(side, level, h):
         return SEG * (6 * side + 2 * (level - 1) + HALF[h][2])
@@ -185,53 +187,56 @@ def rank_program(g, core, T, topo):
     def level_step(side, level, h, k, eng):
         _, nb, num, _ = HALF[h]
         d = seg(side, level, h)
-        lo = d + 1 + Q * k
+        n = Q if level == 1 else 16 * nb
+        lo = d + 1 + n * k
         name, oc = "o%d" % level, 12 * num + 4 * (k - 1)
         if level == 1:
-            n = 16 * nb if side == 0 else Q
-            gather_max(T.lv[:, lo:lo + n], T.lv[:, d:lo], T[name][:, oc:oc + n // 16], T.lv[:, lo:lo + n],
+            gather_max(T.lv[:, lo:lo + n], T.lv[:, d:lo], T[name][:, oc:oc + 4], T.lv[:, lo:lo + n],
                        [("lv", d, lo + n), (name, oc, oc + 4)], [("lv", lo, lo + n)])
             return
         s = seg(side, level - 1, h)
-        own, src = T.lv[:, s + 1 + k:s + 257:4], ("lv", s, s + 257)
+        own, src = T.lv[:, s + 1 + k:s + 1 + 4 * n:4], ("lv", s, s + 257)
         if k == 0:
-            move(T.lv[:, lo:lo + Q], own, [src], [("lv", lo, lo + Q)], eng)
+            move(T.lv[:, lo:lo + n], own, [src], [("lv", lo, lo + n)], eng)
         else:
-            gather_max(T.lv[:, lo:lo + Q], T.lv[:, d:lo], T[name][:, oc:oc + 4], own,
-                       [src, ("lv", d, lo), (name, oc, oc + 4)], [("lv", lo, lo + Q)])
+            gather_max(T.lv[:, lo:lo + n], T.lv[:, d:lo], T[name][:, oc:oc + nb], own,
+                       [src, ("lv", d, lo), (name, oc, oc + 4)], [("lv", lo, lo + n)])
 
     def last_level(h, k):
-        a = HALF[h][0] + Q * k
-        s = seg(0, 3, h)
-        gather_max(T.rc[:, H + a:H + a + Q], T.rc[:, 0:H + a], T.o4[:, a // 16:a // 16 + 4], T.lv[:, s + 1 + k:s + 257:4],
-                   [("lv", s, s + 257), ("rc", 0, H + a), ("o4", a // 16, a // 16 + 4)], [("rc", H + a, H + a + Q)])
+        a, nb, num, _ = HALF[h]
+        n, s, oc = 16 * nb, seg(0, 3, h), 16 * num + 4 * k
+        a += H + n * k
+        gather_max(T.rc[:, a:a + n], T.rc[:, 0:a], T.o4[:, oc:oc + nb], T.lv[:, s + 1 + k:s + 1 + 4 * n:4],
+                   [("lv", s, s + 257), ("rc", 0, a), ("o4", oc, oc + 4)], [("rc", a, a + n)])
 
     def pick(level, h, k):
-        a, _, num, _ = HALF[h]
-        out = "vs%d" % level
-        o = a + Q * k if level == 4 else 192 * num + Q * (k - 1)
+        _, nb, num, _ = HALF[h]
+        o = 384 * (level - 1) + (256 * num + Q * k if level == 4 else 192 * num + Q * (k - 1))
         s = seg(1, max(level - 1, 1), h)
         if level == 1:
-            src, R = T.lv[:, s + 1 + Q * k:s + 1 + Q * k + Q], ("lv", s + 1 + Q * k, s + 1 + Q * k + Q)
-            op("V", lambda: V.tensor_tensor_scan(T[out][:, o:o + Q], src, T.k1[:], -4 * BIG, ALU.max, ALU.add),
-               [R, whole("k1")], [(out, o, o + Q)])
+            n, src, R = Q, T.lv[:, s + 1 + Q * k:s + 1 + Q * k + Q], ("lv", s + 1 + Q * k, s + 1 + Q * k + Q)
         else:
-            src, R = T.lv[:, s + 1 + k:s + 257:4], ("lv", s, s + 257)
-            op("V", lambda: V.tensor_tensor_scan(T[out][:, o:o + Q], T.km[:], src, col(CB), ALU.mult, ALU.max),
-               [R, whole("km"), creg(CB)], [(out, o, o + Q)])
+            n, src, R = 16 * nb, T.lv[:, s + 1 + k:s + 1 + Q * nb:4], ("lv", s, s + 257)
+        op("V", lambda: V.tensor_tensor_scan(T.vs[:, o:o + n], T.km[:, 0:n], src, col(CB), ALU.mult, ALU.max),
+           [R, whole("km"), creg(CB)], [("vs", o, o + Q)])
 
     def offsets(level, h, part):
         a, nb, num, _ = HALF[h]
-        src, out = "vs%d" % level, "o%d" % level
+        out = "o%d" % level
         if level == 4:
-            ts(T.o4[:, a // 16:a // 16 + 4 * nb], T.vs4[:, a + 15:a + Q * nb:16], col(M1), H + a - BIG, ALU.mult, ALU.add,
-               [(src, a, a + Q * nb), creg(M1)], [(out, a // 16, a // 16 + 4 * nb)])
+            o = 1152 + 256 * num
+            ts(T.o4[:, 16 * num:16 * num + 16], T.vs[:, o + 15:o + 256:16], col(M1), H + a - BIG, ALU.mult, ALU.add,
+               [("vs", o, o + 256), creg(M1)], [(out, 16 * num, 16 * num + 16)])
             return
-        lo, hi = ((0, 1), (1, 3), (0, 3))[part]
-        mul, c = ((C1, C1), (M16, C2), (M4, C3))[level - 1]
-        ts(T[out][:, 12 * num + 4 * lo:12 * num + 4 * hi], T[src][:, 192 * num + Q * lo + 15:192 * num + Q * hi:16],
-           -64.0 if level == 1 else col(mul), col(c), ALU.mult, ALU.add,
-           [(src, 192 * num + Q * lo, 192 * num + Q * hi), creg(c), creg(mul)], [(out, 12 * num + 4 * lo, 12 * num + 4 * hi)])
+        hi = nb - 1 if level == 1 else 3
+        o, c, mul = 384 * (level - 1) + 192 * num, C1 + 3 * num + level - 1, (M64, M16, M4)[level - 1]
+        lo, hi, src, R = 12 * num, 12 * num + 4 * hi, T.vs[:, o + 15:o + Q * hi:16], ("vs", o, o + Q * hi)
+        if part == 0:
+            tt(T.t1[:, lo:hi], src, T.bt[:, lo:hi], ALU.subtract, [R, ("bt", lo, hi)], [("t1", lo, hi)])
+            return
+        if level == 1:
+            src, R = T.t1[:, lo:hi], ("t1", lo, hi)
+        ts(T[out][:, lo:hi], src, col(mul), col(c), ALU.mult, ALU.add, [R, creg(c), creg(mul)], [(out, lo, hi)])
 
     def send(name, wide):
         if rank + 1 >= n_ranks:
@@ -262,8 +267,8 @@ def rank_program(g, core, T, topo):
         if kind == "p":
             mm(pb, "qu", "su", 0, q, s, H + a, H + a + Q * nb, True, True)
         elif kind == "r":
-            lo, n, j = seg(0, 1, h) + 1 + Q * k, 16 * nb, 256 * num + Q * k
-            tt(T.lv[:, lo:lo + n], pv(pb, k, Q * nb, 4), T.jq[:, j:j + n], ALU.min, [bank(pb), ("jq", j, j + n)], [("lv", lo, lo + n)])
+            lo, j = seg(0, 1, h) + 1 + Q * k, 256 * num + Q * k
+            tt(T.lv[:, lo:lo + Q], pv(pb, k, Q * nb, nb), T.jq[:, j:j + Q], ALU.min, [bank(pb), ("jq", j, j + Q)], [("lv", lo, lo + Q)])
         elif kind in "abd":
             level_step(0, 1 + "abd".index(kind), h, k, eng)
         elif kind == "h":
@@ -274,20 +279,20 @@ def rank_program(g, core, T, topo):
                [whole("km"), ("rc", H + a, H + a + Q), creg(CI)], [("rs", a, a + Q)])
 
     def layer_step(kind, t, h, k, eng):
-        a, b, fb, sb = PIECE[h]
+        a, b, sb = (UNPACK if kind in "FW" else PIECE)[h]
         q, s, fw, tn = "q%d" % t, "s%d" % t, "fw%d" % t, "tt%d" % (t + 1)
         w = (H + C) * k
         if kind == "y":
-            mm(sb[3], "qv", "sv", 0, q, s, H + a, H + b, True, True)
+            mm(4 + LAST.index(h), "qv", "sv", 0, q, s, H + a, H + b, True, True)
         elif kind == "s":
-            move(T.yb[:, a:b], pv(sb[3], 0, b - a), [bank(sb[3])], [("yb", a, b)], eng)
+            move(T.yb[:, a:b], pv(4 + LAST.index(h), 0, b - a), [bank(4 + LAST.index(h))], [("yb", a, b)], eng)
         elif kind == "m":
             ts(T.off[:, a // 16:b // 16], T.rs[:, a + 15:b:16], col(CR), BIG + H, ALU.mult, ALU.add,
                [("rs", a, b), creg(CR)], [("off", a // 16, b // 16)])
         elif kind == "F":
-            mm(fb[k], "qe", "se", 128 * k, q, s, H + a, H + b, True, True)
+            mm(sb[k], "qe", "se", 128 * k, q, s, H + a, H + b, True, True)
         elif kind == "W":
-            scaled(T[fw][:, w + H + a:w + H + b], fb[k], b - a, [(fw, w + H + a, w + H + b)], eng)
+            scaled(T[fw][:, w + H + a:w + H + b], sb[k], b - a, [(fw, w + H + a, w + H + b)], eng)
         elif kind == "G":
             if rank > 0:
                 mm(HALO_BANKS[k], "qe", "se", 128 * k, q, s, 0, H, True, True)
@@ -311,21 +316,21 @@ def rank_program(g, core, T, topo):
             quant("q%d" % (t + 1), "s%d" % (t + 1), H + a, H + b, tn, 4 * a)
 
     def dma(eng, out, in_, R, W, grp):
-        q = {"s": S, "a": A, "g": g}[eng]
+        q = {"s": S, "a": A}[eng]
         op(eng.upper(), lambda: q.dma_start(out, in_), R, W, grp)
 
     def store(eng, out, in_, R):
-        dma(eng, out, in_, R, [], "dOl" if eng == "g" else "dOut")
+        dma(eng, out, in_, R, [], "dOut")
 
     for t in range(ROUNDS):
         now[0] = "arr%d" % t
         arrive(t)
     now[0] = "load"
     for i in range(16):
-        dma("sa"[i % 2], T.drep[i::16, 0:C], T.dist[:], [], [("drep", 0, C)], "dD")
-    dma("a", T.xt[:, 4 * MID:4 * C], T.x[:, 4 * MID:4 * C], [], [("xt", 4 * MID, 4 * C)], "dXL")
+        dma("sa"[i % 2], T.drep[i::16, :], T.dist[:], [], [("drep", 0, C)], "dD")
     dma("a", T.ut[:], T.u[:], [], [("ut", 0, 512)], "dU")
     dma("s", T.xt[:, 0:4 * MID], T.x[:, 0:4 * MID], [], [("xt", 0, 4 * MID)], "dXF")
+    dma("a", T.xt[:, 4 * MID:4 * C], T.x[:, 4 * MID:4 * C], [], [("xt", 4 * MID, 4 * C)], "dXL")
     dma("s", T.qw[:].bitcast(dt.uint8), T.wc[:], [], [("qw", 0, 512)], "dW")
     dma("s", T.sw[:], T.ws[:], [], [("sw", 0, 512)], "dW")
     dma("s", T.vt[:], T.v[:], [], [("vt", 0, 512)], "dV")
@@ -333,42 +338,43 @@ def rank_program(g, core, T, topo):
     qn, sn = "q%d" % ROUNDS, "s%d" % ROUNDS
     pi_, pr_ = T.pm[:, 0:1], T.pm[:, 1:2]
     ireg, rreg = ("pm", 0, 1), ("pm", 1, 2)
-    ray = seg(0, 1, "Y") + 1
     once = {
         "ipi": lambda e: iota("pi", [[0, 1]], 0, 1, False),
-        "ilt": lambda e: iota("lt", [[16, 2], [28, 4], [4, 4]], 0, 0),
-        "ijv": lambda e: iota("jv", [[1, 4], [4, Q]], int(BIG), 0),
+        "ilt": lambda e: iota("lt", [[28, 4], [4, 4]], 0, 0),
+        "ily": lambda e: iota("ly", [[1, 3], [48, 4]], MID, 0),
         "iit": lambda e: iota("it", [[2, 64]], 256, -2, False),
-        "icc": lambda e: iota("cc", [[255, 4], [0, 16]], int(4 * BIG), 0),
+        "ict": lambda e: iota("ct", [[0, 3], [1, 4]], 0, 0),
         "ihn": lambda e: iota("hn", [[1, H]], -H - int(BIG), 0),
         "fpad": lambda e: fill("lv", 0, 12 * SEG, -2 * BIG, SEG),
-        "fray": lambda e: fill("lv", ray, ray + 256, -1.0),
-        "fd": lambda e: fill("drep", C, C + 8, 1),
-        "fe": lambda e: fill("e64", 0, 520, 64.0),
-        "iem": lambda e: op("G", lambda: g.affine_select(T.em[:], T.e64[:], [[1, 520]], ALU.is_equal, 0.0, -3, -4), [whole("e64")], [whole("em")]),
+        "fvs": lambda e: fill("vs", 63, 1664, 0.0, Q),
+        "fe": lambda e: fill("e64", 0, 128, 64.0),
+        "fz": lambda e: fill("em", 0, 520, 0.0),
+        "iem": lambda e: op("G", lambda: g.affine_select(T.em[:, 3:515:4], T.e64[:], [[1, 128]], ALU.is_equal, 0.0, 0, -1), [whole("e64")], [whole("em")]),
         "pmi": lambda e: ts(pi_, T.pi[:], 15, None, ALU.bitwise_and, None, [whole("pi")], [ireg]),
         "pmr": lambda e: ts(pr_, T.pi[:], 3, None, ALU.bitwise_and, None, [whole("pi")], [rreg]),
+        "pf": lambda e: move(T.pf[:], T.pm[:], [whole("pm")], [whole("pf")], "v"),
         "la": lambda e: ts(col(LA), pi_, 0.25, None, ALU.mult, None, [ireg], [creg(LA)]),
         "lb": lambda e: ts(col(LB), pr_, 111.75, None, ALU.mult, None, [rreg], [creg(LB)]),
-        "lo": lambda e: ts(T.lo[:], T.lt[:], col(LA), col(LB), ALU.add, ALU.add, [whole("lt"), creg(LA, 2)], [whole("lo")]),
-        "c2": lambda e: ts(col(C2), pi_, -255.0, 1 - 16 * BIG, ALU.mult, ALU.add, [ireg], [creg(C2)]),
-        "c3": lambda e: ts(col(C3), pr_, -255.0, 1 - 4 * BIG, ALU.mult, ALU.add, [rreg], [creg(C3)]),
-        "ks": lambda e: ts(col(KS), pi_, 0.0, -128 * BIG, ALU.is_equal, ALU.mult, [ireg], [creg(KS)]),
-        "c1": lambda e: ts(col(C1), col(C2), 16 * BIG, col(KS), ALU.add, ALU.add, [creg(C2), creg(KS)], [creg(C1)]),
+        "lo": lambda e: ts(T.lo[:, 0:16], T.lt[:], col(LA), col(LB), ALU.add, ALU.add, [whole("lt"), creg(LA, 2)], [("lo", 0, 16)]),
+        "l3": lambda e: ts(col(L3), pi_, 3.0, None, ALU.mult, None, [ireg], [creg(L3)]),
+        "l84": lambda e: affine(col(L84), T.pf[:, 0:1], 84.0, 0.0, [whole("pf")], [creg(L84)], e),
+        "ty": lambda e: ts(T.ty[:], T.ly[:], col(L3), None, ALU.add, None, [whole("ly"), creg(L3)], [whole("ty")]),
+        "tb": lambda e: ts(T.tb[:], T.ty[:], 4, None, ALU.arith_shift_right, None, [whole("ty")], [whole("tb")]),
+        "w28": lambda e: affine(T.w28[:], T.ly[:], 28.0, col(L84), [whole("ly"), creg(L84)], [whole("w28")], e),
+        "wb": lambda e: ts(T.wb[:], T.tb[:], -447.0, None, ALU.mult, None, [whole("tb")], [whole("wb")]),
+        "wc": lambda e: tt(T.wc2[:], T.wb[:], T.w28[:], ALU.add, [whole("wb"), whole("w28")], [whole("wc2")]),
+        "ly": lambda e: move(T.lo[:, 16:28], T.wc2[:], [whole("wc2")], [("lo", 16, 28)], "v"),
         "ci": lambda e: ts(col(CI), pi_, 15.0, 0.5, ALU.is_lt, ALU.subtract, [ireg], [creg(CI)]),
         "cr": lambda e: affine(col(CR), col(CI), -2.0 / TINY, 0.0, [creg(CI)], [creg(CR)], e),
         "m1": lambda e: affine(col(M1), col(CI), 2.0, 0.0, [creg(CI)], [creg(M1)], e),
         "m4": lambda e: affine(col(M4), col(CI), 8.0, 0.0, [creg(CI)], [creg(M4)], e),
         "m16": lambda e: affine(col(M16), col(CI), 32.0, 0.0, [creg(CI)], [creg(M16)], e),
+        "m64": lambda e: affine(col(M64), col(CI), 128.0, 0.0, [creg(CI)], [creg(M64)], e),
         "cb": lambda e: affine(col(CB), col(CI), 4 * BIG, 0.0, [creg(CI)], [creg(CB)], e),
         "jm": lambda e: ts(T.jm[:], T.it[:], 31, None, ALU.bitwise_and, None, [whole("it")], [whole("jm")]),
         "km": lambda e: ts(T.km[:], T.jm[:], -3.0, 1.0, ALU.add, ALU.min, [whole("jm")], [whole("km")]),
-        "sel": lambda e: ts(T.sel[:], T.jm[:], 0.0, 0.25, ALU.is_equal, ALU.mult, [whole("jm")], [whole("sel")]),
-        "pre": lambda e: ts(T.pre[:], T.jm[:], 30.0, -2 * BIG, ALU.is_equal, ALU.mult, [whole("jm")], [whole("pre")]),
-        "ka": lambda e: tt(T.ka[:], T.sel[:], T.cc[:], ALU.mult, [whole("sel"), whole("cc")], [whole("ka")]),
-        "k1": lambda e: tt(T.k1[:], T.ka[:], T.pre[:], ALU.add, [whole("ka"), whole("pre")], [whole("k1")]),
         "rcn": lambda e: affine(T.rc[:, 0:H], T.hn[:], TINY, 0.0, [whole("hn")], [("rc", 0, H)], e),
-        "uo": lambda e: ts(T.uo[:], T.jv[:, 0:32:4], BIG, None, ALU.subtract, None, [("jv", 0, 32)], [whole("uo")]),
+        "uo": lambda e: ts(T.uo[:], T.jvX[:, 0:32:4], BIG, None, ALU.subtract, None, [("jvX", 0, 32)], [whole("uo")]),
         "qu": lambda e: quant("qu0", "su0", 0, 128, "ut", 0),
         "pk": lambda e: op("V", lambda: V.tensor_copy(T.qu[:].bitcast(dt.uint32), T.qu0[:].bitcast(dt.uint32).indirect(T.uo[:])),
                            [whole("qu0"), whole("uo")], [whole("qu")]),
@@ -376,30 +382,37 @@ def rank_program(g, core, T, topo):
         "qY": lambda e: quant("q0", "s0", H + MID, H + C, "xt", 4 * MID),
         "qX": lambda e: quant("q0", "s0", H, H + MID, "xt", 0),
         "qv": lambda e: quant("qv", "sv", 0, 128, "vt", 0),
-        "ol": lambda e: affine(T.olb[:], T.rc[:, H:H + C], 1.0 / TINY, BIG, [("rc", H, H + C)], [whole("olb")], e),
+        "ol": lambda e: affine(T.olb[:, 0:MID], T.rc[:, H:H + MID], 1.0 / TINY, BIG, [("rc", H, H + MID)], [("olb", 0, MID)], e),
+        "oy": lambda e: affine(T.olb[:, MID:C], T.rc[:, H + MID:H + C], 1.0 / TINY, BIG, [("rc", H + MID, H + C)], [("olb", MID, C)], e),
         "od": lambda e: store(e, T.ol[:], T.olb[0::16, :], [whole("olb")]),
     }
     for k in range(4):
         once["qe%d" % k] = lambda e, k=k: quant("qe", "se", 128 * k, 128 * k + 128, "em", 3 - k)
         once["os%d" % k] = lambda e, k=k: store(e, T.osc[4 * k:4 * k + 4, :], T[sn][32 * k:32 * k + 4, H:H + C], [(sn, H, H + C)])
     for h, (a, nb, num, _) in HALF.items():
-        va = seg(1, 1, h) + 1
-        once["jq" + h] = lambda e, a=a, num=num: affine(T.jq[:, 256 * num:256 * num + 256], T.jv[:], TINY, (a - 2 * BIG) * TINY,
-                                                        [whole("jv")], [("jq", 256 * num, 256 * num + 256)], e)
-        once["v0" + h] = lambda e, va=va, num=num: tt(T.lv[:, va:va + 256], T.drep[:].indirect(T.lo[:, 16 * num:16 * num + 16]), T.jv[:], ALU.subtract,
-                                                      [whole("drep"), ("lo", 16 * num, 16 * num + 16), whole("jv")], [("lv", va, va + 256)])
+        va, n, jv = seg(1, 1, h) + 1, Q * nb, "jv" + h
+        once["i" + jv] = lambda e, jv=jv, nb=nb: iota(jv, [[1, nb], [nb, Q]], int(BIG), 0)
+        once["MG" + h] = lambda e, n=n, num=num: affine(col(MG + num), col(CI), (n - 1) / 2, 0.0, [creg(CI)], [creg(MG + num)], e)
+        once["BT" + h] = lambda e, num=num: affine(T.bt[:, 12 * num:12 * num + 12], T.ct[:], col(MG + num), 0.0,
+                                                   [whole("ct"), creg(MG + num)], [("bt", 12 * num, 12 * num + 12)], e)
+        for level, (src, add) in enumerate(((0, 64), (0, 16), (1, 4))):
+            once["C%d%s" % (level + 1, h)] = lambda e, c=C1 + 3 * num + level, n=n, src=src, add=add: affine(
+                col(c), T.pf[:, src:src + 1], 1.0 - n, 1 - add * BIG, [whole("pf")], [creg(c)], e)
+        once["jq" + h] = lambda e, a=a, num=num, n=n, jv=jv: affine(T.jq[:, 256 * num:256 * num + n], T[jv][:], TINY, (a - 2 * BIG) * TINY,
+                                                                    [whole(jv)], [("jq", 256 * num, 256 * num + n)], e)
+        once["v0" + h] = lambda e, va=va, num=num, n=n, jv=jv: tt(
+            T.lv[:, va:va + n], T.drep[:].indirect(T.lo[:, 16 * num:16 * num + n // 16]), T[jv][:], ALU.subtract,
+            [whole("drep"), ("lo", 16 * num, 16 * num + 16), whole(jv)], [("lv", va, va + n)])
         for level in (1, 2, 3, 4):
-            for k in (range(nb) if level == 4 else range(1, 4)):
+            for k in range(4):
                 once["S%d%s%d" % (level, h, k)] = lambda e, level=level, h=h, k=k: pick(level, h, k)
-            for part in range(1 if level == 4 else 3):
-                once["o%d%s%d" % (level, h, part)] = lambda e, level=level, h=h, part=part: offsets(level, h, part)
-            if level < 4:
-                for k in range(4):
-                    once["u%d%s%d" % (level, h, k)] = lambda e, level=level, h=h, k=k: level_step(1, level, h, k, e)
+                once["o%d%s%d" % (level, h, k)] = lambda e, level=level, h=h, k=k: offsets(level, h, k)
+                once["u%d%s%d" % (level, h, k)] = lambda e, level=level, h=h, k=k: level_step(1, level, h, k, e)
     for t in range(ROUNDS):
         once["xq%d" % t] = lambda e, t=t: send("q%d" % t, True)
         once["xs%d" % t] = lambda e, t=t: send("s%d" % t, False)
-    for h, (a, b, _, _) in PIECE.items():
+    for h in LAST:
+        a, b, _ = PIECE[h]
         once["O" + h] = lambda e, a=a, b=b: store(e, T.oc[:, 4 * a:4 * b], T[qn][:, H + a:H + b].bitcast(dt.uint8), [(qn, H + a, H + b)])
         once["Y" + h] = lambda e, a=a, b=b: store(e, T.y[:, a:b], T.yb[:, a:b], [("yb", a, b)])
 
@@ -413,4 +426,4 @@ def rank_program(g, core, T, topo):
         else:
             layer_step(name[0], int(name[1]), name[2], int(name[3:] or 0), eng)
 
-    _emit(g, T, ops, ["sent", "dOl", "dOut"])
+    _emit(g, T, ops, ["sent", "dOut"])

from concourse.mybir import dt, AluOpType, ActivationFunctionType

C, H, ROUNDS = 448, 128, 3
Q = 64
SEG = 264
BIG = 1024.0
TINY = 2.0 ** -98
BANK = 512
X4, U8, F32, BF, I32, U16 = "float8_e4m3fn_x4", "uint8", "float32", "bfloat16", "int32", "uint16"

SCRATCH = {"ps": ("psum", [128, 8 * BANK], F32)}
for _ty, _bufs in (
        (I32, {"drep": C, "ty": 12, "tb": 12, "pi": 1, "pm": 2, "it": 64, "jm": 64}),
        (BF, {"xt": 4 * C, "ut": 512, "vt": 512, "e64": 128, "em": 520, "zt": 4 * C, "tt1": 4 * C,
              "tt2": 4 * C, "tt3": 4 * C, "fw0": 4 * (H + C), "fw1": 4 * (H + C), "fw2": 4 * (H + C)}),
        (X4, {"qu0": 128, "qu": 128, "qv": 128, "qw": 512, "qe": 512, "qz": C, "q0": C + H, "q1": C + H, "q2": C + H, "q3": C + H}),
        (U8, {"su0": 128, "su": 128, "sv": 128, "sw": 512, "se": 512, "sz": C, "s0": C + H, "s1": C + H, "s2": C + H, "s3": C + H}),
        (U16, {"o1": 24, "o2": 24, "o3": 24, "o4": 32, "off": 28, "lo": 32, "uo": 8}),
        (F32, {"lv": 12 * SEG, "rc": H + C, "rs": C, "vs": 1664, "w28": 12, "wb": 12, "wc2": 12,
               "jvX": 256, "jvY": 192, "jq": 512, "lt": 16, "ly": 12, "pf": 2, "ct": 12, "bt": 24, "t1": 24,
               "km": 64, "hn": H, "col": 24, "olb": C, "yb": C})):
    for _name, _n in _bufs.items():
        SCRATCH[_name] = ("sbuf", [128, _n], _ty)

SEMAPHORES = ["sV", "sA", "sP", "sG", "sent", "arr0", "arr1", "arr2",
              "dD", "dXL", "dXF", "dU", "dV", "dW", "dOut"]

ALU, ACT = AluOpType, ActivationFunctionType

HALF = {"X": (0, 4, 0, 7), "Y": (256, 3, 1, 3)}
PIECE = {"P": (0, 128, (0, 1, 2, 3)), "Q": (128, 256, (4, 5, 6, 7)), "R": (256, C, (0, 1, 2, 3))}
UNPACK = {"P": (0, 128, (4, 5, 6, 4)), "Q": (128, 256, (5, 6, 4, 5)), "R": (256, C, (0, 1, 2, 0))}
HALO_BANKS = (4, 5, 6, 7)
LAST = "PQR"
MID = 256

ORDER = "fe fz ipi pmi iit pmr fpad fvs jm l3 ci m4.a ily lb pf la l84.a km cr.a m16.v cb.a MGX.v iem ty qe3 qe2 ilt tb w28.a lo qe0 qe1 ijvX wb v0X wc uo ict m64.a qu S1X3 jqX.a MGY.v S1X1 S1X2 BTX.a C2Y.a ijvY pk ly C1X.a o1X0 C3X.a qX F0P0 C2X.a ihn o1X2 ps.a p0X v0Y u1X1 F0P1 BTY.a rcn.a qY F0R0 p0Y u1X2 C1Y.a r0X1 F0P2 F0R2 S1Y2 r0X0 xq0 xs0 W0P0.a S1Y1 u1X3 r0X3 jqY.a a0X1 o1Y0 u2X0.a S2X1 S2X3 S2X2 F0P3 r0X2 o1Y2 F0R1 r0Y0 W0R0.a r0Y1 o2X2 W0P3.a F0R3 a0X2 u1Y1 u2X1 a0X3 u1Y2 u2X2 a0Y1 S2Y1 W0R2.a W0P1.a F0Q0 u2X3 b0X0.a S2Y2 b0X1 F0Q2 S2Y3 u2Y0.a W0R3.a S3X1 S3X3 S3X2 b0X2 r0Y2 o3X2 W0R1.a o2Y2 b0X3 u3X0.a u3X1 u2Y1 W0P2.a a0Y2 C3Y.a F0Q1 d0X0.a W0Q1.a u3X2 u2Y2 d0X1 u3X3 u2Y3 d0X2 b0Y0.a m1.a G0P3 G0P2 S4X0 H0P2.a c0Q2 W0Q2.a G0P0 W0Q0.a S4X3 u3Y0.a H0P3.a F0Q3 S4X1 c0P2 S4X2 b0Y1 d0X3 o4X0 H0P0.a S3Y3 b0Y2 S3Y1 S3Y2 h0X0 W0Q3.a G0P1 b0Y3 c0P3 o3Y2 h0X1 n0X0 u3Y1 n0X1 h0X2 c0P1 u3Y2 d0Y0.a d0Y1 H0P1.a m0P g0P0.a h0X3 u3Y3 d0Y2 n0X2 c0Q0 n0X3 S4Y2 g0P1.a S4Y3 S4Y1 g0P2.a S4Y0 m0Q g0Q1.a c0Q3 c0Q1 c0P0 g0P3.v d0Y3 o4Y0 g0Q2.a g0Q0.a z0P w0P0 h0Y0 e0P0.a w0P1 e0P1.a g0Q3.v w0P3 h0Y1 z0Q e0P3.a h0Y2 w0P2 e0P2.v n0Y0 h0Y3 w0Q2 w0Q3 w0Q0 e0Q2.a n0Y1 e0Q3.v w0Q1 n0Y2 e0Q1.v e0Q0.a c0R2 m0R g0R2.a t0P F1P1 t0Q g0R1.a p1X g0R0.v g0R3.v c0R1 r1X0 F1P2 W1P2.a r1X1 c0R3 r1X2 c0R0 F1P0 z0R w0R0 a1X1 w0R2 r1X3 W1P0.v a1X2 w0R3 e0R0.a e0R3.a qv a1X3 w0R1 e0R1.v F1P3 b1X0.v b1X1 e0R2.a t0R p1Y b1X2 b1X3 F1R0 W1P1.a F1Q1 r1Y1 xq1 xs1 W1P3.a r1Y0 W1Q1.a d1X0.v r1Y2 a1Y1 F1Q2 d1X1 a1Y2 d1X2 F1Q0 W1Q2.a b1Y0.v d1X3 b1Y1 h1X0 c1P3 b1Y2 F1R2 W1R0.a h1X1 b1Y3 F1R1 F1R3 W1Q0.a n1X0 W1R2.a n1X1 F1Q3 W1R1.a W1Q3.a c1P1 d1Y0.v h1X2 m1P W1R3.a G1P3 H1P3.a G1P1 H1P1.a c1P0 G1P2 d1Y1 G1P0 h1X3 n1X2 d1Y2 n1X3 H1P2.v d1Y3 H1P0.a g1P3.a m1Q g1P1.a c1Q3 g1P0.a g1P2.v h1Y0 z1P w1P3 g1Q1.a g1Q3.a w1P0 c1P2 h1Y1 w1P2 g1Q2.v c1Q2 c1Q1 c1Q0 h1Y2 n1Y0 w1P1 g1Q0.a z1Q w1Q3 w1Q2 e1P3.a h1Y3 w1Q0 w1Q1 e1P0.v c1R0 e1P2.a n1Y1 n1Y2 e1Q3.v e1P1.a m1R e1Q0.v e1Q2.a t1P e1Q1.a F2P1 g1R0.v t1Q g1R2.a g1R1.a F2P2 g1R3.v W2P1.a W2P2.v z1R c1R3 p2X r2X0 r2X1 c1R2 F2Q0 F2Q1 c1R1 w1R3 a2X1 r2X3 r2X2 w1R1 e1R1.v w1R0 w1R2 W2Q1.a a2X2 e1R2.v a2X3 e1R3.a e1R0.a t1R xq2 F2P0 b2X0.v p2Y W2P0.a b2X1 F2P3 F2R2 F2R0 W2Q0.a r2Y0 W2R2.a W2R0.a F2R3 xs2 r2Y1 W2P3.a F2R1 F2Q2 W2Q2.a b2X2 r2Y2 a2Y1 b2X3 a2Y2 d2X0.v W2R1.a b2Y0.v d2X1 b2Y1 d2X2 F2Q3 c2P3 W2Q3.a W2R3.a b2Y2 G2P0 d2X3 b2Y3 d2Y0.a H2P0.a h2X0 G2P3 h2X1 G2P1 H2P1.a G2P2 H2P2.a n2X0 H2P3.a d2Y1 n2X1 c2P0 h2X2 d2Y2 m2P h2X3 d2Y3 n2X3 c2Q1 c2P1 n2X2 g2P1.a h2Y0 c2Q2 c2Q0 g2P0.a g2P2.v g2P3.a m2Q g2Q0.a h2Y1 g2Q1.a z2P g2Q2.a h2Y2 g2Q3.v h2Y3 c2P2 n2Y0 w2P1 w2P3 e2P3.a n2Y1 w2P2 e2P1.a w2P0 n2Y2 z2Q w2Q1 c2R1 e2P2.a m2R g2R0.a w2Q0 g2R2.a c2Q3 w2Q2 e2P0.v c2R2 c2R0 g2R1.v g2R3.v t2P z2R e2Q0.a w2Q3 e2Q2.v oy.v e2Q1.a e2Q3.a y3P s3P.v c2R3 w2R1 t2Q OP.s w2R3 e2R3.v w2R2 e2R1.a w2R0 e2R0.v YP.s OQ.s y3Q s3Q.v YQ.s e2R2.a t2R ol.a y3R os3.a OR.s os1.a os2.s s3R.v od.s os0.s YR.s"


def _clash(a, b):
    return a[0] == b[0] and a[1] < b[2] and b[1] < a[2] and (a[3] is None or b[3] is None or a[3] == b[3])


def _emit(g, T, ops, tail):
    queue = {"V": g.vector, "A": g.scalar, "P": g.tensor, "G": g, "S": g.sync}
    total = {}
    for o in ops:
        if o["grp"]:
            total[o["grp"]] = total.get(o["grp"], 0) + o["inc"]
    known = {k: {} for k in queue}
    seq = {k: 0 for k in queue}
    reads, writes = {}, {}
    for n, o in enumerate(ops):
        e = o["eng"]
        need = {}
        hits = []
        for a in o["R"]:
            hits += [p for p, b in writes.get(a[0], []) if _clash(a, b)]
            if a[0] == "ps":
                hits += [p for p, b in reads.get(a[0], []) if p["eng"] != e and _clash(a, b)]
        for a in o["W"]:
            hits += [p for p, b in writes.get(a[0], []) + reads.get(a[0], []) if _clash(a, b)]
        for p in hits:
            if not (p["grp"] and p["grp"] == o["grp"]) and not (o["chain"] and p["eng"] == e):
                if p["key"] not in need or need[p["key"]]["n"] < p["n"]:
                    need[p["key"]] = p
        o["waits"] = []
        if e is not None:
            for p in sorted(need.values(), key=lambda p: -p["n"]):
                if known[e].get(p["key"], 0) < p["val"]:
                    o["waits"].append(p)
                    p["sig"] = True
                    for k, v in p["after"].items():
                        known[e][k] = max(known[e].get(k, 0), v)
        o["n"] = n
        if o["grp"]:
            o["key"], o["val"] = o["grp"], 1
        else:
            seq[e] += 1
            o["key"], o["val"] = e, seq[e]
        o["after"] = dict(known[e]) if e is not None else {}
        o["after"][o["key"]] = o["val"]
        for a in o["R"]:
            reads.setdefault(a[0], []).append((o, a))
        for a in o["W"]:
            writes.setdefault(a[0], []).append((o, a))
    count = {k: 0 for k in queue}
    waited = {}
    for o in ops:
        e = o["eng"]
        if e is None:
            continue
        for p in o["waits"]:
            name, val = (p["grp"], total[p["grp"]]) if p["grp"] else ("s" + p["eng"], p["count"])
            queue[e].wait_ge(T.sem[name], val)
            waited[name] = max(waited.get(name, 0), val)
        ins = o["fn"]()
        if o["grp"]:
            if o["dma"]:
                ins.then_inc(T.sem[o["grp"]], 16)
        elif o.get("sig"):
            count[e] += 1
            o["count"] = count[e]
            ins.then_inc(T.sem["s" + e], 1)
    for name in tail:
        if waited.get(name, 0) < total.get(name, 0):
            g.wait_ge(T.sem[name], total[name])


def rank_program(g, core, T, topo):
    rank = T.rank_of(core)
    if rank is None:
        return
    n_ranks = len(T.cores)
    ops = []
    now = [None]
    V, A, P, S = g.vector, g.scalar, g.tensor, g.sync

    def reg(xs):
        return [(x[0], x[1], x[2], x[3] if len(x) > 3 else None) for x in xs]

    def op(eng, fn, R=(), W=(), grp=None, inc=16, dma=True, chain=False):
        ops.append({"eng": eng, "fn": fn, "R": reg(R), "W": reg(W), "grp": grp, "inc": inc, "dma": dma, "chain": chain, "word": now[0]})

    def bank(k):
        return ("ps", BANK * k, BANK * k + BANK)

    def pv(k, a, b, step=1):
        return T.ps[:, BANK * k + a:BANK * k + b:step]

    def ts(out, in0, s1, s2, op0, op1, R, W):
        if s2 is None:
            op("V", lambda: V.tensor_scalar(out, in0, s1, None, op0), R, W)
        else:
            op("V", lambda: V.tensor_scalar(out, in0, s1, s2, op0, op1), R, W)

    def tt(out, in0, in1, alu, R, W):
        op("V", lambda: V.tensor_tensor(out, in0, in1, alu), R, W)

    def move(out, in_, R, W, eng):
        if eng == "v":
            op("V", lambda: V.tensor_copy(out, in_), R, W)
        else:
            op("A", lambda: A.activation(out, in_, ACT.Copy), R, W)

    def affine(out, in_, mul, add, R, W, eng):
        if eng == "v":
            ts(out, in_, mul, add, ALU.mult, ALU.add, R, W)
        else:
            op("A", lambda: A.activation(out, in_, ACT.Identity, bias=add, scale=mul), R, W)

    def fill(name, a, b, val, step=1):
        op("V", lambda: V.memset(T[name][:, a:b:step], val), [], [(name, a, b)])

    def iota(name, pattern, base, cm, real=True):
        if real:
            op("G", lambda: g.iota(T[name][:], pattern, base, cm, allow_small_or_imprecise_dtypes=True), [], [whole(name)])
        else:
            op("G", lambda: g.iota(T[name][:], pattern, base, cm), [], [whole(name)])

    def quant(q, s, a, b, src, c0):
        op("V", lambda: V.quantize_mx(T[q][:, a:b], T[s][:, a:b], T[src][:, c0:c0 + 4 * (b - a)]),
           [(src, c0, c0 + 4 * (b - a))], [(q, a, b), (s, a, b)])

    def mm(k, wq, ws, wa, q, s, a, b, start, stop):
        op("P", lambda: P.matmul_mx(T.ps[:, BANK * k:BANK * k + b - a], T[wq][:, wa:wa + 128], T[ws][:, wa:wa + 128],
                                    T[q][:, a:b], T[s][:, a:b], start, stop),
           [(wq, wa, wa + 128), (ws, wa, wa + 128), (q, a, b), (s, a, b)], [bank(k)], chain=not start)

    def col(k, n=1):
        return T.col[:, k:k + n]

    def creg(k, n=1):
        return ("col", k, k + n)

    def whole(name):
        return (name, 0, SCRATCH[name][1][1])

    C1, LA, LB, CI, CR, M1, M4, M16, CB, M64, L3, L84, MG = [0] + list(range(6, 18))

    def seg(side, level, h):
        return SEG * (6 * side + 2 * (level - 1) + HALF[h][2])

    def gather_max(out, win, offs, in1, R, W):
        tt(out, win.indirect(offs), in1, ALU.max, R, W)

    def level_step(side, level, h, k, eng):
        _, nb, num, _ = HALF[h]
        d = seg(side, level, h)
        n = Q if level == 1 else 16 * nb
        lo = d + 1 + n * k
        name, oc = "o%d" % level, 12 * num + 4 * (k - 1)
        if level == 1:
            gather_max(T.lv[:, lo:lo + n], T.lv[:, d:lo], T[name][:, oc:oc + 4], T.lv[:, lo:lo + n],
                       [("lv", d, lo + n), (name, oc, oc + 4)], [("lv", lo, lo + n)])
            return
        s = seg(side, level - 1, h)
        own, src = T.lv[:, s + 1 + k:s + 1 + 4 * n:4], ("lv", s, s + 257)
        if k == 0:
            move(T.lv[:, lo:lo + n], own, [src], [("lv", lo, lo + n)], eng)
        else:
            gather_max(T.lv[:, lo:lo + n], T.lv[:, d:lo], T[name][:, oc:oc + nb], own,
                       [src, ("lv", d, lo), (name, oc, oc + 4)], [("lv", lo, lo + n)])

    def last_level(h, k):
        a, nb, num, _ = HALF[h]
        n, s, oc = 16 * nb, seg(0, 3, h), 16 * num + 4 * k
        a += H + n * k
        gather_max(T.rc[:, a:a + n], T.rc[:, 0:a], T.o4[:, oc:oc + nb], T.lv[:, s + 1 + k:s + 1 + 4 * n:4],
                   [("lv", s, s + 257), ("rc", 0, a), ("o4", oc, oc + 4)], [("rc", a, a + n)])

    def pick(level, h, k):
        _, nb, num, _ = HALF[h]
        o = 384 * (level - 1) + (256 * num + Q * k if level == 4 else 192 * num + Q * (k - 1))
        s = seg(1, max(level - 1, 1), h)
        if level == 1:
            n, src, R = Q, T.lv[:, s + 1 + Q * k:s + 1 + Q * k + Q], ("lv", s + 1 + Q * k, s + 1 + Q * k + Q)
        else:
            n, src, R = 16 * nb, T.lv[:, s + 1 + k:s + 1 + Q * nb:4], ("lv", s, s + 257)
        op("V", lambda: V.tensor_tensor_scan(T.vs[:, o:o + n], T.km[:, 0:n], src, col(CB), ALU.mult, ALU.max),
           [R, whole("km"), creg(CB)], [("vs", o, o + Q)])

    def offsets(level, h, part):
        a, nb, num, _ = HALF[h]
        out = "o%d" % level
        if level == 4:
            o = 1152 + 256 * num
            ts(T.o4[:, 16 * num:16 * num + 16], T.vs[:, o + 15:o + 256:16], col(M1), H + a - BIG, ALU.mult, ALU.add,
               [("vs", o, o + 256), creg(M1)], [(out, 16 * num, 16 * num + 16)])
            return
        hi = nb - 1 if level == 1 else 3
        o, c, mul = 384 * (level - 1) + 192 * num, C1 + 3 * num + level - 1, (M64, M16, M4)[level - 1]
        lo, hi, src, R = 12 * num, 12 * num + 4 * hi, T.vs[:, o + 15:o + Q * hi:16], ("vs", o, o + Q * hi)
        if part == 0:
            tt(T.t1[:, lo:hi], src, T.bt[:, lo:hi], ALU.subtract, [R, ("bt", lo, hi)], [("t1", lo, hi)])
            return
        if level == 1:
            src, R = T.t1[:, lo:hi], ("t1", lo, hi)
        ts(T[out][:, lo:hi], src, col(mul), col(c), ALU.mult, ALU.add, [R, creg(c), creg(mul)], [(out, lo, hi)])

    def send(name, wide):
        if rank + 1 >= n_ranks:
            return
        dst = T.cores[rank + 1]
        rid, pid = topo.addr(dst, core)
        mask = topo.mask(core, dst)
        out, in_ = T[name][:, 0:H], T[name][:, C:C + H]
        if wide:
            out, in_ = out.bitcast(dt.uint8), in_.bitcast(dt.uint8)
        op("G", lambda: g.remote_dma(out, in_, T.sem["arr" + name[1]], T.sem.sent, pid, rid, mask),
           [(name, C, C + H)], [], "sent", len(topo.engines(core, dst)), False)

    def arrive(t):
        if rank > 0:
            n_eng = len(topo.engines(T.cores[rank - 1], core))
            op(None, None, [], [("q%d" % t, 0, H), ("s%d" % t, 0, H)], "arr%d" % t, 2 * n_eng, False)

    def scaled(out, k, n, W, eng):
        if eng == "v":
            ts(out, pv(k, 0, n), 1.0 / 64, None, ALU.mult, None, [bank(k)], W)
        else:
            op("A", lambda: A.activation(out, pv(k, 0, n), ACT.Copy, scale=1.0 / 64), [bank(k)], W)

    def root_step(kind, t, h, k, eng):
        a, nb, num, pb = HALF[h]
        q, s = "q%d" % t, "s%d" % t
        if kind == "p":
            mm(pb, "qu", "su", 0, q, s, H + a, H + a + Q * nb, True, True)
        elif kind == "r":
            lo, j = seg(0, 1, h) + 1 + Q * k, 256 * num + Q * k
            tt(T.lv[:, lo:lo + Q], pv(pb, k, Q * nb, nb), T.jq[:, j:j + Q], ALU.min, [bank(pb), ("jq", j, j + Q)], [("lv", lo, lo + Q)])
        elif kind in "abd":
            level_step(0, 1 + "abd".index(kind), h, k, eng)
        elif kind == "h":
            last_level(h, k)
        elif kind == "n":
            a += Q * k
            op("V", lambda: V.tensor_tensor_scan(T.rs[:, a:a + Q], T.km[:], T.rc[:, H + a:H + a + Q], col(CI), ALU.mult, ALU.max),
               [whole("km"), ("rc", H + a, H + a + Q), creg(CI)], [("rs", a, a + Q)])

    def layer_step(kind, t, h, k, eng):
        a, b, sb = (UNPACK if kind in "FW" else PIECE)[h]
        q, s, fw, tn = "q%d" % t, "s%d" % t, "fw%d" % t, "tt%d" % (t + 1)
        w = (H + C) * k
        if kind == "y":
            mm(4 + LAST.index(h), "qv", "sv", 0, q, s, H + a, H + b, True, True)
        elif kind == "s":
            move(T.yb[:, a:b], pv(4 + LAST.index(h), 0, b - a), [bank(4 + LAST.index(h))], [("yb", a, b)], eng)
        elif kind == "m":
            ts(T.off[:, a // 16:b // 16], T.rs[:, a + 15:b:16], col(CR), BIG + H, ALU.mult, ALU.add,
               [("rs", a, b), creg(CR)], [("off", a // 16, b // 16)])
        elif kind == "F":
            mm(sb[k], "qe", "se", 128 * k, q, s, H + a, H + b, True, True)
        elif kind == "W":
            scaled(T[fw][:, w + H + a:w + H + b], sb[k], b - a, [(fw, w + H + a, w + H + b)], eng)
        elif kind == "G":
            if rank > 0:
                mm(HALO_BANKS[k], "qe", "se", 128 * k, q, s, 0, H, True, True)
        elif kind == "H":
            if rank > 0:
                scaled(T[fw][:, w:w + H], HALO_BANKS[k], H, [(fw, w, w + H)], eng)
            else:
                affine(T[fw][:, w:w + H], T.e64[:, 0:H], 0.0, 0.0, [("e64", 0, H)], [(fw, w, w + H)], eng)
        elif kind == "c":
            mm(sb[k], "qe", "se", 128 * k, q, s, H + a, H + b, True, False)
        elif kind == "g":
            move(T.zt[:, 4 * a + k:4 * b:4], T[fw][:, w:w + H + b].indirect(T.off[:, a // 16:b // 16]),
                 [(fw, w, w + H + b), ("off", a // 16, b // 16)], [("zt", 4 * a, 4 * b, k)], eng)
        elif kind == "z":
            quant("qz", "sz", a, b, "zt", 4 * a)
        elif kind == "w":
            mm(sb[k], "qw", "sw", 128 * k, "qz", "sz", a, b, False, True)
        elif kind == "e":
            scaled(T[tn][:, 4 * a + k:4 * b:4], sb[k], b - a, [(tn, 4 * a, 4 * b, k)], eng)
        elif kind == "t":
            quant("q%d" % (t + 1), "s%d" % (t + 1), H + a, H + b, tn, 4 * a)

    def dma(eng, out, in_, R, W, grp):
        q = {"s": S, "a": A}[eng]
        op(eng.upper(), lambda: q.dma_start(out, in_), R, W, grp)

    def store(eng, out, in_, R):
        dma(eng, out, in_, R, [], "dOut")

    for t in range(ROUNDS):
        now[0] = "arr%d" % t
        arrive(t)
    now[0] = "load"
    for i in range(16):
        dma("sa"[i % 2], T.drep[i::16, :], T.dist[:], [], [("drep", 0, C)], "dD")
    dma("a", T.ut[:], T.u[:], [], [("ut", 0, 512)], "dU")
    dma("s", T.xt[:, 0:4 * MID], T.x[:, 0:4 * MID], [], [("xt", 0, 4 * MID)], "dXF")
    dma("a", T.xt[:, 4 * MID:4 * C], T.x[:, 4 * MID:4 * C], [], [("xt", 4 * MID, 4 * C)], "dXL")
    dma("s", T.qw[:].bitcast(dt.uint8), T.wc[:], [], [("qw", 0, 512)], "dW")
    dma("s", T.sw[:], T.ws[:], [], [("sw", 0, 512)], "dW")
    dma("s", T.vt[:], T.v[:], [], [("vt", 0, 512)], "dV")

    qn, sn = "q%d" % ROUNDS, "s%d" % ROUNDS
    pi_, pr_ = T.pm[:, 0:1], T.pm[:, 1:2]
    ireg, rreg = ("pm", 0, 1), ("pm", 1, 2)
    once = {
        "ipi": lambda e: iota("pi", [[0, 1]], 0, 1, False),
        "ilt": lambda e: iota("lt", [[28, 4], [4, 4]], 0, 0),
        "ily": lambda e: iota("ly", [[1, 3], [48, 4]], MID, 0),
        "iit": lambda e: iota("it", [[2, 64]], 256, -2, False),
        "ict": lambda e: iota("ct", [[0, 3], [1, 4]], 0, 0),
        "ihn": lambda e: iota("hn", [[1, H]], -H - int(BIG), 0),
        "fpad": lambda e: fill("lv", 0, 12 * SEG, -2 * BIG, SEG),
        "fvs": lambda e: fill("vs", 63, 1664, 0.0, Q),
        "fe": lambda e: fill("e64", 0, 128, 64.0),
        "fz": lambda e: fill("em", 0, 520, 0.0),
        "iem": lambda e: op("G", lambda: g.affine_select(T.em[:, 3:515:4], T.e64[:], [[1, 128]], ALU.is_equal, 0.0, 0, -1), [whole("e64")], [whole("em")]),
        "pmi": lambda e: ts(pi_, T.pi[:], 15, None, ALU.bitwise_and, None, [whole("pi")], [ireg]),
        "pmr": lambda e: ts(pr_, T.pi[:], 3, None, ALU.bitwise_and, None, [whole("pi")], [rreg]),
        "pf": lambda e: move(T.pf[:], T.pm[:], [whole("pm")], [whole("pf")], "v"),
        "la": lambda e: ts(col(LA), pi_, 0.25, None, ALU.mult, None, [ireg], [creg(LA)]),
        "lb": lambda e: ts(col(LB), pr_, 111.75, None, ALU.mult, None, [rreg], [creg(LB)]),
        "lo": lambda e: ts(T.lo[:, 0:16], T.lt[:], col(LA), col(LB), ALU.add, ALU.add, [whole("lt"), creg(LA, 2)], [("lo", 0, 16)]),
        "l3": lambda e: ts(col(L3), pi_, 3.0, None, ALU.mult, None, [ireg], [creg(L3)]),
        "l84": lambda e: affine(col(L84), T.pf[:, 0:1], 84.0, 0.0, [whole("pf")], [creg(L84)], e),
        "ty": lambda e: ts(T.ty[:], T.ly[:], col(L3), None, ALU.add, None, [whole("ly"), creg(L3)], [whole("ty")]),
        "tb": lambda e: ts(T.tb[:], T.ty[:], 4, None, ALU.arith_shift_right, None, [whole("ty")], [whole("tb")]),
        "w28": lambda e: affine(T.w28[:], T.ly[:], 28.0, col(L84), [whole("ly"), creg(L84)], [whole("w28")], e),
        "wb": lambda e: ts(T.wb[:], T.tb[:], -447.0, None, ALU.mult, None, [whole("tb")], [whole("wb")]),
        "wc": lambda e: tt(T.wc2[:], T.wb[:], T.w28[:], ALU.add, [whole("wb"), whole("w28")], [whole("wc2")]),
        "ly": lambda e: move(T.lo[:, 16:28], T.wc2[:], [whole("wc2")], [("lo", 16, 28)], "v"),
        "ci": lambda e: ts(col(CI), pi_, 15.0, 0.5, ALU.is_lt, ALU.subtract, [ireg], [creg(CI)]),
        "cr": lambda e: affine(col(CR), col(CI), -2.0 / TINY, 0.0, [creg(CI)], [creg(CR)], e),
        "m1": lambda e: affine(col(M1), col(CI), 2.0, 0.0, [creg(CI)], [creg(M1)], e),
        "m4": lambda e: affine(col(M4), col(CI), 8.0, 0.0, [creg(CI)], [creg(M4)], e),
        "m16": lambda e: affine(col(M16), col(CI), 32.0, 0.0, [creg(CI)], [creg(M16)], e),
        "m64": lambda e: affine(col(M64), col(CI), 128.0, 0.0, [creg(CI)], [creg(M64)], e),
        "cb": lambda e: affine(col(CB), col(CI), 4 * BIG, 0.0, [creg(CI)], [creg(CB)], e),
        "jm": lambda e: ts(T.jm[:], T.it[:], 31, None, ALU.bitwise_and, None, [whole("it")], [whole("jm")]),
        "km": lambda e: ts(T.km[:], T.jm[:], -3.0, 1.0, ALU.add, ALU.min, [whole("jm")], [whole("km")]),
        "rcn": lambda e: affine(T.rc[:, 0:H], T.hn[:], TINY, 0.0, [whole("hn")], [("rc", 0, H)], e),
        "uo": lambda e: ts(T.uo[:], T.jvX[:, 0:32:4], BIG, None, ALU.subtract, None, [("jvX", 0, 32)], [whole("uo")]),
        "qu": lambda e: quant("qu0", "su0", 0, 128, "ut", 0),
        "pk": lambda e: op("V", lambda: V.tensor_copy(T.qu[:].bitcast(dt.uint32), T.qu0[:].bitcast(dt.uint32).indirect(T.uo[:])),
                           [whole("qu0"), whole("uo")], [whole("qu")]),
        "ps": lambda e: move(T.su[:], T.su0[:].indirect(T.uo[:]), [whole("su0"), whole("uo")], [whole("su")], e),
        "qY": lambda e: quant("q0", "s0", H + MID, H + C, "xt", 4 * MID),
        "qX": lambda e: quant("q0", "s0", H, H + MID, "xt", 0),
        "qv": lambda e: quant("qv", "sv", 0, 128, "vt", 0),
        "ol": lambda e: affine(T.olb[:, 0:MID], T.rc[:, H:H + MID], 1.0 / TINY, BIG, [("rc", H, H + MID)], [("olb", 0, MID)], e),
        "oy": lambda e: affine(T.olb[:, MID:C], T.rc[:, H + MID:H + C], 1.0 / TINY, BIG, [("rc", H + MID, H + C)], [("olb", MID, C)], e),
        "od": lambda e: store(e, T.ol[:], T.olb[0::16, :], [whole("olb")]),
    }
    for k in range(4):
        once["qe%d" % k] = lambda e, k=k: quant("qe", "se", 128 * k, 128 * k + 128, "em", 3 - k)
        once["os%d" % k] = lambda e, k=k: store(e, T.osc[4 * k:4 * k + 4, :], T[sn][32 * k:32 * k + 4, H:H + C], [(sn, H, H + C)])
    for h, (a, nb, num, _) in HALF.items():
        va, n, jv = seg(1, 1, h) + 1, Q * nb, "jv" + h
        once["i" + jv] = lambda e, jv=jv, nb=nb: iota(jv, [[1, nb], [nb, Q]], int(BIG), 0)
        once["MG" + h] = lambda e, n=n, num=num: affine(col(MG + num), col(CI), (n - 1) / 2, 0.0, [creg(CI)], [creg(MG + num)], e)
        once["BT" + h] = lambda e, num=num: affine(T.bt[:, 12 * num:12 * num + 12], T.ct[:], col(MG + num), 0.0,
                                                   [whole("ct"), creg(MG + num)], [("bt", 12 * num, 12 * num + 12)], e)
        for level, (src, add) in enumerate(((0, 64), (0, 16), (1, 4))):
            once["C%d%s" % (level + 1, h)] = lambda e, c=C1 + 3 * num + level, n=n, src=src, add=add: affine(
                col(c), T.pf[:, src:src + 1], 1.0 - n, 1 - add * BIG, [whole("pf")], [creg(c)], e)
        once["jq" + h] = lambda e, a=a, num=num, n=n, jv=jv: affine(T.jq[:, 256 * num:256 * num + n], T[jv][:], TINY, (a - 2 * BIG) * TINY,
                                                                    [whole(jv)], [("jq", 256 * num, 256 * num + n)], e)
        once["v0" + h] = lambda e, va=va, num=num, n=n, jv=jv: tt(
            T.lv[:, va:va + n], T.drep[:].indirect(T.lo[:, 16 * num:16 * num + n // 16]), T[jv][:], ALU.subtract,
            [whole("drep"), ("lo", 16 * num, 16 * num + 16), whole(jv)], [("lv", va, va + n)])
        for level in (1, 2, 3, 4):
            for k in range(4):
                once["S%d%s%d" % (level, h, k)] = lambda e, level=level, h=h, k=k: pick(level, h, k)
                once["o%d%s%d" % (level, h, k)] = lambda e, level=level, h=h, k=k: offsets(level, h, k)
                once["u%d%s%d" % (level, h, k)] = lambda e, level=level, h=h, k=k: level_step(1, level, h, k, e)
    for t in range(ROUNDS):
        once["xq%d" % t] = lambda e, t=t: send("q%d" % t, True)
        once["xs%d" % t] = lambda e, t=t: send("s%d" % t, False)
    for h in LAST:
        a, b, _ = PIECE[h]
        once["O" + h] = lambda e, a=a, b=b: store(e, T.oc[:, 4 * a:4 * b], T[qn][:, H + a:H + b].bitcast(dt.uint8), [(qn, H + a, H + b)])
        once["Y" + h] = lambda e, a=a, b=b: store(e, T.y[:, a:b], T.yb[:, a:b], [("yb", a, b)])

    for word in ORDER.split():
        name, eng = word.split(".") if "." in word else (word, None)
        now[0] = word
        if name in once:
            once[name](eng)
        elif name[0] in "prabdhn":
            root_step(name[0], int(name[1]), name[2], int(name[3:] or 0), eng)
        else:
            layer_step(name[0], int(name[1]), name[2], int(name[3:] or 0), eng)

    _emit(g, T, ops, ["sent", "dOut"])
